import numpy as np, ml_dtypes
CORES = [6,15,38,47]
N = 4
BF = ml_dtypes.bfloat16
L, S, NR, NC, RO, ST = 256, 16, 4096, 1024, 4, 1
def kill(rng, R, share):
    return np.where(rng.random((N, 8, 1, NR)) < share, 64, R)
def shares(rng):
    return np.stack([rng.permutation(np.array([0.1, 0.3, 0.3, 0.5, 0.5, 0.7, 0.7, 0.85])) for q in range(N)])[:, :, None, None]
def parts(rng):
    a = rng.choice(np.array([0.3, 1.0]), (N, 8, 1, NR))
    R = np.clip((16 + 32 * a * (rng.random((N, 8, 16, NR)) - 0.5)).astype(np.int64), 0, 31)
    H = rng.integers(90, 180, (N, 8, RO)) - 12 * np.arange(RO)
    return (rng.integers(0, 256, (N, 8, 16)), kill(rng, R, shares(rng)), rng.integers(0, NR, (N, 8, 16, NC)), rng.integers(0, 4096, (N, 8, NR)),
            rng.integers(0, 32, (N, 8, 16, L)), rng.integers(0, 4096, (N, 8, L)), np.maximum(H, 0))
def pack(w, R, C, P, Z, F, H):
    i = lambda a, *s: np.ascontiguousarray(a.reshape(*s)).astype(np.int32)
    return {"rec": np.ascontiguousarray(R.reshape(N, 128, NR)).astype(np.float32).astype(BF), "cel": i(C, N, 128, NC), "po": i(P, N, 8, NR),
            "pat": np.ascontiguousarray(Z.reshape(N, 128, L)).astype(np.float32).astype(BF), "phi": i(F, N, 8, L), "th": i(H, N, 8, RO), "wt": i(w, N, 128, 1)}
def lowest(ok, c):
    first = np.full((8, NC), L); lane = np.arange(L)[None, :]; g = np.arange(8)[:, None]
    np.minimum.at(first, (np.broadcast_to(g, c.shape), c), np.where(ok, lane, L))
    return ok & (first[g, c] == lane)
def look(R, C, Z, c):
    s = np.take_along_axis(C, c[:, None, :], 2)
    v = np.take_along_axis(R, s.reshape(8, 1, 16 * L), 2).reshape(8, 16, 16, L)
    return s, np.sum(np.abs(v - Z[:, :, None, :]), axis=1), v[:, 0] < 64
def at(a, k):
    return np.take_along_axis(a, k[:, None, :], 1)[:, 0]
def visit(R, C, P, Z, F, w, h, t):
    h1 = h[:, None, None]
    u = np.sum(w[:, :, None] * Z, axis=1) & 4095
    c = ((F * u >> 5) + F + 77 * t) & (NC - 1); e = ((c * u >> 5) + c + 1) & (NC - 1)
    s, d, live = look(R, C, Z, c); s2, d2, live2 = look(R, C, Z, e)
    sup = live & (d < h1); riv = live & (d >= h1)
    gain = 4 * np.sum(np.where(sup, h1 - d, 0), axis=1); loss = np.sum(np.where(riv, d - h1, 0), axis=1)
    acc = lowest(gain >= loss, c)
    has = np.any(sup, axis=1); y = np.argmin(np.where(sup, d, 9999), axis=1); ny = at(s, y)
    foe = np.any(riv, axis=1); nv = at(s, np.argmax(np.where(riv, d, -1), axis=1))
    zn = np.where(has[:, None, :], (Z + np.take_along_axis(R, ny[:, None, :], 2)) >> 1, Z)
    fn = np.where(acc & has, (np.take_along_axis(P, ny, 1) + 5 * at(d, y) + F) & 4095, (5 * F + u) & 4095)
    n = S * np.arange(L)[None, :] + (u & (S - 1))
    R2 = R.copy(); C2 = C.copy(); P2 = P.copy()
    g, i = np.nonzero(acc & foe); R2[g, :, nv[g, i]] = 64
    g, i = np.nonzero(acc); R2[g, :, n[g, i]] = zn[g, :, i]; P2[g, n[g, i]] = fn[g, i]
    g, i = np.nonzero(acc & np.any(~live, axis=1)); row = np.argmax(~live, axis=1)
    C2[g, row[g, i], c[g, i]] = n[g, i]
    acc2 = lowest(acc & ~np.any(live2 & (d2 < h1), axis=1), e)
    g, i = np.nonzero(acc2 & np.any(~live2, axis=1)); row = 15 - np.argmax(~live2[:, ::-1], axis=1)
    C2[g, row[g, i], e[g, i]] = n[g, i]
    return R2, C2, P2, zn, fn, acc
def setup_inputs(rng):
    return pack(*parts(rng))
def setup_inputs_spread(rng):
    w, R, C, P, Z, F, H = parts(rng)
    R = np.minimum((32 * rng.random((N, 8, 16, NR)) ** np.exp2(rng.integers(-2, 3, (N, 8, 1, NR)))).astype(np.int64), 31)
    Z = np.minimum((32 * rng.random((N, 8, 16, L)) ** np.exp2(rng.integers(-2, 3, (N, 8, 1, L)))).astype(np.int64), 31)
    C = np.minimum((NR * rng.random((N, 8, 16, NC)) ** 3).astype(np.int64), NR - 1)
    P = np.minimum(np.exp2(12 * rng.random((N, 8, NR))).astype(np.int64), 4095); F = np.minimum(np.exp2(12 * rng.random((N, 8, L))).astype(np.int64), 4095)
    w = np.minimum(np.exp2(8 * rng.random((N, 8, 16))).astype(np.int64), 255)
    H = np.where(rng.random((N, 8, RO)) < 0.6, rng.integers(60, 220, (N, 8, RO)), rng.integers(0, 481, (N, 8, RO)))
    return pack(w, kill(rng, R, shares(rng)), C, P, Z, F, H)
def edge(rng, n):
    k = rng.integers(0, 4, (N, 8, 1, n))
    return 31 * np.where(k <= 1, 0, np.where(k == 2, 1, rng.integers(0, 2, (N, 8, 16, n))))
def setup_inputs_ends(rng):
    w = 255 * rng.integers(0, 2, (N, 8, 16)); R = kill(rng, edge(rng, NR), 0.4); Z = edge(rng, L)
    C = np.where(rng.random((N, 8, 16, NC)) < 0.7, (NR - 1) * rng.integers(0, 2, (N, 8, 16, NC)), rng.integers(0, NR, (N, 8, 16, NC)))
    P = 4095 * rng.integers(0, 2, (N, 8, NR)); F = 4095 * rng.integers(0, 2, (N, 8, L)); H = 480 * rng.integers(0, 2, (N, 8, RO))
    for q in range(N):
        for g in range(6):
            R[q, g, :, 0] = (0, 31, 64)[(q + g) % 3]; R[q, g, :, NR - 1] = (0, 31, 64)[(q + g + 1) % 3]
    w[:, 5] = 0; w[:, 5, 0] = 195; Z[:, 5, 0, 0] = 21; F[:, 5, 0] = 4095
    R[:, 6] = 64; Z[:, 6] = 0; F[:, 6] = 0
    H[:, 7, 0] = 0; H[:, 7, 1] = 480; R[:, 7, :, 0] = 31; R[:, 7, :, NR - 1] = 0
    C[:, 7, :, 0] = 0; C[:, 7, :, NC - 1] = 0; C[:, 7, :, 77] = NR - 1
    for k in (0, 5, L - 2, L - 1):
        Z[:, 7, :, k] = 0; F[:, 7, k] = 0
    for q in range(N):
        a = visit(R[q], C[q], P[q], Z[q], F[q], w[q], H[q, :, 0], 0)[5]; a[6] = False
        m = 1 + ((30 - int(np.count_nonzero(a))) & 31)
        F[q, 6, rng.permutation(L)[:m - 1]] = np.arange(1, m)
    return pack(w, R, C, P, Z, F, H)
def selfsame(rng, u0, p0):
    p = np.arange(4096)[:, None]; u = np.arange(256)[None, :]
    c = ((p * u >> 5) + p) & (NC - 1); e = ((c * u >> 5) + c + 1) & (NC - 1)
    c0 = ((p0 * u0 >> 5) + p0) & (NC - 1); e0 = ((c0 * u0 >> 5) + c0 + 1) & (NC - 1)
    i, j = np.nonzero((c == e) & (c != c0) & (c != e0)); z = int(rng.integers(0, len(i)))
    return int(j[z]), int(i[z])
def setup_inputs_corners(rng):
    w, R, C, P, Z, F, H = parts(rng)
    for q in range(N):
        for g in range(8):
            o = (g + q) & 7
            if o == 0:
                R[q, g] = 64; Z[q, g] = 0; F[q, g] = rng.permutation(NC)[:L]
                w[q, g] = 0; w[q, g, 0] = 163; Z[q, g, 0, 0] = 25; F[q, g, 0] = 4093
                u, p = selfsame(rng, 4075, 4093)
                w[q, g, 1] = 1; w[q, g, 2] = 32; Z[q, g, 1, 1] = u & 31; Z[q, g, 2, 1] = u >> 5; F[q, g, 1] = p
            elif o == 1:
                R[q, g] = rng.integers(0, 32, (16, NR))
            elif o == 2:
                h = NR // 2; R[q, g, :, :h] = rng.integers(0, 32, (16, h)); R[q, g, :, h:] = 64
                C[q, g] = rng.integers(0, h, (16, NC)) + h * (np.arange(NC) & 1)[None, :]
                C[q, g, 15, 2::4] = h + rng.integers(0, h, NC // 4); C[q, g, 0, 3::4] = rng.integers(0, h, NC // 4)
            elif o == 3:
                C[q, g] = rng.integers(0, NR, (1, NC))
            elif o == 4:
                w[q, g] = 0; C[q, g] = S * rng.integers(0, L, (16, NC))
            elif o == 5:
                H[q, g] = 0; R[q, g] = np.where(R[q, g, :1] == 64, 64, 7 + (rng.random((1, NR)) < 0.1)); Z[q, g] = 7 + (rng.random((1, L)) < 0.1)
            elif o == 6:
                H[q, g] = 480; R[q, g] = np.where(R[q, g, :1] == 64, 64, 31 * rng.integers(0, 2, (1, NR))); Z[q, g] = 31 * rng.integers(0, 2, (1, L))
            else:
                w[q, g] = 255; C[q, g] = rng.choice(np.array([0, 1, S - 1, S, NR - S, NR - 2, NR - 1]), (16, NC))
                F[q, g] = 4095 * rng.integers(0, 2, L); P[q, g] = 4095 * rng.integers(0, 2, NR)
    return pack(w, R, C, P, Z, F, H)
def meet(rng):
    p = rng.integers(0, 4096, 1024)[:, None]; u = np.arange(1024)[None, :]
    c = ((p * u >> 5) + p) & (NC - 1); e = ((c * u >> 5) + c + 1) & (NC - 1); k = e[int(rng.integers(0, 1024)), int(rng.integers(512, 1024))]
    i, j = np.nonzero(e == k); o = rng.permutation(len(i)); i, j = i[o], j[o]
    x = np.resize(rng.permutation(np.unique(c[i, j], return_index=True)[1]), L); i, j = i[x], j[x]
    a, b = np.nonzero((e != k) & ~np.isin(c, c[i, j])); z = int(rng.integers(0, len(a)))
    return u[0, j], p[i, 0], int(u[0, b[z]]), int(p[a[z], 0])
def setup_inputs_crowd(rng):
    w, R, C, P, Z, F, H = parts(rng)
    for q in range(N):
        for g in range(8):
            o = (g + q) & 7; f0 = int(rng.integers(0, 4095))
            if q < 2:
                R[q, g] = 64; Z[q, g] = 0; F[q, g] = rng.permutation(NC)[:L]; H[q, g, 1] = int(rng.integers(220, 260))
            elif o <= 2:
                Z[q, g] = Z[q, g, :, :1].copy(); F[q, g] = f0; H[q, g, 0] = 480
                if o == 1: F[q, g, L - 1] = f0 + 1
                if o == 2: F[q, g, 1::2] = f0 + 1
            elif o <= 4:
                u, p, u1, p1 = meet(rng)
                if o == 4: u[L - 1] = u1; p[L - 1] = p1
                w[q, g] = 0; w[q, g, 0] = 1; w[q, g, 1] = 32; R[q, g] = 64; Z[q, g, 0] = u & 31; Z[q, g, 1] = u >> 5; F[q, g] = p
            elif o <= 6:
                w[q, g] = 0; R[q, g] = rng.integers(0, 4, (16, NR)); R[q, g, :, NR - 1] = 31; Z[q, g] = rng.integers(0, 4, (16, L)); F[q, g] = rng.permutation(NC)[:L]; H[q, g, 0] = 200
                C[q, g] = rng.integers(0, NR - 1, (16, NC)); C[q, g, rng.integers(0, 16, NC), np.arange(NC)] = NR - 1
                if o == 6: C[q, g, :, F[q, g, 3]] = rng.integers(0, NR - 1, 16)
            else:
                w[q, g] = 0; F[q, g] = f0; H[q, g, 0] = 150
    F[1, 7, L - 1] = F[1, 7, 0]
    return pack(w, R, C, P, Z, F, H)
def setup_inputs_ties(rng):
    w, R, C, P, Z, F, H = parts(rng)
    R = kill(rng, 8 * rng.integers(0, 2, (N, 8, 16, NR)), shares(rng)); Z = 8 * rng.integers(0, 2, (N, 8, 16, L)); H = 8 * rng.integers(4, 11, (N, 8, RO))
    C[:, :, 15] = np.where(rng.random((N, 8, NC)) < 0.3, C[:, :, 0], C[:, :, 15])
    return pack(w, R, C, P, Z, F, H)
def check_inputs(d):
    bad = []
    for k, lo, hi in (("rec", 0, 64), ("cel", 0, NR - 1), ("po", 0, 4095), ("pat", 0, 31), ("phi", 0, 4095), ("th", 0, 480), ("wt", 0, 255)):
        a = np.asarray(d[k]).astype(np.float64)
        if not (np.min(a) >= lo and np.max(a) <= hi and np.all(a == np.floor(a))): bad.append("range of " + k)
    a = np.asarray(d["rec"]).astype(np.float32).reshape(N, 8, 16, NR)
    if not np.all(np.all(a == 64, axis=2) | np.all(a <= 31, axis=2)): bad.append("a record of rec is neither living nor dead")
    return bad
def reference(rec, cel, po, pat, phi, th, wt):
    R = list(rec.astype(np.float32).astype(np.int32).reshape(N, 8, 16, NR)); C = list(cel.astype(np.int32).reshape(N, 8, 16, NC)); P = list(po.astype(np.int64))
    Z = list(pat.astype(np.float32).astype(np.int32).reshape(N, 8, 16, L)); F = list(phi.astype(np.int64))
    w = wt.astype(np.int32).reshape(N, 8, 16); H = th.astype(np.int64); A = [0] * N
    for t in range(RO):
        for q in range(N):
            R[q], C[q], P[q], Z[q], F[q], acc = visit(R[q], C[q], P[q], Z[q], F[q], w[q], H[q, :, t] + (A[q] & 31), t)
            A[q] = int(np.count_nonzero(acc))
        Z = [Z[(q - ST) % N] for q in range(N)]; F = [F[(q - ST) % N] for q in range(N)]
    return {"yrec": np.stack(R).reshape(N, 128, NR).astype(np.float32).astype(BF), "ycel": np.stack(C).reshape(N, 128, NC).astype(np.float32), "ypo": np.stack(P).astype(np.float32),
            "ypat": np.stack(Z).reshape(N, 128, L).astype(np.float32).astype(BF), "yphi": np.stack(F).astype(np.float32)}

@@ -1,0 +1,506 @@
+from concourse.mybir import AluOpType as A, AxisListType, ActivationFunctionType as F
+
+NV = 4
+CH = [(0, 4), (4, 4), (8, 4), (12, 4)]
+CM = ["a", "v", "a", "v"]
+ZM = ["g", "a"] * 8
+EM = ["v", "v", "v", "v", "v", "a", "a", "a"]
+TRN = 3.0
+CY = 0.83e-3 * 1.2
+
+B, H, F4, I4, U2 = "bfloat16", "float16", "float32", "int32", "uint16"
+SHAPES = {
+    B: "R:4608 x2:4096 ze:4096 ve:4096 sup:256 sg:256 sg2:256 xs:256 x4:256 zh:256 ckb:256 mM:256 s64:256 accb:16",
+    H: "crow:256 vrow:256 winr:256 sa_:256 sb_:256 sq_:256 pg:256 phh:256 thh:4 Bh:128 Ih:128 r16h:256 L3:48 v16:16",
+    F4: "C:1280 PT:4352 posf:256 erF:256 sF:256 sF2:256 nd:256 nd2:256 sm:256 kr:256 sx:256 phr:256 thf:4 hc:8 hA:4 hB:4 hm:4 "
+        "B8a:8 B8:8 g16:8 g16b:8 K3:48 rc:2 Cr:256 d0n:256 d0x:256 ck:256 par:2 r16:256 RM:48 acc:32 T2c:32 la:32 col:16",
+    I4: "Ci:1024 pos:256 phl:256 thl:4 wl:1 ai:1 CI:48",
+    U2: "su:256 su2:256 lau:32",
+}
+LF = "u32 has t3 t4 t5 ps pdh w5 w6 f0 f0a dif ph rr dl l2 foe flg vk unq cnd cn0 w2 vrm nek cf jr I16 b256 i16 zt iL tr tc pw pwb".split()
+LI = "ui u2 xq xr ye kI ny w1 fI vs fr fr2".split()
+LU = "cu eu zo nyu dlu l2u".split()
+MB = "Bb W1 Do Dg Zb Ib In Y1 Y2".split()
+MF = "one idf Bba Bf shp shm Utf Ulf".split()
+SCRATCH = {}
+for _d, _l in SHAPES.items():
+    for _x in _l.split():
+        SCRATCH[_x.split(":")[0]] = ("sbuf", [128, int(_x.split(":")[1])], _d)
+for _x in ("xa", "xe", "EQ", "EQe", "EQv"):
+    SCRATCH[_x] = ("sbuf", [128, 16, 256], B)
+for _x, _d in (("Sb", B), ("Sk", B), ("Sw", B), ("Sh", H), ("Pk", H), ("Sp", H)):
+    SCRATCH[_x] = ("sbuf", [128, 16, 128], _d)
+for _x, _l, _n, _d in (("lf", LF, 16, F4), ("li", LI, 16, I4), ("lu", LU, 16, U2), ("mb", MB, 128, B), ("mf", MF, 128, F4)):
+    SCRATCH[_x] = ("sbuf", [128, len(_l), _n], _d)
+SCRATCH["s16"] = ("sbuf", [128, 8, 2, 16], H)
+SCRATCH["t16"] = ("sbuf", [128, 8, 32], H)
+SCRATCH["W4"] = ("sbuf", [128, 4, 128], H)
+for _t in range(NV + 1):
+    SCRATCH["zin%d" % _t] = ("sbuf", [128, 256], B)
+    SCRATCH["fin%d" % _t] = ("sbuf", [128, 16], H)
+for _t in range(NV):
+    SCRATCH["zout%d" % _t] = ("sbuf", [128, 256], B)
+    SCRATCH["fout%d" % _t] = ("sbuf", [128, 16], H)
+for _b in range(8):
+    SCRATCH["b%d" % _b] = ("psum", [128, 512], F4)
+DMAS = ["rec", "cel", "wt", "pat", "phi", "th", "po", "pt", "yrec", "ycel", "ypo", "ypat", "yphi"]
+SEMAPHORES = ["qv", "qa", "qp", "qg"] + ["d" + n for n in DMAS] + ["%s%d" % (k, t) for k in ("zr", "zl", "fr", "fl") for t in range(NV)]
+
+
+def dv(n, rate=1.0, k=1):
+    return k * max(64, n * rate + 12) * CY
+
+
+def dp(n, k=1):
+    return k * max(64, n) * 0.45e-3 + 0.03
+
+
+def program(T, g, me, nxt, topo):
+    v, a, p, s = g.vector, g.scalar, g.tensor, g.sync
+    ops = []
+    last = {}
+
+    def add(q, fns, w, r, d, sem=None, val=0, net=None):
+        o = {"q": q, "f": fns, "d": d, "sem": sem, "val": val, "i": len(ops), "wait": set(), "ord": set(), "net": net}
+        rs, ws = r.split(), w.split()
+        for key in sorted(set(rs + ws)):
+            L = last.setdefault(key, [None, []])
+            if key[0] == "b" and key[1:].isdigit():
+                if L[0] is not None:
+                    free = ops[L[0]]["q"] == q and (q == "p" or not L[1])
+                    o["ord" if free else "wait"].add(L[0])
+                last[key] = [o["i"], key in ws]
+                continue
+            if key in rs and L[0] is not None:
+                o["wait"].add(L[0])
+            if key in ws:
+                for x in ([L[0]] if L[0] is not None else []) + L[1]:
+                    o["ord" if ops[x]["q"] == q and ops[x]["sem"] is None and x != L[0] else "wait"].add(x)
+                last[key] = [o["i"], []]
+            else:
+                L[1].append(o["i"])
+        o["ord"] -= o["wait"]
+        ops.append(o)
+        return o["i"]
+
+    def V(fn, w, r, n, rate=1.0):
+        return add("v", [fn], w, r, dv(n, rate))
+
+    def S_(fn, w, r, n, rate=1.0):
+        return add("a", [fn], w, r, dv(n, rate))
+
+    def G(fn, w, r, n):
+        return add("g", [fn], w, r, 0.2 + 2 * n * CY)
+
+    def PM(args, n, w, r):
+        return add("p", [(lambda x=x: p.matmul(*x)) for x in args], w, r, dp(n, len(args)))
+
+    def D(name, out, in_, w, r, d, q="s"):
+        return add(q, [lambda: (s if q == "s" else a).dma_start(out, in_)], w, r, d, "d" + name, 16)
+
+    TS, TT, TC, MS, ACT = v.tensor_scalar, v.tensor_tensor, v.tensor_copy, v.memset, a.activation
+    RED = lambda out, in_: v.tensor_reduce(out, in_, AxisListType.X, A.add)
+    R16 = range(16)
+    (u32, has, t3, t4, t5, ps, pdh, w5, w6, f0, f0a, dif, ph, rr, dl, l2, foe, flg, vk, unq, cnd, cn0, w2, vrm, nek, cf, jr, I16, b256, i16, zt, iL,
+     tr, tc, pw, pwb) = [T.lf[:, k, :] for k in range(len(LF))]
+    ui, u2, xq, xr, ye, kI, ny, w1, fI, vs, fr, fr2 = [T.li[:, k, :] for k in range(len(LI))]
+    cu, eu, zo, nyu, dlu, l2u = [T.lu[:, k, :] for k in range(len(LU))]
+    Bb, W1, Do, Dg, Zb, Ib, In, Y1, Y2 = [T.mb[:, k, :] for k in range(len(MB))]
+    one, idf, Bba, Bf, shp, shm, Utf, Ulf = [T.mf[:, k, :] for k in range(len(MF))]
+    pc, gs, jc, j16, p2, wf, bn, bx, af = [T.col[:, k:k + 1] for k in range(9)]
+    lfc = lambda name, b: T.lf[:, LF.index(name), b:b + 1]
+
+    def pick(out, src, bank):
+        PM([(out, T.Pk[:, j, :], T[src][:, j:256:16], j == 0, j == 15) for j in R16], 16, bank, "Pk " + src)
+
+    def spread(bank, off, src, lo, hi):
+        PM([(T[bank][:, off + j:off + 16 * (hi - lo):16], T.Sp[:, j, :], T[src][:, lo:hi], True, True) for j in R16], hi - lo, bank, "Sp " + src)
+
+    V(lambda: MS(T.phl[:], 0), "phl", "", 256)
+    V(lambda: MS(T.thl[:], 0), "thl", "", 4)
+    D("pat", T.zin0[:], T.pat[:], "zin0", "", 2.0)
+    D("wt", T.wl[:], T.wt[:], "wl", "", 2.0)
+    D("phi", T.phl[0:128:16, :], T.phi[:], "phl", "", 2.0)
+    D("cel", T.Ci[:], T.cel[:], "Ci", "", 3.5)
+    D("rec", T.R[:, 0:4096], T.rec[:], "R", "", 6.0, "a")
+    D("th", T.thl[0:128:16, :], T.th[:], "thl", "", 2.0)
+    D("po", T.pos[:], T.po[:], "pos", "", 2.0)
+    V(lambda: MS(one, 1.0), "one", "", 128)
+    iota = lambda out, pat, base=0, cm=0: g.iota(out, pat, base, cm, allow_small_or_imprecise_dtypes=True)
+    sel = lambda out, in_, pat, op, base, cm: g.affine_select(out, in_, pat, op, 0.0, base, cm)
+    G(lambda: sel(T.B8a[:], T.mf[:, 0, 0:8], [[-16, 8]], A.is_ge, 0, 1), "B8a", "one", 8)
+    G(lambda: sel(T.B8[:], T.B8a[:], [[16, 8]], A.is_ge, 15, -1), "B8", "B8a", 8)
+    G(lambda: iota(T.g16[:], [[16, 8]]), "g16", "", 8)
+    G(lambda: iota(pc, [[0, 1]], 0, 1), "pc", "", 1)
+    G(lambda: iota(jr, [[1, 16]]), "jr", "", 16)
+    G(lambda: iota(b256, [[256, 16]]), "b256", "", 16)
+    G(lambda: sel(idf, one, [[-1, 128]], A.is_equal, 0, 1), "idf", "one", 128)
+    G(lambda: sel(Bba, one, [[-16, 8], [0, 16]], A.is_ge, 0, 1), "Bba", "one", 128)
+    G(lambda: sel(Bf, Bba, [[16, 8], [0, 16]], A.is_ge, 15, -1), "Bf", "Bba", 128)
+    V(lambda: MS(T.Sb[:], 0.0), "Sb", "", 2048, 0.5)
+    add("v", [(lambda j=j: TC(T.Sb[:, j, j:128:16], T.B8[:])) for j in R16], "Sb", "B8", dv(8, 1, 16))
+    V(lambda: TC(wf, T.wl[:]), "wf", "wl", 1)
+    V(lambda: TS(T.Sw[:], T.Sb[:], wf, None, A.mult), "Sw", "Sb wf", 2048, 0.5)
+    V(lambda: TC(T.C[:, 0:1024], T.Ci[:]), "C", "Ci", 1024)
+    V(lambda: MS(T.C[:, 1024:1280], 0.0), "C", "", 256)
+    S_(lambda: ACT(T.Sk[:], T.Sb[:], F.Copy, scale=65536.0), "Sk", "Sb", 2048)
+    V(lambda: TT(T.g16b[:], T.g16[:], T.B8[:], A.mult), "g16b", "g16 B8", 8)
+    V(lambda: RED(gs, T.g16b[:]), "gs", "g16b", 8)
+    V(lambda: TT(jc, pc, gs, A.subtract), "jc", "pc gs", 1)
+    V(lambda: TS(I16, jr, jc, None, A.is_equal), "I16", "jr jc", 16)
+    V(lambda: TS(j16, jc, 16.0, None, A.mult), "j16", "jc", 1)
+    V(lambda: TS(bn, jc, -1.0, None, A.mult), "bn", "jc", 1)
+    V(lambda: TS(bx, jc, -15.0, None, A.add), "bx", "jc", 1)
+    V(lambda: TS(i16, b256, j16, None, A.add), "i16", "b256 j16", 16)
+    V(lambda: TS(iL, i16, 0.0625, None, A.mult), "iL", "i16", 16)
+    V(lambda: TS(tr, iL, 4096.0, None, A.add), "tr", "iL", 16)
+    V(lambda: TS(tc, iL, 1024.0, None, A.add), "tc", "iL", 16)
+    V(lambda: TS(zt, iL, 4352.0, None, A.add), "zt", "iL", 16)
+    V(lambda: TT(T.K3[:, 0:16], tr, i16, A.subtract), "K3", "i16 tr", 16)
+    V(lambda: TC(T.K3[:, 16:32], tc), "K3", "tc", 16)
+    V(lambda: TC(T.K3[:, 32:48], tc), "K3", "tc", 16)
+    V(lambda: TC(T.T2c[:, 0:16], tr), "T2c", "tr", 16)
+    V(lambda: TC(T.T2c[:, 16:32], tc), "T2c", "tc", 16)
+    for k, (x, y) in enumerate(((65536.0, -16777216.0), (65536.0, 61440.0 - 16777216.0), (1.0, -512.0), (80.0, 0.0))):
+        V(lambda k=k, x=x: MS(T.hA[:, k:k + 1], x), "hA", "", 1)
+        V(lambda k=k, y=y: MS(T.hB[:, k:k + 1], y), "hB", "", 1)
+    V(lambda: TC(T.Sh[:], T.Sb[:]), "Sh", "Sb", 2048, 0.5)
+    V(lambda: TS(T.Pk[:], T.Sb[:], lfc("I16", 0), None, A.mult), "Pk", "Sb I16", 2048, 0.5)
+    V(lambda: TC(Bb, Bf), "Bb", "Bf", 128)
+    V(lambda: TC(T.Bh[:], Bf), "Bh", "Bf", 128)
+    add("v", [(lambda j=j: TS(T.Sp[:, j, :], Bb, lfc("I16", j), None, A.mult)) for j in R16], "Sp", "Bb I16", dv(128, 0.5, 16))
+    V(lambda: RED(T.rc[:, 0:1], T.B8[:, 0:8:2]), "rc", "B8", 4)
+    V(lambda: RED(T.rc[:, 1:2], T.B8[:, 1:8:2]), "rc", "B8", 4)
+    G(lambda: sel(shp, one, [[-1, 128]], A.is_equal, 16, 1), "shp", "one", 128)
+    G(lambda: sel(shm, one, [[-1, 128]], A.is_equal, -16, 1), "shm", "one", 128)
+    for k, (src, key, r) in enumerate(((idf, "idf", 0), (shp, "shp", 0), (shm, "shm", 1), (idf, "idf", 1))):
+        V(lambda k=k, src=src, r=r: TS(T.W4[:, k, :], src, T.rc[:, r:r + 1], None, A.mult), "W4", key + " rc", 128)
+    G(lambda: iota(T.ck[:], [[0, 16], [4096, 16]], 2048), "ck", "", 256)
+    V(lambda: RED(T.par[:, 0:1], T.lf[:, LF.index("I16"), 0:16:2]), "par", "I16", 8)
+    V(lambda: TS(T.par[:, 1:2], T.par[:, 0:1], 16777216.0, -16777216.0, A.mult, A.add), "par", "par", 1)
+    V(lambda: TS(T.ckb[:], T.ck[:], T.par[:, 0:1], T.par[:, 1:2], A.mult, A.add), "ckb", "ck par", 256)
+    V(lambda: MS(W1, 0.015625), "W1", "", 128, 0.5)
+    G(lambda: iota(T.r16[:], [[16, 256]]), "r16", "", 256)
+    V(lambda: TC(T.r16h[:], T.r16[:]), "r16h", "r16", 256)
+    V(lambda: TC(T.Ih[:], idf), "Ih", "idf", 128)
+    V(lambda: TC(Ib, idf), "Ib", "idf", 128)
+    V(lambda: TS(In, idf, -1.0, None, A.mult), "In", "idf", 128)
+    V(lambda: MS(T.d0n[:], 0.0), "d0n", "", 256)
+    V(lambda: MS(T.d0n[:, 0:256:16], 134217728.0), "d0n", "", 16)
+    add("v", [(lambda j=j: MS(T.Cr[:, j:256:16], float(2 ** (16 - j)))) for j in R16], "Cr", "", dv(16, 1, 16))
+    V(lambda: TS(pw, T.Cr[:, 0:16], 0.5, None, A.mult), "pw", "Cr", 16)
+    V(lambda: TT(pwb, pw, I16, A.mult), "pwb", "pw I16", 16)
+    V(lambda: RED(p2, pwb), "p2", "pwb", 16)
+    V(lambda: TS(Do, Bb, 65536.0, None, A.mult), "Do", "Bb", 128, 0.5)
+    V(lambda: TS(Dg, Bb, p2, None, A.mult), "Dg", "Bb p2", 128, 0.5)
+    V(lambda: MS(Zb, 0.0), "Zb", "", 128, 0.5)
+    V(lambda: MS(T.s64[:], 64.0), "s64", "", 256, 0.5)
+    V(lambda: MS(T.d0x[:], 8192.0), "d0x", "", 256)
+    V(lambda: MS(T.d0x[:, 0:256:16], -268435456.0), "d0x", "", 16)
+    G(lambda: sel(Utf, Bf, [[1, 128]], A.is_gt, 0, -1), "Utf", "Bf", 128)
+    G(lambda: sel(Ulf, Bf, [[-1, 128]], A.is_gt, 0, 1), "Ulf", "Bf", 128)
+    V(lambda: TT(Y1, idf, Utf, A.subtract), "Y1", "idf Utf", 128, 2)
+    V(lambda: TT(Y2, idf, Ulf, A.subtract), "Y2", "idf Ulf", 128, 2)
+    G(lambda: iota(T.PT[:], [[0, 4352]]), "PT", "", 4352)
+    V(lambda: MS(T.R[:, 4096:4352], 0.0), "R", "", 256, 0.5)
+    V(lambda: TC(T.thh[:], T.thl[:]), "thh", "thl", 4)
+    PM([(T.b3[:, 64:68], T.Bh[:], T.thh[:], True, True)], 4, "b3", "Bh thh")
+    V(lambda: TC(T.thf[:], T.b3[:, 64:68]), "thf", "b3", 4)
+    V(lambda: TS(T.phh[:], T.phl[:], -2048.0, None, A.add), "phh", "phl", 256)
+    pick(T.b5[:, 256:272], "phh", "b5")
+    V(lambda: TC(T.fin0[:], T.b5[:, 256:272]), "fin0", "b5", 16)
+    V(lambda: TC(T.posf[:], T.pos[:]), "posf", "pos", 256)
+    D("pt", T.PT[0:128:16, 0:4096], T.posf[:], "PT", "posf", 2.5)
+
+    def dedupe(eq, bank, eng, row, rkey, key, flag):
+        for q in range(4):
+            bs = range(4 * q, 4 * q + 4)
+            e = lambda b: T[eq][:, b, 0:256 - 16 * b]
+            ek = "%s.%d" % (eq, q)
+            if eng == "v":
+                add("v", [(lambda b=b: TS(e(b), row[:, 16 * b:256], lfc(key, b), lfc(flag, b), A.is_equal, A.mult)) for b in bs],
+                    ek, "%s %s %s" % (rkey, key, flag), sum(dv(256 - 16 * b, 0.5) for b in bs))
+            else:
+                d = sum(dv(256 - 16 * b) for b in bs)
+                add("a", [(lambda b=b: ACT(e(b), row[:, 16 * b:256], F.Square, bias=lfc(key, b))) for b in bs], ek, rkey + " " + key, d)
+                add("a", [(lambda b=b: ACT(e(b), e(b), F.Relu, bias=lfc(flag, b), scale=-1.0)) for b in bs], ek, ek + " " + flag, d)
+        for q in range(4):
+            bs = range(4 * q, 4 * q + 4)
+            ms = [] if q else [(T[bank][:, 0:256], Zb, T.s64[:], True, False)]
+            ms += [(T[bank][:, 16 * b + 16:256], Do, T[eq][:, b, 16:256 - 16 * b], False, False) for b in bs if b < 15]
+            if q == 3:
+                ms.append((T[bank][:, 0:256], Dg, T[eq][:, :, 0:16], False, True))
+            PM(ms, 200 - 40 * q, bank, ("%s.%d Do" % (eq, q)) + (" Zb s64" if not q else "") + (" Dg @.0 @.1 @.2".replace("@", eq) if q == 3 else ""))
+        V(lambda: TT(T.winr[:], T[bank][:, 0:256], T.Cr[:], A.is_lt), "winr", bank + " Cr", 256)
+        pick(T[bank][:, 256:272], "winr", bank)
+
+    def send(key, src, dst, t):
+        rid, pid, _ = topo.addr(nxt)
+        m, n = topo.mask(me, nxt), len(topo.engines(me, nxt))
+        i = add("g", [lambda: g.remote_dma(T[dst][:], T[src][:], T.sem["%sr%d" % (key, t)], T.sem["%sl%d" % (key, t)], pid, rid, m)],
+                "", src, 0.3, "%sl%d" % (key, t), n)
+        add("n", [], dst, "", TRN, "%sr%d" % (key, t), n, i)
+
+    ZE = " ".join("ze.%d" % k for k in R16)
+    WB = T.b5[:, 256:272]
+    for t in range(NV):
+        zi, fi, zo_, fo = "zin%d" % t, "fin%d" % t, "zout%d" % t, "fout%d" % t
+        zin, fin, zout, fout = T[zi], T[fi], T[zo_], T[fo]
+        PM([(T.b3[:, 0:16], T.Sw[:, j, :], zin[:, j:256:16], j == 0, j == 15) for j in R16], 16, "b3", "Sw " + zi)
+        V(lambda: TC(xr, T.b3[:, 0:16]), "xr", "b3", 16)
+        V(lambda: TS(ui, xr, 4095, None, A.bitwise_and), "ui", "xr", 16)
+        V(lambda: TS(u32, ui, 32.0, None, A.add), "u32", "ui", 16)
+        V(lambda t=t: TS(u2, ui, 2048.0, 2464.0 * t, A.mult, A.add), "u2", "ui", 16)
+        V(lambda: TS(u2, u2, 32767, None, A.bitwise_and), "u2", "u2", 16)
+        for k in R16:
+            zk = T.ze[:, k:4096:16]
+            if ZM[k] == "a":
+                S_(lambda zk=zk, zin=zin: ACT(zk, zin[:], F.Copy), "ze.%d" % k, zi, 256)
+            elif ZM[k] == "g":
+                G(lambda zk=zk, zin=zin: sel(zk, zin[:], [[0, 256]], A.is_gt, 1, 0), "ze.%d" % k, zi, 256)
+            else:
+                V(lambda zk=zk, zin=zin: TC(zk, zin[:]), "ze.%d" % k, zi, 256, 0.5)
+        S_(lambda zin=zin: ACT(T.zh[:], zin[:], F.Copy, bias=-0.5), "zh", zi, 256)
+        S_(lambda zin=zin: ACT(T.R[:, 4352:4608], zin[:], F.Copy), "Rz", zi, 256)
+        V(lambda fin=fin: TT(xq, u32, fin[:], A.mult), "xq", "u32 " + fi, 16)
+        V(lambda: TT(xq, xq, u2, A.add), "xq", "xq u2", 16)
+        V(lambda: TS(T.CI[:, 16:32], xq, 5, 1023, A.arith_shift_right, A.bitwise_and), "ci", "xq", 16)
+        V(lambda: TC(cu, T.CI[:, 16:32]), "cu", "ci", 16)
+        V(lambda: TC(T.su[:], T.C[:, 0:1024].indirect(cu)), "su", "C cu", 256, 1.5)
+        S_(lambda: ACT(T.sF[:], T.C[:, 0:1024].indirect(cu), F.Copy), "sF", "C cu", 256, 1.5)
+        V(lambda: TT(ye, T.CI[:, 16:32], u32, A.mult), "ye", "ci u32", 16)
+        V(lambda: TS(ye, ye, 32.0, None, A.add), "ye", "ye", 16)
+        V(lambda: TS(T.CI[:, 32:48], ye, 5, 1023, A.arith_shift_right, A.bitwise_and), "ei", "ye", 16)
+        V(lambda: TC(eu, T.CI[:, 32:48]), "eu", "ei", 16)
+        V(lambda: TC(T.su2[:], T.C[:, 0:1024].indirect(eu)), "su2", "C eu", 256, 1.5)
+        V(lambda: TS(T.CI[:, 0:16], ui, 15, None, A.bitwise_and), "mi", "ui", 16)
+        V(lambda: TC(T.L3[:], T.CI[:]), "L3", "ci mi ei", 48)
+        V(lambda: TC(cf, T.CI[:, 16:32]), "cf", "ci", 16)
+        V(lambda: TS(nek, T.CI[:, 32:48], -1.0, None, A.mult), "nek", "ei", 16)
+        V(lambda: TT(T.RM[:], T.CI[:], T.K3[:], A.subtract), "RM", "ci mi ei K3", 48)
+        PM([(T.b0[:, 256:512], T.Ih[:], T.r16h[:], True, False)] +
+           [(T.b0[:, 256 + j:512:16], T.Sp[:, j, :], T.L3[:, 0:16], False, j == 15) for j in R16], 30, "b0", "Ih r16h Sp L3")
+        spread("b4", 0, "L3", 16, 48)
+        V(lambda: TC(T.crow[:], T.b4[:, 0:256]), "crow", "b4", 256)
+        S_(lambda: ACT(T.erF[:], T.b4[:, 256:512], F.Copy), "erF", "b4", 256)
+        for r in range(2):
+            V(lambda r=r: TS(T.s16[:, :, r, :], T.su[:, 128 * r:128 * r + 128], -2048.0, None, A.add), "s16", "su", 128, 0.5)
+        V(lambda: v.transpose(T.t16[:], T.s16[:]), "t16", "s16", 256, 0.5)
+        PM([(T.b0[:, 0:256], W1, T.ckb[:], True, False)], 256, "b0", "W1 ckb")
+        PM([(T.b0[:, 128 * r:128 * r + 128], T.W4[:, 2 * r + h, :], T.t16[:, :, 16 * h:16 * h + 16], False, False)
+            for r in range(2) for h in range(2)], 128, "b0", "W4 t16")
+
+        def records(eng, su, buf, out, lo, hi, key, okey):
+            n = hi - lo
+            win = T.R[:, 0:4096].indirect(T[su][:, lo // 16:hi // 16])
+            xo = T[out][:, lo // 256:hi // 256, :]
+            if eng == "v":
+                V(lambda: TT(T[buf][:, lo:hi], win, T.ze[:, lo:hi], A.subtract), key, "R " + su + " " + ZE, n, 1.5)
+                S_(lambda: ACT(xo, T[buf][:, lo:hi], F.Abs), okey, key, n)
+                return
+            bk = "b%d" % (6 + lo // 512 % 2)
+            S_(lambda: ACT(T[buf][:, lo:hi], win, F.Copy), key, "R " + su, n, 1.5)
+            PM([(T[bk][:], Ib, T[buf][:, lo:hi], True, False), (T[bk][:], In, T.ze[:, lo:hi], False, True)], 512, bk, "Ib In " + key + " " + ZE)
+            S_(lambda: ACT(xo, T[bk][:], F.Abs), okey, bk, n)
+
+        for k, (b0, nb) in enumerate(CH):
+            lo, hi = 256 * b0, 256 * (b0 + nb)
+            xl = []
+            for y in range(lo, hi, hi - lo if CM[k] == "v" else 512):
+                xl.append("xa.%d" % y)
+                records(CM[k], "su", "x2", "xa", y, hi if CM[k] == "v" else y + 512, "x2.%d" % y, xl[-1])
+            xl = " ".join(xl)
+            PM([(T.b0[:, 16 * b0:16 * (b0 + nb)], T.Sk[:, j, :], T.xa[:, b0:b0 + nb, 16 * j:16 * j + 16], False, k == len(CH) - 1 and j == 15)
+                for j in R16], 16 * nb, "b0", "Sk " + xl)
+            PM([(T.b1[:, 16 * b0:16 * (b0 + nb)], T.Sb[:, j, :], T.xa[:, b0:b0 + nb, j:256:16], j == 0, j == 15)
+                for j in R16], 16 * nb, "b1", "Sb " + xl)
+        for k in range(8):
+            records(EM[k], "su2", "ve", "xe", 512 * k, 512 * k + 512, "ve.%d" % k, "xe.%d" % k)
+            if k % 2:
+                b0 = 2 * k - 2
+                PM([(T.b2[:, 16 * b0:16 * b0 + 64], T.Sb[:, j, :], T.xe[:, b0:b0 + 4, j:256:16], j == 0, j == 15)
+                    for j in R16], 64, "b2", "Sb xe.%d xe.%d" % (k - 1, k))
+        if t == 0:
+            V(lambda: TC(T.hc[:, 0:1], T.thf[:, 0:1]), "h", "thf", 1)
+        else:
+            V(lambda: TC(T.ai[:], T.b3[:, 128:129]), "ai", "b3", 1)
+            V(lambda: TS(T.ai[:], T.ai[:], 31, None, A.bitwise_and), "ai", "ai", 1)
+            V(lambda t=t: TT(T.hc[:, 0:1], T.ai[:], T.thf[:, t:t + 1], A.add), "h", "ai thf", 1)
+        V(lambda: TS(T.hm[:], T.hA[:], T.hc[:, 0:1], None, A.mult), "hm", "h hA", 4)
+        V(lambda: TT(T.hc[:, 1:5], T.hm[:], T.hB[:], A.add), "hs", "hm hB", 4)
+        V(lambda: v.tensor_tensor_scan(T.sm[:], T.d0n[:], T.b0[:, 0:256], 0.0, A.add, A.min), "sm", "d0n b0", 256)
+        V(lambda: TS(T.sa_[:], T.b1[:, 0:256], T.hc[:, 0:1], 4.0, A.min, A.mult), "sa_", "b1 h", 256)
+        V(lambda: TS(T.sb_[:], T.b1[:, 0:256], T.hc[:, 0:1], 512.0, A.max, A.min), "sb_", "b1 h", 256)
+        V(lambda: TS(T.sq_[:], T.b1[:, 0:256], 512.0, T.hc[:, 3:4], A.is_ge, A.mult), "sq_", "b1 hs", 256)
+        for k, n in enumerate(("sa_", "sb_", "sq_")):
+            PM([(T.b3[:, 16:32], T.Sh[:, j, :], T[n][:, j:256:16], k == 0 and j == 0, k == 2 and j == 15) for j in R16], 16, "b3", "Sh " + n)
+        V(lambda: TS(ps, T.b3[:, 16:32], T.hc[:, 4:5], None, A.is_le), "ps", "b3 hs", 16)
+        sml = T.sm[:, 15:256:16]
+        V(lambda: TS(has, sml, T.hc[:, 1:2], None, A.is_lt), "has", "sm hs", 16)
+        V(lambda: TC(kI, sml), "kI", "sm", 16)
+        V(lambda: TS(ny, kI, 4095, None, A.bitwise_and), "ny", "kI", 16)
+        V(lambda: TT(t3, ny, zt, A.subtract), "t3", "ny zt", 16)
+        V(lambda: TT(t4, t3, has, A.mult), "t4", "t3 has", 16)
+        V(lambda: TT(t5, t4, zt, A.add), "t5", "t4 zt", 16)
+        V(lambda: TC(zo, t5), "zo", "t5", 16)
+        V(lambda: TT(T.xs[:], T.R[:].indirect(zo), T.zh[:], A.add), "xs", "R Rz zh zo", 256, 1.5)
+        V(lambda: TS(T.x4[:], T.xs[:], 16777216.0, 16777216.0, A.add, A.subtract), "x4", "xs", 256, 0.5)
+        V(lambda zout=zout: TS(zout[:], T.x4[:], 0.5, None, A.mult), zo_, "x4", 256, 0.5)
+        send("z", zo_, "zin%d" % (t + 1), t)
+        V(lambda: TC(nyu, ny), "nyu", "ny", 16)
+        V(lambda: TS(T.pg[:], T.PT[:, 0:4096].indirect(nyu), -2048.0, None, A.add), "pg", "PT nyu", 256, 1.5)
+        pick(T.b4[:, 256:272], "pg", "b4")
+        V(lambda: TS(w1, kI, 16, None, A.arith_shift_right), "w1", "kI", 16)
+        V(lambda: TS(w5, w1, 5.0, 5376.0, A.mult, A.add), "w5", "w1", 16)
+        V(lambda fin=fin: TT(w6, w5, fin[:], A.add), "w6", "w5 " + fi, 16)
+        V(lambda fin=fin: TS(f0a, fin[:], 5.0, 10240.0, A.mult, A.add), "f0a", fi, 16)
+        V(lambda: TT(f0, f0a, ui, A.add), "f0", "f0a ui", 16)
+        V(lambda: TT(w6, w6, f0, A.subtract), "w6", "w6 f0", 16)
+        V(lambda: TT(dif, T.b4[:, 256:272], w6, A.add), "dif", "b4 w6", 16)
+        V(lambda: TT(ph, ps, has, A.mult), "ph", "ps has", 16)
+        V(lambda: TT(pdh, ph, dif, A.mult), "pdh", "ph dif", 16)
+        dedupe("EQ", "b5", "v", T.crow, "crow", "cf", "ps")
+        V(lambda: TT(rr, WB, pdh, A.mult), "rr", "b5 pdh", 16)
+        V(lambda: TT(fr, rr, f0, A.add), "fr", "rr f0", 16)
+        V(lambda: TS(fr2, fr, 4095, None, A.bitwise_and), "fr2", "fr", 16)
+        V(lambda fout=fout: TS(fout[:], fr2, -2048.0, None, A.add), fo, "fr2", 16)
+        send("f", fo, "fin%d" % (t + 1), t)
+        V(lambda: TT(T.acc[:, 0:16], WB, ps, A.mult), "acc", "b5 ps", 16)
+        V(lambda: TT(T.acc[:, 16:32], WB, ps, A.mult), "acc2", "b5 ps", 16)
+        if t < NV - 1:
+            S_(lambda: ACT(T.accb[:], T.acc[:, 0:16], F.Copy, accum_out=af), "accb af", "acc", 16)
+            PM([(T.b3[:, 128:129], one, af, True, True)], 256, "b3", "one af")
+        S_(lambda: ACT(T.mM[:], T.b0[:, 0:256], F.Relu, bias=-64.0 * 16777216.0, scale=64.0), "mM", "b0", 256)
+        V(lambda: TT(T.kr[:], T.b0[:, 0:256], T.mM[:], A.subtract), "kr", "b0 mM", 256)
+        V(lambda: v.tensor_tensor_scan(T.sx[:], T.d0x[:], T.kr[:], 0.0, A.add, A.max), "sx", "d0x kr", 256)
+        sxl = T.sx[:, 15:256:16]
+        V(lambda: TC(fI, sxl), "fI", "sx", 16)
+        V(lambda: TS(foe, sxl, T.hc[:, 2:3], None, A.is_ge), "foe", "sx hs", 16)
+        V(lambda: TS(vs, fI, 4095, None, A.bitwise_and), "vs", "fI", 16)
+        V(lambda: TS(vk, vs, -2048.0, None, A.add), "vk", "vs", 16)
+        V(lambda: TS(T.v16[:], vs, -2048.0, None, A.add), "v16", "vs", 16)
+        V(lambda: TT(vrm, vs, tr, A.subtract), "vrm", "vs tr", 16)
+        spread("b4", 0, "v16", 0, 16)
+        V(lambda: TC(T.vrow[:], T.b4[:, 0:256]), "vrow", "b4", 256)
+        V(lambda: TT(flg, foe, T.acc[:, 0:16], A.mult), "flg", "foe acc", 16)
+        dedupe("EQv", "b5", "v", T.vrow, "vrow", "vk", "flg")
+        V(lambda: TT(unq, WB, flg, A.mult), "unq", "b5 flg", 16)
+        V(lambda: TT(dl, unq, vrm, A.mult), "dl", "unq vrm", 16)
+        V(lambda: TT(dl, dl, tr, A.add), "dl", "dl tr", 16)
+        V(lambda: TC(dlu, dl), "dlu", "dl", 16)
+        V(lambda: TC(T.R[:, 0:4352].indirect(dlu), T.s64[:]), "R", "dlu s64", 256, 3.5)
+        V(lambda: TT(T.la[:], T.acc[:], T.RM[:, 0:32], A.mult), "la", "acc acc2 RM", 32)
+        V(lambda: TT(T.la[:], T.la[:], T.T2c[:], A.add), "la", "la T2c", 32)
+        V(lambda: TC(T.lau[:], T.la[:]), "lau", "la", 32)
+        V(lambda zout=zout: TC(T.R[:, 0:4352].indirect(T.lau[:, 0:16]), zout[:]), "R", "lau " + zo_, 256, 3.5)
+        PM([(T.b4[:, 256 + j:512:16], T.Sp[:, j, :], fout[:], True, True) for j in R16], 16, "b4", "Sp " + fo)
+        S_(lambda: ACT(T.phr[:], T.b4[:, 256:512], F.Copy, bias=2048.0), "phr", "b4", 256)
+        V(lambda: TC(T.PT[:].indirect(T.lau[:, 0:16]), T.phr[:]), "PT", "lau phr", 256, 3.5)
+        S_(lambda: ACT(T.sg[:], T.b1[:, 0:256], F.Sign, bias=-511.5), "sg", "b1", 256)
+        PM([(T.b1[:, 256:512], Y1, T.sg[:], True, True)], 256, "b1", "Y1 sg")
+        S_(lambda: ACT(T.b1[:, 256:512], T.b1[:, 256:512], F.Relu, bias=bn), "b1", "bn", 256)
+        V(lambda: TT(T.nd[:], T.b0[:, 256:512], T.sF[:], A.subtract), "nd", "b0 sF", 256)
+        V(lambda: TT(T.nd[:], T.nd[:], T.b1[:, 256:512], A.mult), "nd", "nd b1", 256)
+        V(lambda: TT(T.C[:].indirect(T.lau[:, 16:32]), T.nd[:], T.sF[:], A.add), "C", "lau nd sF", 256, 3.5)
+        S_(lambda: ACT(T.sup[:], T.b2[:, 0:256], F.Relu, bias=T.hc[:, 0:1], scale=-1.0), "sup", "b2 h", 256)
+        S_(lambda: ACT(T.sg2[:], T.b2[:, 0:256], F.Sign, bias=-511.5), "sg2", "b2", 256)
+        PM([(T.b2[:, 256:512], Y2, T.sg2[:], True, True)], 256, "b2", "Y2 sg2")
+        S_(lambda: ACT(T.b2[:, 256:512], T.b2[:, 256:512], F.Relu, bias=bx), "b2", "bx", 256)
+        PM([(T.b7[:, 0:16], T.Sb[:, j, :], T.sup[:, j:256:16], j == 0, j == 15) for j in R16], 16, "b7", "Sb sup")
+        V(lambda: TS(cn0, T.b7[:, 0:16], 0.0, None, A.is_equal), "cn0", "b7", 16)
+        V(lambda: TT(cnd, cn0, T.acc[:, 0:16], A.mult), "cnd", "cn0 acc", 16)
+        dedupe("EQe", "b6", "a", T.erF, "erF", "nek", "cnd")
+        V(lambda: TT(w2, T.b6[:, 256:272], cnd, A.mult), "w2", "b6 cnd", 16)
+        V(lambda: TT(l2, w2, T.RM[:, 32:48], A.mult), "l2", "w2 RM", 16)
+        V(lambda: TT(l2, l2, tc, A.add), "l2", "l2 tc", 16)
+        V(lambda: TC(l2u, l2), "l2u", "l2", 16)
+        S_(lambda: ACT(T.sF2[:], T.C[:, 0:1024].indirect(eu), F.Copy), "sF2", "C eu", 256, 1.5)
+        V(lambda: TT(T.nd2[:], T.b0[:, 256:512], T.sF2[:], A.subtract), "nd2", "b0 sF2", 256)
+        V(lambda: TT(T.nd2[:], T.nd2[:], T.b2[:, 256:512], A.mult), "nd2", "nd2 b2", 256)
+        V(lambda: TT(T.C[:].indirect(l2u), T.nd2[:], T.sF2[:], A.add), "C", "l2u nd2 sF2", 256, 3.5)
+    D("yrec", T.yrec[:], T.R[:, 0:4096], "", "R", 6.0)
+    D("ycel", T.ycel[:], T.C[:, 0:1024], "", "C", 4.0, "a")
+    D("ypo", T.ypo[:], T.PT[0:128:16, 0:4096], "", "PT", 3.0)
+    zl, fl = "zin%d" % NV, "fin%d" % NV
+    D("ypat", T.ypat[:], T[zl][:], "", zl, 2.0)
+    spread("b4", 0, fl, 0, 16)
+    V(lambda: TS(T.phr[:], T.b4[:, 0:256], 2048.0, None, A.add), "phr", "b4", 256)
+    D("yphi", T.yphi[:], T.phr[0:128:16, :], "", "phr", 2.0)
+    return ops
+
+
+def schedule(ops):
+    n = len(ops)
+    succ = [[] for _ in ops]
+    need = [0] * n
+    for o in ops:
+        deps = o["wait"] | o["ord"] | ({o["net"]} if o["net"] is not None else set())
+        need[o["i"]] = len(deps)
+        for x in sorted(deps):
+            succ[x].append(o["i"])
+    pri = [0.0] * n
+    for i in range(n - 1, -1, -1):
+        pri[i] = ops[i]["d"] + max([pri[k] + 0.1 for k in succ[i]] or [0.0])
+    free = {q: 0.0 for q in "vapgs"}
+    ready = {q: [] for q in "vapgsn"}
+    at = [0.0] * n
+    for i in range(n):
+        if need[i] == 0:
+            ready[ops[i]["q"]].append(i)
+    order = []
+    while len(order) < n:
+        st, q = min((max(free.get(q, 0.0), min(at[i] for i in L)), q) for q, L in ready.items() if L)
+        i = max((i for i in ready[q] if at[i] <= st + 1e-9), key=lambda i: pri[i])
+        ready[q].remove(i)
+        o = ops[i]
+        if q != "n":
+            free[q] = st + (o["d"] if o["sem"] is None else 0.1)
+        end = st + o["d"]
+        order.append(i)
+        for k in succ[i]:
+            need[k] -= 1
+            same = ops[k]["q"] == q
+            at[k] = max(at[k], st if same and i not in ops[k]["wait"] else end + (0.03 if same else 0.1))
+            if need[k] == 0:
+                ready[ops[k]["q"]].append(k)
+    return order
+
+
+def rank_program(g, core, T, topo):
+    rank = T.rank_of(core)
+    if rank is None:
+        return
+    nxt = T.cores[(rank + 1) % len(T.cores)]
+    ops = program(T, g, core, nxt, topo)
+    eng = {"v": g.vector, "a": g.scalar, "p": g.tensor, "g": g, "s": g.sync}
+    cnt = {q: 0 for q in "vapg"}
+    seen = {q: {} for q in "vapgs"}
+    clock, ev, final = {}, {}, {}
+    for i in schedule(ops):
+        o = ops[i]
+        q = o["q"]
+        if q == "n":
+            ev[i] = (o["sem"], o["val"])
+            clock[i] = {o["sem"]: o["val"]}
+            final[o["sem"]] = o["val"]
+            continue
+        for x in sorted(o["wait"], key=lambda x: (-ev[x][1], x)):
+            sm, val = ev[x]
+            if seen[q].get(sm, 0) < val:
+                eng[q].wait_ge(T.sem[sm], val)
+                for k, y in clock[x].items():
+                    if seen[q].get(k, 0) < y:
+                        seen[q][k] = y
+        for f in o["f"]:
+            ins = f()
+            if o["sem"] is None:
+                ins.then_inc(T.sem["q" + q], 1)
+                cnt[q] += 1
+            elif o["sem"][0] == "d":
+                ins.then_inc(T.sem[o["sem"]], 16)
+        ev[i] = (o["sem"], o["val"]) if o["sem"] else ("q" + q, cnt[q])
+        clock[i] = dict(seen[q])
+        clock[i][ev[i][0]] = ev[i][1]
+        final[ev[i][0]] = ev[i][1]
+    for sm, val in final.items():
+        g.wait_ge(T.sem[sm], val)

@@ -1,40 +1,46 @@
 from concourse.mybir import AluOpType as A, AxisListType, ActivationFunctionType as F
 
 NV = 4
-CH = [(0, 4), (4, 4), (8, 4), (12, 4)]
-CM = ["a", "v", "a", "v"]
-ZM = ["g", "a"] * 8
-EM = ["v", "v", "v", "v", "v", "a", "a", "a"]
-TRN = 3.0
-CY = 0.83e-3 * 1.2
+CM = [(0, 64, "c"), (64, 64, "c"), (128, 64, "b"), (192, 64, "b")]
+EM = [(0, 64, "c"), (64, 64, "c"), (128, 64, "c"), (192, 64, "c")]
+VP = 32
+EP = [(0, 12), (12, 16)]
+ZE0, ZE = "va" * 8, "ga" * 8
+EVAC = "a"
+PTG = 2816
+TRN = 4.5
+KMAX, OWN = "v", "a"
+ROUNDS, SPAN, JIT = 1500, 12.0, 4.0
+ORDER = []
+CY, PE, WAKE = 0.9e-3, 0.45e-3, 0.25
+GA, SC = 1.56, 3.8
+BIG = 16384.0
 
 B, H, F4, I4, U2 = "bfloat16", "float16", "float32", "int32", "uint16"
 SHAPES = {
-    B: "R:4608 x2:4096 ze:4096 ve:4096 sup:256 sg:256 sg2:256 xs:256 x4:256 zh:256 ckb:256 mM:256 s64:256 accb:16",
-    H: "crow:256 vrow:256 winr:256 sa_:256 sb_:256 sq_:256 pg:256 phh:256 thh:4 Bh:128 Ih:128 r16h:256 L3:48 v16:16",
-    F4: "C:1280 PT:4352 posf:256 erF:256 sF:256 sF2:256 nd:256 nd2:256 sm:256 kr:256 sx:256 phr:256 thf:4 hc:8 hA:4 hB:4 hm:4 "
-        "B8a:8 B8:8 g16:8 g16b:8 K3:48 rc:2 Cr:256 d0n:256 d0x:256 ck:256 par:2 r16:256 RM:48 acc:32 T2c:32 la:32 col:16",
+    B: "R:4352 xg:4096 xa:4096 eg:4096 ea:4096 sup:256 mM:256 sg2:256 xs:256 x4:256 ck:512 s64:256 on:256 accb:16 k16:32 "
+       "Wb:144 W2:144 Wn:144 W3:144 Ww:144 Vs:240",
+    H: "rows:512 vrow:256 s16:256 nrow:256 pg:256 phh:256 thh:4 L3:32 v16:16 mneg:16 uh:16 w5h:16",
+    F4: "C:1280 PT:4352 posf:256 sF:256 sF2:256 a1:256 a2:256 n1:256 n2:256 phr:256 thf:4 hc:4 hB:4 kr:256 Iw:160 thr:128 "
+        "B8a:8 B8:8 g16:8 g16b:8 K3:48 rc:2 d0n:256 d0x:256 RM:48 kf:32 T2c:32 la:32 col:16",
     I4: "Ci:1024 pos:256 phl:256 thl:4 wl:1 ai:1 CI:48",
     U2: "su:256 su2:256 lau:32",
 }
-LF = "u32 has t3 t4 t5 ps pdh w5 w6 f0 f0a dif ph rr dl l2 foe flg vk unq cnd cn0 w2 vrm nek cf jr I16 b256 i16 zt iL tr tc pw pwb".split()
+LF = "u32 nh t3 t4 tq ps ph pdh rr acc dl l2 foe flg vk fv cnd cr vrm jr I16 b256 i16 iL tr tc pw pwb hf".split()
 LI = "ui u2 xq xr ye kI ny w1 fI vs fr fr2".split()
-LU = "cu eu zo nyu dlu l2u".split()
-MB = "Bb W1 Do Dg Zb Ib In Y1 Y2".split()
-MF = "one idf Bba Bf shp shm Utf Ulf".split()
+LU = "cu eu zo dlu l2u".split()
+MB = "Ib In I5 I4n I6 Y1 Y2 Y2c".split()
+MF = "one Bba Bta Bt Utf Ulf".split()
 SCRATCH = {}
 for _d, _l in SHAPES.items():
     for _x in _l.split():
         SCRATCH[_x.split(":")[0]] = ("sbuf", [128, int(_x.split(":")[1])], _d)
-for _x in ("xa", "xe", "EQ", "EQe", "EQv"):
-    SCRATCH[_x] = ("sbuf", [128, 16, 256], B)
-for _x, _d in (("Sb", B), ("Sk", B), ("Sw", B), ("Sh", H), ("Pk", H), ("Sp", H)):
-    SCRATCH[_x] = ("sbuf", [128, 16, 128], _d)
-for _x, _l, _n, _d in (("lf", LF, 16, F4), ("li", LI, 16, I4), ("lu", LU, 16, U2), ("mb", MB, 128, B), ("mf", MF, 128, F4)):
-    SCRATCH[_x] = ("sbuf", [128, len(_l), _n], _d)
-SCRATCH["s16"] = ("sbuf", [128, 8, 2, 16], H)
-SCRATCH["t16"] = ("sbuf", [128, 8, 32], H)
-SCRATCH["W4"] = ("sbuf", [128, 4, 128], H)
+for _x, _s, _d in (("EQ", [16, 256], B), ("EQe", [16, 256], B), ("EQv", [16, 256], B), ("ze", [4096], B), ("Sp", [16, 128], B),
+                   ("Bf", [8, 16], F4), ("Wt", [8, 16], B), ("Xm", [2, 8, 8], B), ("W4", [12, 128], B), ("T2", [3, 256], H),
+                   ("ts", [8, 32], H), ("td", [8, 32], H), ("tx", [8, 32], H), ("sm", [256], F4), ("sx", [256], F4),
+                   ("lf", [len(LF), 16], F4), ("li", [len(LI), 16], I4), ("lu", [len(LU), 16], U2), ("mb", [len(MB), 128], B),
+                   ("mf", [len(MF), 128], F4)):
+    SCRATCH[_x] = ("sbuf", [128] + _s, _d)
 for _t in range(NV + 1):
     SCRATCH["zin%d" % _t] = ("sbuf", [128, 256], B)
     SCRATCH["fin%d" % _t] = ("sbuf", [128, 16], H)
@@ -47,35 +53,31 @@ DMAS = ["rec", "cel", "wt", "pat", "phi", "th", "po", "pt", "yrec", "ycel", "ypo
 SEMAPHORES = ["qv", "qa", "qp", "qg"] + ["d" + n for n in DMAS] + ["%s%d" % (k, t) for k in ("zr", "zl", "fr", "fl") for t in range(NV)]
 
 
-def dv(n, rate=1.0, k=1):
-    return k * max(64, n * rate + 12) * CY
-
-
-def dp(n, k=1):
-    return k * max(64, n) * 0.45e-3 + 0.03
+def dv(n, rate=1.0):
+    return 0.055 + n * rate * CY if rate > 1.2 else max(64, n * rate) * CY
 
 
 def program(T, g, me, nxt, topo):
     v, a, p, s = g.vector, g.scalar, g.tensor, g.sync
     ops = []
-    last = {}
+    last, tags, now = {}, set(), [-1]
 
     def add(q, fns, w, r, d, sem=None, val=0, net=None):
-        o = {"q": q, "f": fns, "d": d, "sem": sem, "val": val, "i": len(ops), "wait": set(), "ord": set(), "net": net}
         rs, ws = r.split(), w.split()
+        o = {"q": q, "f": fns, "d": d, "sem": sem, "val": val, "i": len(ops), "wait": set(), "ord": set(), "net": net,
+             "bank": sorted(set(k[:2] for k in rs + ws if k[0] == "b" and k[2:3] == "."))}
+        name = "".join(c for c in w if c != str(now[0]) and c != str(now[0] + 1)) if "in" in w or "out" in w else w or "send " + r[0]
+        while (name, now[0]) in tags:
+            name += "+"
+        o["tag"] = (name, now[0])
+        tags.add(o["tag"])
         for key in sorted(set(rs + ws)):
             L = last.setdefault(key, [None, []])
-            if key[0] == "b" and key[1:].isdigit():
-                if L[0] is not None:
-                    free = ops[L[0]]["q"] == q and (q == "p" or not L[1])
-                    o["ord" if free else "wait"].add(L[0])
-                last[key] = [o["i"], key in ws]
-                continue
             if key in rs and L[0] is not None:
                 o["wait"].add(L[0])
             if key in ws:
                 for x in ([L[0]] if L[0] is not None else []) + L[1]:
-                    o["ord" if ops[x]["q"] == q and ops[x]["sem"] is None and x != L[0] else "wait"].add(x)
+                    o["ord" if ops[x]["q"] == q and ops[x]["sem"] is None and (x != L[0] or q == "p") else "wait"].add(x)
                 last[key] = [o["i"], []]
             else:
                 L[1].append(o["i"])
@@ -90,10 +92,10 @@ def program(T, g, me, nxt, topo):
         return add("a", [fn], w, r, dv(n, rate))
 
     def G(fn, w, r, n):
-        return add("g", [fn], w, r, 0.2 + 2 * n * CY)
+        return add("g", [fn], w, r, 0.17 + 2 * n * CY)
 
     def PM(args, n, w, r):
-        return add("p", [(lambda x=x: p.matmul(*x)) for x in args], w, r, dp(n, len(args)))
+        return add("p", [(lambda x=x: p.matmul(*x)) for x in args], w, r, len(args) * max(64, n) * PE)
 
     def D(name, out, in_, w, r, d, q="s"):
         return add(q, [lambda: (s if q == "s" else a).dma_start(out, in_)], w, r, d, "d" + name, 16)
@@ -101,138 +103,137 @@ def program(T, g, me, nxt, topo):
     TS, TT, TC, MS, ACT = v.tensor_scalar, v.tensor_tensor, v.tensor_copy, v.memset, a.activation
     RED = lambda out, in_: v.tensor_reduce(out, in_, AxisListType.X, A.add)
     R16 = range(16)
-    (u32, has, t3, t4, t5, ps, pdh, w5, w6, f0, f0a, dif, ph, rr, dl, l2, foe, flg, vk, unq, cnd, cn0, w2, vrm, nek, cf, jr, I16, b256, i16, zt, iL,
-     tr, tc, pw, pwb) = [T.lf[:, k, :] for k in range(len(LF))]
+    (u32, nh, t3, t4, tq, ps, ph, pdh, rr, acc, dl, l2, foe, flg, vk, fv, cnd, cr, vrm, jr, I16, b256, i16, iL, tr, tc, pw, pwb,
+     hf) = [T.lf[:, k, :] for k in range(len(LF))]
     ui, u2, xq, xr, ye, kI, ny, w1, fI, vs, fr, fr2 = [T.li[:, k, :] for k in range(len(LI))]
-    cu, eu, zo, nyu, dlu, l2u = [T.lu[:, k, :] for k in range(len(LU))]
-    Bb, W1, Do, Dg, Zb, Ib, In, Y1, Y2 = [T.mb[:, k, :] for k in range(len(MB))]
-    one, idf, Bba, Bf, shp, shm, Utf, Ulf = [T.mf[:, k, :] for k in range(len(MF))]
-    pc, gs, jc, j16, p2, wf, bn, bx, af = [T.col[:, k:k + 1] for k in range(9)]
-    lfc = lambda name, b: T.lf[:, LF.index(name), b:b + 1]
+    cu, eu, zo, dlu, l2u = [T.lu[:, k, :] for k in range(len(LU))]
+    Ib, In, I5, I4n, I6, Y1, Y2, Y2c = [T.mb[:, k, :] for k in range(len(MB))]
+    one, Bba, Bta, Bt, Utf, Ulf = [T.mf[:, k, :] for k in range(len(MF))]
+    pc, gs, jc, j16, p2, p3, wf, af, am, k2 = [T.col[:, k:k + 1] for k in range(10)]
+    lfc = lambda name, lo, hi=None: T.lf[:, LF.index(name), lo:hi or lo + 1]
+    row = lambda name, j: T[name][:, 15 - j:143 - j]
+    idf = T.Iw[:, 16:144]
 
-    def pick(out, src, bank):
-        PM([(out, T.Pk[:, j, :], T[src][:, j:256:16], j == 0, j == 15) for j in R16], 16, bank, "Pk " + src)
+    def evac(out, in_, w, r, n, bias=0.0):
+        if EVAC == "a":
+            return S_(lambda: ACT(out, in_, F.Copy, bias=bias), w, r, n)
+        return V(lambda: TS(out, in_, bias, None, A.add), w, r, n)
 
-    def spread(bank, off, src, lo, hi):
-        PM([(T[bank][:, off + j:off + 16 * (hi - lo):16], T.Sp[:, j, :], T[src][:, lo:hi], True, True) for j in R16], hi - lo, bank, "Sp " + src)
+    def spread(bank, off, src, n, key):
+        PM([(T[bank][:, off + j:off + 16 * n:16], T.Sp[:, j, :], T[src][:, 0:n], True, True) for j in R16], n, key, "Sp " + src)
 
     V(lambda: MS(T.phl[:], 0), "phl", "", 256)
     V(lambda: MS(T.thl[:], 0), "thl", "", 4)
+    D("rec", T.R[:, 0:4096], T.rec[:], "R", "", 7.0, "a")
     D("pat", T.zin0[:], T.pat[:], "zin0", "", 2.0)
     D("wt", T.wl[:], T.wt[:], "wl", "", 2.0)
     D("phi", T.phl[0:128:16, :], T.phi[:], "phl", "", 2.0)
-    D("cel", T.Ci[:], T.cel[:], "Ci", "", 3.5)
-    D("rec", T.R[:, 0:4096], T.rec[:], "R", "", 6.0, "a")
+    D("cel", T.Ci[:], T.cel[:], "Ci", "", 4.0)
     D("th", T.thl[0:128:16, :], T.th[:], "thl", "", 2.0)
-    D("po", T.pos[:], T.po[:], "pos", "", 2.0)
-    V(lambda: MS(one, 1.0), "one", "", 128)
+    D("po", T.pos[:], T.po[:], "pos", "", 2.5)
     iota = lambda out, pat, base=0, cm=0: g.iota(out, pat, base, cm, allow_small_or_imprecise_dtypes=True)
     sel = lambda out, in_, pat, op, base, cm: g.affine_select(out, in_, pat, op, 0.0, base, cm)
+    V(lambda: MS(one, 1.0), "one", "", 128)
+    V(lambda: MS(T.Iw[:], 1.0), "Iw", "", 160)
     G(lambda: sel(T.B8a[:], T.mf[:, 0, 0:8], [[-16, 8]], A.is_ge, 0, 1), "B8a", "one", 8)
     G(lambda: sel(T.B8[:], T.B8a[:], [[16, 8]], A.is_ge, 15, -1), "B8", "B8a", 8)
     G(lambda: iota(T.g16[:], [[16, 8]]), "g16", "", 8)
     G(lambda: iota(pc, [[0, 1]], 0, 1), "pc", "", 1)
     G(lambda: iota(jr, [[1, 16]]), "jr", "", 16)
     G(lambda: iota(b256, [[256, 16]]), "b256", "", 16)
-    G(lambda: sel(idf, one, [[-1, 128]], A.is_equal, 0, 1), "idf", "one", 128)
+    G(lambda: sel(T.Iw[:], T.Iw[:], [[-1, 160]], A.is_equal, 16, 1), "Iw", "Iw", 160)
     G(lambda: sel(Bba, one, [[-16, 8], [0, 16]], A.is_ge, 0, 1), "Bba", "one", 128)
-    G(lambda: sel(Bf, Bba, [[16, 8], [0, 16]], A.is_ge, 15, -1), "Bf", "Bba", 128)
-    V(lambda: MS(T.Sb[:], 0.0), "Sb", "", 2048, 0.5)
-    add("v", [(lambda j=j: TC(T.Sb[:, j, j:128:16], T.B8[:])) for j in R16], "Sb", "B8", dv(8, 1, 16))
+    G(lambda: sel(T.Bf[:], Bba, [[16, 8], [0, 16]], A.is_ge, 15, -1), "Bf", "Bba", 128)
+    G(lambda: sel(Bta, one, [[0, 16], [-16, 8]], A.is_ge, 0, 1), "Bta", "one", 128)
+    G(lambda: sel(Bt, Bta, [[0, 16], [16, 8]], A.is_ge, 15, -1), "Bt", "Bta", 128)
+    G(lambda: sel(Utf, T.Bf[:], [[1, 128]], A.is_gt, 0, -1), "Utf", "Bf", 128)
+    G(lambda: sel(Ulf, T.Bf[:], [[-1, 128]], A.is_gt, 0, 1), "Ulf", "Bf", 128)
+    G(lambda: iota(T.ck[:, 0:256], [[0, 16], [4096, 16]], 2048), "ck0", "", 256)
+    V(lambda: TS(T.ck[:, 256:512], T.ck[:, 0:256], -1.0, 65536.0, A.mult, A.add), "ck", "ck0", 256, 0.5)
+    G(lambda: iota(T.PT[:, 0:PTG], [[0, PTG]]), "PT", "B8 Iw Bf Bt Utf Ulf ck0 jr pc g16 b256", PTG)
+    V(lambda: MS(T.PT[:, PTG:4352], 0.0), "PT1", "", 4352 - PTG)
+    V(lambda: MS(T.Wb[:], 0.0), "Wb", "", 144, 0.5)
+    V(lambda: TC(T.Wb[:, 15:128:16], T.B8[:]), "Wb", "B8", 8)
     V(lambda: TC(wf, T.wl[:]), "wf", "wl", 1)
-    V(lambda: TS(T.Sw[:], T.Sb[:], wf, None, A.mult), "Sw", "Sb wf", 2048, 0.5)
+    for name, x in (("Ww", wf), ("W2", 2.0), ("Wn", -1.0), ("W3", 3.0)):
+        V(lambda name=name, x=x: TS(T[name][:], T.Wb[:], x, None, A.mult), name, "Wb wf" if name == "Ww" else "Wb", 144, 0.5)
     V(lambda: TC(T.C[:, 0:1024], T.Ci[:]), "C", "Ci", 1024)
     V(lambda: MS(T.C[:, 1024:1280], 0.0), "C", "", 256)
-    S_(lambda: ACT(T.Sk[:], T.Sb[:], F.Copy, scale=65536.0), "Sk", "Sb", 2048)
     V(lambda: TT(T.g16b[:], T.g16[:], T.B8[:], A.mult), "g16b", "g16 B8", 8)
     V(lambda: RED(gs, T.g16b[:]), "gs", "g16b", 8)
     V(lambda: TT(jc, pc, gs, A.subtract), "jc", "pc gs", 1)
     V(lambda: TS(I16, jr, jc, None, A.is_equal), "I16", "jr jc", 16)
+    V(lambda: TS(k2, lfc("I16", 0), 2048.0, None, A.mult), "k2", "I16", 1)
     V(lambda: TS(j16, jc, 16.0, None, A.mult), "j16", "jc", 1)
-    V(lambda: TS(bn, jc, -1.0, None, A.mult), "bn", "jc", 1)
-    V(lambda: TS(bx, jc, -15.0, None, A.add), "bx", "jc", 1)
     V(lambda: TS(i16, b256, j16, None, A.add), "i16", "b256 j16", 16)
-    V(lambda: TS(iL, i16, 0.0625, None, A.mult), "iL", "i16", 16)
-    V(lambda: TS(tr, iL, 4096.0, None, A.add), "tr", "iL", 16)
-    V(lambda: TS(tc, iL, 1024.0, None, A.add), "tc", "iL", 16)
-    V(lambda: TS(zt, iL, 4352.0, None, A.add), "zt", "iL", 16)
+    V(lambda: TS(tr, i16, 0.0625, 4096.0, A.mult, A.add), "tr", "i16", 16)
+    V(lambda: TS(tc, i16, 0.0625, 1024.0, A.mult, A.add), "tc", "i16", 16)
+    V(lambda: TS(iL, i16, -1.0, 2048.0, A.mult, A.add), "iL", "i16", 16)
     V(lambda: TT(T.K3[:, 0:16], tr, i16, A.subtract), "K3", "i16 tr", 16)
     V(lambda: TC(T.K3[:, 16:32], tc), "K3", "tc", 16)
     V(lambda: TC(T.K3[:, 32:48], tc), "K3", "tc", 16)
     V(lambda: TC(T.T2c[:, 0:16], tr), "T2c", "tr", 16)
     V(lambda: TC(T.T2c[:, 16:32], tc), "T2c", "tc", 16)
-    for k, (x, y) in enumerate(((65536.0, -16777216.0), (65536.0, 61440.0 - 16777216.0), (1.0, -512.0), (80.0, 0.0))):
-        V(lambda k=k, x=x: MS(T.hA[:, k:k + 1], x), "hA", "", 1)
+    for k, y in enumerate((0.0, -512.0, -256.0, -256.0 if KMAX == "p" else -255.0625)):
         V(lambda k=k, y=y: MS(T.hB[:, k:k + 1], y), "hB", "", 1)
-    V(lambda: TC(T.Sh[:], T.Sb[:]), "Sh", "Sb", 2048, 0.5)
-    V(lambda: TS(T.Pk[:], T.Sb[:], lfc("I16", 0), None, A.mult), "Pk", "Sb I16", 2048, 0.5)
-    V(lambda: TC(Bb, Bf), "Bb", "Bf", 128)
-    V(lambda: TC(T.Bh[:], Bf), "Bh", "Bf", 128)
-    add("v", [(lambda j=j: TS(T.Sp[:, j, :], Bb, lfc("I16", j), None, A.mult)) for j in R16], "Sp", "Bb I16", dv(128, 0.5, 16))
+    add("a", [(lambda j=j: ACT(T.Sp[:, j, :], T.Bf[:], F.Copy, scale=lfc("I16", j))) for j in R16], "Sp", "Bf I16", 16 * dv(128))
     V(lambda: RED(T.rc[:, 0:1], T.B8[:, 0:8:2]), "rc", "B8", 4)
     V(lambda: RED(T.rc[:, 1:2], T.B8[:, 1:8:2]), "rc", "B8", 4)
-    G(lambda: sel(shp, one, [[-1, 128]], A.is_equal, 16, 1), "shp", "one", 128)
-    G(lambda: sel(shm, one, [[-1, 128]], A.is_equal, -16, 1), "shm", "one", 128)
-    for k, (src, key, r) in enumerate(((idf, "idf", 0), (shp, "shp", 0), (shm, "shm", 1), (idf, "idf", 1))):
-        V(lambda k=k, src=src, r=r: TS(T.W4[:, k, :], src, T.rc[:, r:r + 1], None, A.mult), "W4", key + " rc", 128)
-    G(lambda: iota(T.ck[:], [[0, 16], [4096, 16]], 2048), "ck", "", 256)
-    V(lambda: RED(T.par[:, 0:1], T.lf[:, LF.index("I16"), 0:16:2]), "par", "I16", 8)
-    V(lambda: TS(T.par[:, 1:2], T.par[:, 0:1], 16777216.0, -16777216.0, A.mult, A.add), "par", "par", 1)
-    V(lambda: TS(T.ckb[:], T.ck[:], T.par[:, 0:1], T.par[:, 1:2], A.mult, A.add), "ckb", "ck par", 256)
-    V(lambda: MS(W1, 0.015625), "W1", "", 128, 0.5)
-    G(lambda: iota(T.r16[:], [[16, 256]]), "r16", "", 256)
-    V(lambda: TC(T.r16h[:], T.r16[:]), "r16h", "r16", 256)
-    V(lambda: TC(T.Ih[:], idf), "Ih", "idf", 128)
-    V(lambda: TC(Ib, idf), "Ib", "idf", 128)
-    V(lambda: TS(In, idf, -1.0, None, A.mult), "In", "idf", 128)
+    for k, (x, r) in enumerate(((16, 0), (0, 0), (32, 1), (16, 1))):
+        V(lambda k=k, x=x, r=r: TS(T.W4[:, k, :], T.Iw[:, x:x + 128], T.rc[:, r:r + 1], None, A.mult), "W4", "Iw rc", 128)
+    V(lambda: TS(T.W4[:, 4:8, :], T.W4[:, 0:4, :], 65536.0, None, A.mult), "W4d", "W4", 512, 0.5)
+    V(lambda: TS(T.W4[:, 8:12, :], T.W4[:, 0:4, :], 67108864.0, None, A.mult), "W4x", "W4", 512, 0.5)
+    for m, name, x in ((Ib, "Ib", 1.0), (In, "In", -1.0), (I5, "I5", 5.0), (I4n, "I4n", -4.0), (I6, "I6", 6144.0)):
+        S_(lambda m=m, x=x: ACT(m, idf, F.Copy, scale=x), name, "Iw", 128)
     V(lambda: MS(T.d0n[:], 0.0), "d0n", "", 256)
     V(lambda: MS(T.d0n[:, 0:256:16], 134217728.0), "d0n", "", 16)
-    add("v", [(lambda j=j: MS(T.Cr[:, j:256:16], float(2 ** (16 - j)))) for j in R16], "Cr", "", dv(16, 1, 16))
-    V(lambda: TS(pw, T.Cr[:, 0:16], 0.5, None, A.mult), "pw", "Cr", 16)
+    V(lambda: MS(T.d0x[:], 0.0 if KMAX == "p" else 8192.0), "d0x", "", 256)
+    V(lambda: MS(T.d0x[:, 0:256:16], -268435456.0), "d0x", "", 16)
+    V(lambda: MS(hf, 0.5), "hf", "", 16)
+    V(lambda: v.tensor_tensor_scan(pw, hf, hf, 65536.0, A.mult, A.max), "pw", "hf", 16)
     V(lambda: TT(pwb, pw, I16, A.mult), "pwb", "pw I16", 16)
     V(lambda: RED(p2, pwb), "p2", "pwb", 16)
-    V(lambda: TS(Do, Bb, 65536.0, None, A.mult), "Do", "Bb", 128, 0.5)
-    V(lambda: TS(Dg, Bb, p2, None, A.mult), "Dg", "Bb p2", 128, 0.5)
-    V(lambda: MS(Zb, 0.0), "Zb", "", 128, 0.5)
+    V(lambda: TS(p3, p2, 2.0, 1.0, A.mult, A.add), "p3", "p2", 1)
+    V(lambda: TS(T.thr[:], Bt, p3, -1.0, A.mult, A.add), "thr", "Bt p3", 128)
+    V(lambda: MS(T.Wt[:, :, 0:7], 0.0), "Wt", "", 56, 0.5)
+    V(lambda: TS(T.Wt[:, :, 7], T.B8[:], p2, None, A.mult), "Wt", "B8 p2", 8)
+    V(lambda: TS(T.Wt[:, :, 8:16], T.Bf[:, :, 0:8], 65536.0, None, A.mult), "Wt", "Bf", 64)
+    V(lambda: MS(T.Vs[:], 0.0), "Vs", "", 240, 0.5)
+    V(lambda: TC(T.Vs[:, 112:128], I16), "Vs", "I16", 16)
     V(lambda: MS(T.s64[:], 64.0), "s64", "", 256, 0.5)
-    V(lambda: MS(T.d0x[:], 8192.0), "d0x", "", 256)
-    V(lambda: MS(T.d0x[:, 0:256:16], -268435456.0), "d0x", "", 16)
-    G(lambda: sel(Utf, Bf, [[1, 128]], A.is_gt, 0, -1), "Utf", "Bf", 128)
-    G(lambda: sel(Ulf, Bf, [[-1, 128]], A.is_gt, 0, 1), "Ulf", "Bf", 128)
-    V(lambda: TT(Y1, idf, Utf, A.subtract), "Y1", "idf Utf", 128, 2)
-    V(lambda: TT(Y2, idf, Ulf, A.subtract), "Y2", "idf Ulf", 128, 2)
-    G(lambda: iota(T.PT[:], [[0, 4352]]), "PT", "", 4352)
-    V(lambda: MS(T.R[:, 4096:4352], 0.0), "R", "", 256, 0.5)
+    V(lambda: MS(T.on[:], 1.0), "on", "", 256, 0.5)
+    V(lambda: MS(T.k16[:, 0:16], -16384.0), "k16", "", 16)
+    V(lambda: MS(T.k16[:, 16:32], 3328.0), "k16", "", 16)
+    V(lambda: TT(Utf, idf, Utf, A.subtract), "Utf", "Iw Utf", 128, 2)
+    V(lambda: TT(Ulf, idf, Ulf, A.subtract), "Ulf", "Iw Ulf", 128, 2)
+    for m, name, src, key, x in ((Y1, "Y1", Utf, "Utf", BIG), (Y2, "Y2", Ulf, "Ulf", -BIG / 2)):
+        S_(lambda m=m, src=src, x=x: ACT(m, src, F.Copy, scale=x), name, key, 128)
+    V(lambda: TT(Y2c, Y2, I6, A.add), "Y2c", "Y2 I6", 128)
     V(lambda: TC(T.thh[:], T.thl[:]), "thh", "thl", 4)
-    PM([(T.b3[:, 64:68], T.Bh[:], T.thh[:], True, True)], 4, "b3", "Bh thh")
-    V(lambda: TC(T.thf[:], T.b3[:, 64:68]), "thf", "b3", 4)
-    V(lambda: TS(T.phh[:], T.phl[:], -2048.0, None, A.add), "phh", "phl", 256)
-    pick(T.b5[:, 256:272], "phh", "b5")
-    V(lambda: TC(T.fin0[:], T.b5[:, 256:272]), "fin0", "b5", 16)
+    PM([(T.b3[:, 132:136], T.Sp[:, 0, :], T.thh[:], True, True)], 4, "b3.th", "Sp thh")
+    V(lambda: TC(T.thf[:], T.b3[:, 132:136]), "thf", "b3.th", 4)
+    V(lambda: TS(T.phh[:], T.phl[:], -2048.0, lfc("I16", 0), A.add, A.mult), "phh", "phl I16", 256)
+    PM([(T.b5[:, 256:272], row("Wb", j), T.phh[:, j:256:16], j == 0, j == 15) for j in R16], 16, "b5.w", "Wb phh")
+    V(lambda: TC(T.fin0[:], T.b5[:, 256:272]), "fin0", "b5.w", 16)
     V(lambda: TC(T.posf[:], T.pos[:]), "posf", "pos", 256)
-    D("pt", T.PT[0:128:16, 0:4096], T.posf[:], "PT", "posf", 2.5)
+    D("pt", T.PT[0:128:16, 0:4096], T.posf[:], "PT PT1", "posf", 2.5)
 
-    def dedupe(eq, bank, eng, row, rkey, key, flag):
-        for q in range(4):
-            bs = range(4 * q, 4 * q + 4)
-            e = lambda b: T[eq][:, b, 0:256 - 16 * b]
-            ek = "%s.%d" % (eq, q)
-            if eng == "v":
-                add("v", [(lambda b=b: TS(e(b), row[:, 16 * b:256], lfc(key, b), lfc(flag, b), A.is_equal, A.mult)) for b in bs],
-                    ek, "%s %s %s" % (rkey, key, flag), sum(dv(256 - 16 * b, 0.5) for b in bs))
-            else:
-                d = sum(dv(256 - 16 * b) for b in bs)
-                add("a", [(lambda b=b: ACT(e(b), row[:, 16 * b:256], F.Square, bias=lfc(key, b))) for b in bs], ek, rkey + " " + key, d)
-                add("a", [(lambda b=b: ACT(e(b), e(b), F.Relu, bias=lfc(flag, b), scale=-1.0)) for b in bs], ek, ek + " " + flag, d)
-        for q in range(4):
-            bs = range(4 * q, 4 * q + 4)
-            ms = [] if q else [(T[bank][:, 0:256], Zb, T.s64[:], True, False)]
-            ms += [(T[bank][:, 16 * b + 16:256], Do, T[eq][:, b, 16:256 - 16 * b], False, False) for b in bs if b < 15]
-            if q == 3:
-                ms.append((T[bank][:, 0:256], Dg, T[eq][:, :, 0:16], False, True))
-            PM(ms, 200 - 40 * q, bank, ("%s.%d Do" % (eq, q)) + (" Zb s64" if not q else "") + (" Dg @.0 @.1 @.2".replace("@", eq) if q == 3 else ""))
-        V(lambda: TT(T.winr[:], T[bank][:, 0:256], T.Cr[:], A.is_lt), "winr", bank + " Cr", 256)
-        pick(T[bank][:, 256:272], "winr", bank)
+    def first(eq, bank, rows, rkey, key, kkey, flag, parts):
+        lo = lambda b: 64 * (b // 4)
+        part = lambda b: [k for k, (x, y) in enumerate(parts) if x <= b < y][0]
+        for b in R16:
+            V(lambda b=b: TS(T[eq][:, b, lo(b):256], rows(lo(b), 256), key(b), lfc(flag, b), A.is_equal, A.mult),
+              "%s.%d" % (eq, b), "%s %s %s.%d" % (rkey, kkey, flag, part(b)), 256 - lo(b), 0.5)
+        for h, bs in ((0, (0, 1, 2)), (0, (4, 5, 6, 7, 3)), (1, (0, 1, 2, 3)), (1, (4, 5, 6, 7)), (1, (8, 9, 10)), (1, (12, 13, 14, 15, 11))):
+            ms = []
+            for b in bs:
+                x = max(lo(b), 128 * h)
+                w = T.Wt[:, :, 7 - b % 8:15 - b % 8] if b // 8 == h else T.Wt[:, :, 8:16]
+                ms.append((T[bank][x - 128 * h:128, 384 + 64 * h:448 + 64 * h], T[eq][:, b, x:128 * h + 128], w, b == 0, b == 8 * h + 3))
+            PM(ms, 64, "%s.n %s.g" % (bank, bank), "Wt " + " ".join("%s.%d" % (eq, b) for b in bs))
+        V(lambda: TT(T.Xm[:], T[bank][:, 384:512], T.thr[:], A.is_lt), "Xm", bank + ".n thr", 128)
+        PM([(T[bank][:, 256:272], T.Vs[:, 112 - 16 * k:240 - 16 * k], T.Xm[:, :, k, :], k == 0, k == 7) for k in range(8)], 16,
+           "%s.w %s.g" % (bank, bank), "Vs Xm")
 
     def send(key, src, dst, t):
         rid, pid, _ = topo.addr(nxt)
@@ -241,228 +242,297 @@ def program(T, g, me, nxt, topo):
                 "", src, 0.3, "%sl%d" % (key, t), n)
         add("n", [], dst, "", TRN, "%sr%d" % (key, t), n, i)
 
-    ZE = " ".join("ze.%d" % k for k in R16)
-    WB = T.b5[:, 256:272]
+    ALL = [(0, 16)]
     for t in range(NV):
+        now[0] = t
         zi, fi, zo_, fo = "zin%d" % t, "fin%d" % t, "zout%d" % t, "fout%d" % t
         zin, fin, zout, fout = T[zi], T[fi], T[zo_], T[fo]
-        PM([(T.b3[:, 0:16], T.Sw[:, j, :], zin[:, j:256:16], j == 0, j == 15) for j in R16], 16, "b3", "Sw " + zi)
-        V(lambda: TC(xr, T.b3[:, 0:16]), "xr", "b3", 16)
+        PM([(T.b3[:, 0:16], row("Ww", j), zin[:, j:256:16], j == 0, j == 15) for j in R16], 16, "b3.u", "Ww " + zi)
+        V(lambda: TC(xr, T.b3[:, 0:16]), "xr", "b3.u", 16)
         V(lambda: TS(ui, xr, 4095, None, A.bitwise_and), "ui", "xr", 16)
+        V(lambda: TS(T.CI[:, 0:16], xr, 15, None, A.bitwise_and), "mi", "xr", 16)
         V(lambda: TS(u32, ui, 32.0, None, A.add), "u32", "ui", 16)
-        V(lambda t=t: TS(u2, ui, 2048.0, 2464.0 * t, A.mult, A.add), "u2", "ui", 16)
-        V(lambda: TS(u2, u2, 32767, None, A.bitwise_and), "u2", "u2", 16)
+        V(lambda t=t: TS(u2, T.CI[:, 0:16], 2048.0, 2464.0 * t, A.mult, A.add), "u2", "mi", 16)
+        z0 = min(x for x, n, m in CM + EM if m != "c")
         for k in R16:
-            zk = T.ze[:, k:4096:16]
-            if ZM[k] == "a":
-                S_(lambda zk=zk, zin=zin: ACT(zk, zin[:], F.Copy), "ze.%d" % k, zi, 256)
-            elif ZM[k] == "g":
-                G(lambda zk=zk, zin=zin: sel(zk, zin[:], [[0, 256]], A.is_gt, 1, 0), "ze.%d" % k, zi, 256)
+            out, in_, n = T.ze[:, 16 * z0 + k:4096:16], zin[:, z0:256], 256 - z0
+            eng = (ZE if t else ZE0)[k]
+            if eng == "g":
+                G(lambda out=out, in_=in_, n=n: sel(out, in_, [[0, n]], A.is_gt, 1, 0), "ze.%d" % k, zi, n)
+            elif eng == "a":
+                S_(lambda out=out, in_=in_: ACT(out, in_, F.Copy), "ze.%d" % k, zi, n)
             else:
-                V(lambda zk=zk, zin=zin: TC(zk, zin[:]), "ze.%d" % k, zi, 256, 0.5)
-        S_(lambda zin=zin: ACT(T.zh[:], zin[:], F.Copy, bias=-0.5), "zh", zi, 256)
-        S_(lambda zin=zin: ACT(T.R[:, 4352:4608], zin[:], F.Copy), "Rz", zi, 256)
+                V(lambda out=out, in_=in_: TC(out, in_), "ze.%d" % k, zi, n, 0.5)
+        G(lambda zin=zin: sel(T.R[:, 4096:4352], zin[:], [[0, 256]], A.is_gt, 1, 0), "Rd", zi, 256)
         V(lambda fin=fin: TT(xq, u32, fin[:], A.mult), "xq", "u32 " + fi, 16)
         V(lambda: TT(xq, xq, u2, A.add), "xq", "xq u2", 16)
         V(lambda: TS(T.CI[:, 16:32], xq, 5, 1023, A.arith_shift_right, A.bitwise_and), "ci", "xq", 16)
         V(lambda: TC(cu, T.CI[:, 16:32]), "cu", "ci", 16)
-        V(lambda: TC(T.su[:], T.C[:, 0:1024].indirect(cu)), "su", "C cu", 256, 1.5)
-        S_(lambda: ACT(T.sF[:], T.C[:, 0:1024].indirect(cu), F.Copy), "sF", "C cu", 256, 1.5)
+        V(lambda: TC(T.su[:], T.C[:, 0:1024].indirect(cu)), "su", "C cu", 256, GA)
+        S_(lambda: ACT(T.sF[:], T.C[:, 0:1024].indirect(cu), F.Copy), "sF", "C cu", 256, GA)
         V(lambda: TT(ye, T.CI[:, 16:32], u32, A.mult), "ye", "ci u32", 16)
         V(lambda: TS(ye, ye, 32.0, None, A.add), "ye", "ye", 16)
         V(lambda: TS(T.CI[:, 32:48], ye, 5, 1023, A.arith_shift_right, A.bitwise_and), "ei", "ye", 16)
         V(lambda: TC(eu, T.CI[:, 32:48]), "eu", "ei", 16)
-        V(lambda: TC(T.su2[:], T.C[:, 0:1024].indirect(eu)), "su2", "C eu", 256, 1.5)
-        V(lambda: TS(T.CI[:, 0:16], ui, 15, None, A.bitwise_and), "mi", "ui", 16)
-        V(lambda: TC(T.L3[:], T.CI[:]), "L3", "ci mi ei", 48)
-        V(lambda: TC(cf, T.CI[:, 16:32]), "cf", "ci", 16)
-        V(lambda: TS(nek, T.CI[:, 32:48], -1.0, None, A.mult), "nek", "ei", 16)
+        V(lambda: TC(T.su2[:], T.C[:, 0:1024].indirect(eu)), "su2", "C eu", 256, GA)
+        V(lambda: TC(T.L3[:], T.CI[:, 16:48]), "L3", "ci ei", 32)
+        V(lambda: TC(T.kf[:], T.CI[:, 16:48]), "kf", "ci ei", 32)
         V(lambda: TT(T.RM[:], T.CI[:], T.K3[:], A.subtract), "RM", "ci mi ei K3", 48)
-        PM([(T.b0[:, 256:512], T.Ih[:], T.r16h[:], True, False)] +
-           [(T.b0[:, 256 + j:512:16], T.Sp[:, j, :], T.L3[:, 0:16], False, j == 15) for j in R16], 30, "b0", "Ih r16h Sp L3")
-        spread("b4", 0, "L3", 16, 48)
-        V(lambda: TC(T.crow[:], T.b4[:, 0:256]), "crow", "b4", 256)
-        S_(lambda: ACT(T.erF[:], T.b4[:, 256:512], F.Copy), "erF", "b4", 256)
-        for r in range(2):
-            V(lambda r=r: TS(T.s16[:, :, r, :], T.su[:, 128 * r:128 * r + 128], -2048.0, None, A.add), "s16", "su", 128, 0.5)
-        V(lambda: v.transpose(T.t16[:], T.s16[:]), "t16", "s16", 256, 0.5)
-        PM([(T.b0[:, 0:256], W1, T.ckb[:], True, False)], 256, "b0", "W1 ckb")
-        PM([(T.b0[:, 128 * r:128 * r + 128], T.W4[:, 2 * r + h, :], T.t16[:, :, 16 * h:16 * h + 16], False, False)
-            for r in range(2) for h in range(2)], 128, "b0", "W4 t16")
+        V(lambda: TT(T.mneg[:], iL, T.CI[:, 0:16], A.subtract), "mneg", "iL mi", 16)
+        V(lambda: TS(T.uh[:], ui, -2048.0, None, A.add), "uh", "ui", 16)
+        spread("b4", 0, "L3", 32, "b4.0 b4.1")
+        evac(T.rows[:], T.b4[:], "rows", "b4.0 b4.1", 512)
+        if OWN != "p":
+            spread("b4", 0, "mneg", 16, "b4.0")
+            evac(T.nrow[:], T.b4[:, 0:256], "nrow", "b4.0", 256)
+        PM([(T.b3[:, 64:80], I5, fin[:], True, False), (T.b3[:, 64:80], Ib, T.uh[:], False, True)], 16, "b3.f", "I5 Ib uh " + fi)
+        def turn(dst, k0, key, stop, off=0, out="b0.k"):
+            PM([(T.b0[:, off + 128 * r:off + 128 * r + 128], T.W4[:, k0 + 2 * r + h, :], T[dst][:, :, 16 * h:16 * h + 16], False, stop and r + h == 2)
+                for r in range(2) for h in range(2)], 128, out + " b0.g", key + " " + dst)
+        V(lambda: TS(T.s16[:], T.su[:], -2048.0, None, A.add), "s16", "su", 256, 0.5)
+        V(lambda: v.transpose(T.ts[:], T.s16[:]), "ts", "s16", 256, 0.5)
+        PM([(T.b0[:, 0:256], Ib, T.ck[:, 0:256], True, False)], 256, "b0.k b0.g", "Ib ck")
+        turn("ts", 0, "W4", False)
 
-        def records(eng, su, buf, out, lo, hi, key, okey):
-            n = hi - lo
-            win = T.R[:, 0:4096].indirect(T[su][:, lo // 16:hi // 16])
-            xo = T[out][:, lo // 256:hi // 256, :]
-            if eng == "v":
-                V(lambda: TT(T[buf][:, lo:hi], win, T.ze[:, lo:hi], A.subtract), key, "R " + su + " " + ZE, n, 1.5)
-                S_(lambda: ACT(xo, T[buf][:, lo:hi], F.Abs), okey, key, n)
+        def records(part, su, xg, xa, k, bank):
+            l0, nl, mode = part
+            lo, hi = 16 * l0, 16 * (l0 + nl)
+            gk, ak, out = "%s.%d" % (xg, k), "%s.%d" % (xa, k), T[bank][:, l0:l0 + nl]
+            if mode == "c":
+                S_(lambda: ACT(T[xg][:, lo:hi], T.R[:, 0:4096].indirect(T[su][:, l0:l0 + nl]), F.Copy), gk, "R " + su, hi - lo, GA)
+                for y in range(2):
+                    bk = "b%d" % (6 + y)
+                    ms = []
+                    for j in range(8):
+                        o = T[bk][:, nl * j:nl * j + nl]
+                        ms += [(o, Ib, T[xg][:, lo + 8 * y + j:hi:16], True, False), (o, In, zin[:, l0:l0 + nl], False, True)]
+                    PM(ms, nl, bk + ".x", "Ib In %s %s" % (gk, zi))
+                    S_(lambda bk=bk, y=y: ACT(T[xa][:, lo + 8 * nl * y:lo + 8 * nl * (y + 1)], T[bk][:, 0:8 * nl], F.Abs), "%s.%d" % (ak, y), bk + ".x", 8 * nl)
+                PM([(out, row("Wb", j), T[xa][:, lo + nl * j:lo + nl * j + nl], j == 0, j == 15) for j in R16], nl, "%s.%d" % (bank, k), "Wb %s.0 %s.1" % (ak, ak))
                 return
-            bk = "b%d" % (6 + lo // 512 % 2)
-            S_(lambda: ACT(T[buf][:, lo:hi], win, F.Copy), key, "R " + su, n, 1.5)
-            PM([(T[bk][:], Ib, T[buf][:, lo:hi], True, False), (T[bk][:], In, T.ze[:, lo:hi], False, True)], 512, bk, "Ib In " + key + " " + ZE)
-            S_(lambda: ACT(xo, T[bk][:], F.Abs), okey, bk, n)
+            zk = " ".join("ze.%d" % z for z in R16)
+            ys = range(l0, l0 + nl, VP)
+            for y in ys:
+                ye_ = min(y + VP, l0 + nl)
+                x, xa_ = T[xg][:, 16 * y:16 * ye_], T[xa][:, 16 * y:16 * ye_]
+                V(lambda x=x, y=y, ye_=ye_: TT(x, T.R[:, 0:4096].indirect(T[su][:, y:ye_]), T.ze[:, 16 * y:16 * ye_], A.subtract),
+                  "%s.%d" % (gk, y), "R %s %s" % (su, zk), 16 * (ye_ - y), GA)
+                if mode == "a":
+                    S_(lambda x=x, xa_=xa_: ACT(xa_, x, F.Abs), "%s.%d" % (ak, y), "%s.%d" % (gk, y), 16 * (ye_ - y))
+                else:
+                    V(lambda x=x, xa_=xa_: TS(xa_, x, 0.0, None, A.max), "%s.%d" % (ak, y), "%s.%d" % (gk, y), 16 * (ye_ - y), 0.5)
+            ks = lambda key: " ".join("%s.%d" % (key, y) for y in ys)
+            if mode == "b":
+                PM([(out, row("Wn", j), T[xg][:, lo + j:hi:16], j == 0, False) for j in R16], nl, "%s.%d %s.g" % (bank, k, bank), "Wn " + ks(gk))
+            PM([(out, row("Wb" if mode == "a" else "W2", j), T[xa][:, lo + j:hi:16], j == 0 and mode == "a", j == 15) for j in R16], nl,
+               "%s.%d %s.g" % (bank, k, bank), "Wb W2 " + ks(ak))
 
-        for k, (b0, nb) in enumerate(CH):
-            lo, hi = 256 * b0, 256 * (b0 + nb)
-            xl = []
-            for y in range(lo, hi, hi - lo if CM[k] == "v" else 512):
-                xl.append("xa.%d" % y)
-                records(CM[k], "su", "x2", "xa", y, hi if CM[k] == "v" else y + 512, "x2.%d" % y, xl[-1])
-            xl = " ".join(xl)
-            PM([(T.b0[:, 16 * b0:16 * (b0 + nb)], T.Sk[:, j, :], T.xa[:, b0:b0 + nb, 16 * j:16 * j + 16], False, k == len(CH) - 1 and j == 15)
-                for j in R16], 16 * nb, "b0", "Sk " + xl)
-            PM([(T.b1[:, 16 * b0:16 * (b0 + nb)], T.Sb[:, j, :], T.xa[:, b0:b0 + nb, j:256:16], j == 0, j == 15)
-                for j in R16], 16 * nb, "b1", "Sb " + xl)
-        for k in range(8):
-            records(EM[k], "su2", "ve", "xe", 512 * k, 512 * k + 512, "ve.%d" % k, "xe.%d" % k)
-            if k % 2:
-                b0 = 2 * k - 2
-                PM([(T.b2[:, 16 * b0:16 * b0 + 64], T.Sb[:, j, :], T.xe[:, b0:b0 + 4, j:256:16], j == 0, j == 15)
-                    for j in R16], 64, "b2", "Sb xe.%d xe.%d" % (k - 1, k))
+        for k, part in enumerate(CM):
+            records(part, "su", "xg", "xa", k, "b5" if part[2] == "b" else "b1")
         if t == 0:
-            V(lambda: TC(T.hc[:, 0:1], T.thf[:, 0:1]), "h", "thf", 1)
+            V(lambda: TS(T.hc[:], T.hB[:], T.thf[:, 0:1], None, A.add), "h", "hB thf", 4)
         else:
-            V(lambda: TC(T.ai[:], T.b3[:, 128:129]), "ai", "b3", 1)
-            V(lambda: TS(T.ai[:], T.ai[:], 31, None, A.bitwise_and), "ai", "ai", 1)
-            V(lambda t=t: TT(T.hc[:, 0:1], T.ai[:], T.thf[:, t:t + 1], A.add), "h", "ai thf", 1)
-        V(lambda: TS(T.hm[:], T.hA[:], T.hc[:, 0:1], None, A.mult), "hm", "h hA", 4)
-        V(lambda: TT(T.hc[:, 1:5], T.hm[:], T.hB[:], A.add), "hs", "hm hB", 4)
-        V(lambda: v.tensor_tensor_scan(T.sm[:], T.d0n[:], T.b0[:, 0:256], 0.0, A.add, A.min), "sm", "d0n b0", 256)
-        V(lambda: TS(T.sa_[:], T.b1[:, 0:256], T.hc[:, 0:1], 4.0, A.min, A.mult), "sa_", "b1 h", 256)
-        V(lambda: TS(T.sb_[:], T.b1[:, 0:256], T.hc[:, 0:1], 512.0, A.max, A.min), "sb_", "b1 h", 256)
-        V(lambda: TS(T.sq_[:], T.b1[:, 0:256], 512.0, T.hc[:, 3:4], A.is_ge, A.mult), "sq_", "b1 hs", 256)
-        for k, n in enumerate(("sa_", "sb_", "sq_")):
-            PM([(T.b3[:, 16:32], T.Sh[:, j, :], T[n][:, j:256:16], k == 0 and j == 0, k == 2 and j == 15) for j in R16], 16, "b3", "Sh " + n)
-        V(lambda: TS(ps, T.b3[:, 16:32], T.hc[:, 4:5], None, A.is_le), "ps", "b3 hs", 16)
-        sml = T.sm[:, 15:256:16]
-        V(lambda: TS(has, sml, T.hc[:, 1:2], None, A.is_lt), "has", "sm hs", 16)
-        V(lambda: TC(kI, sml), "kI", "sm", 16)
-        V(lambda: TS(ny, kI, 4095, None, A.bitwise_and), "ny", "kI", 16)
-        V(lambda: TT(t3, ny, zt, A.subtract), "t3", "ny zt", 16)
-        V(lambda: TT(t4, t3, has, A.mult), "t4", "t3 has", 16)
-        V(lambda: TT(t5, t4, zt, A.add), "t5", "t4 zt", 16)
-        V(lambda: TC(zo, t5), "zo", "t5", 16)
-        V(lambda: TT(T.xs[:], T.R[:].indirect(zo), T.zh[:], A.add), "xs", "R Rz zh zo", 256, 1.5)
-        V(lambda: TS(T.x4[:], T.xs[:], 16777216.0, 16777216.0, A.add, A.subtract), "x4", "xs", 256, 0.5)
-        V(lambda zout=zout: TS(zout[:], T.x4[:], 0.5, None, A.mult), zo_, "x4", 256, 0.5)
-        send("z", zo_, "zin%d" % (t + 1), t)
-        V(lambda: TC(nyu, ny), "nyu", "ny", 16)
-        V(lambda: TS(T.pg[:], T.PT[:, 0:4096].indirect(nyu), -2048.0, None, A.add), "pg", "PT nyu", 256, 1.5)
-        pick(T.b4[:, 256:272], "pg", "b4")
+            V(lambda: TS(T.ai[:], T.b3[:, 128:129], 0.03125, -0.484375, A.mult, A.add), "ai", "b3.a", 1)
+            V(lambda: TS(am, T.ai[:], -32.0, T.b3[:, 128:129], A.mult, A.add), "am", "ai b3.a", 1)
+            V(lambda t=t: TS(T.hc[:], T.hB[:], am, T.thf[:, t:t + 1], A.add, A.add), "h", "hB am thf", 4)
+        dn, dd = T.T2[:, 0, :], T.T2[:, 1, :]
+        for bk in ("b1", "b5"):
+            ks = [k for k, part in enumerate(CM) if (part[2] == "b") == (bk == "b5")]
+            if ks:
+                x, y = CM[ks[0]][0], CM[ks[-1]][0] + CM[ks[-1]][1]
+                V(lambda bk=bk, x=x, y=y: TS(T.T2[:, 0, x:y], T[bk][:, x:y], -256.0, 256.0, A.add, A.min), "dn" + bk, " ".join("%s.%d" % (bk, k) for k in ks), y - x)
+        DN = "dnb1 dnb5"
+        V(lambda: v.transpose(T.td[:], dn), "td", DN, 256, 0.5)
+        turn("td", 4, "W4d", True)
+        V(lambda: TS(dd, dn, 256.0, -1.0, A.is_ge, A.mult), "dd", DN, 256, 0.5)
+        V(lambda: TS(T.T2[:, 2, :], dn, T.hc[:, 2:3], 3.0, A.min, A.mult), "mn", DN + " h", 256, 0.5)
+        PM([(T.b3[:, 144:192], row("Wb", j), T.T2[:, :, j:256:16], j == 0, False) for j in range(15)] + [(T.b3[:, 144:160], Ib, T.k16[:, 0:16], False, False)] +
+           [(T.b3[:, 144:192], row("Wb", 15), T.T2[:, :, 15:256:16], False, True)], 16, "b3.s", "Wb Ib k16 dd mn " + DN)
+        V(lambda: TS(tq, T.b3[:, 160:176], 64.0, T.hc[:, 1:2], A.add, A.mult), "tq", "b3.s h", 16)
+        V(lambda: TT(tq, tq, T.b3[:, 144:160], A.subtract), "tq", "b3.s tq", 16)
+        V(lambda: TT(ps, tq, T.b3[:, 176:192], A.is_ge), "ps.0", "b3.s tq", 16)
+        V(lambda: v.tensor_tensor_scan(T.sm[:], T.d0n[:], T.b0[:, 0:256], 0.0, A.add, A.min), "sm", "d0n b0.k", 256)
+        add("v", [(lambda r=r: TC(T.li[:, LI.index("kI"), r:16:2], T.sm[:, 128 * r + 15:128 * r + 128:16])) for r in range(2)], "kI", "sm", 2 * dv(8))
         V(lambda: TS(w1, kI, 16, None, A.arith_shift_right), "w1", "kI", 16)
-        V(lambda: TS(w5, w1, 5.0, 5376.0, A.mult, A.add), "w5", "w1", 16)
-        V(lambda fin=fin: TT(w6, w5, fin[:], A.add), "w6", "w5 " + fi, 16)
-        V(lambda fin=fin: TS(f0a, fin[:], 5.0, 10240.0, A.mult, A.add), "f0a", fi, 16)
-        V(lambda: TT(f0, f0a, ui, A.add), "f0", "f0a ui", 16)
-        V(lambda: TT(w6, w6, f0, A.subtract), "w6", "w6 f0", 16)
-        V(lambda: TT(dif, T.b4[:, 256:272], w6, A.add), "dif", "b4 w6", 16)
-        V(lambda: TT(ph, ps, has, A.mult), "ph", "ps has", 16)
-        V(lambda: TT(pdh, ph, dif, A.mult), "pdh", "ph dif", 16)
-        dedupe("EQ", "b5", "v", T.crow, "crow", "cf", "ps")
-        V(lambda: TT(rr, WB, pdh, A.mult), "rr", "b5 pdh", 16)
-        V(lambda: TT(fr, rr, f0, A.add), "fr", "rr f0", 16)
+        V(lambda: TS(ny, kI, 4095, None, A.bitwise_and), "ny", "kI", 16)
+        V(lambda: TS(nh, w1, T.hc[:, 2:3], 8192.0, A.is_ge, A.mult), "nh", "w1 h", 16)
+        V(lambda: TT(t3, ny, nh, A.add), "t3", "ny nh", 16)
+        V(lambda: TT(t4, t3, tr, A.min), "t4", "t3 tr", 16)
+        V(lambda: TC(zo, t4), "zo", "t4", 16)
+        V(lambda zin=zin: TT(T.xs[:], T.R[:].indirect(zo), zin[:], A.add), "xs", "R Rd zo " + zi, 256, GA)
+        V(lambda: TS(T.x4[:], T.xs[:], 0.5, 191.75, A.mult, A.add), "x4", "xs", 256, 0.5)
+        V(lambda zout=zout: TS(zout[:], T.x4[:], -192.0, None, A.add), zo_, "x4", 256, 0.5)
+        send("z", zo_, "zin%d" % (t + 1), t)
+        if EVAC == "a":
+            S_(lambda: ACT(T.pg[:], T.PT[:].indirect(zo), F.Copy, bias=-2048.0), "pg", "PT PT1 zo", 256, GA)
+        else:
+            V(lambda: TS(T.pg[:], T.PT[:].indirect(zo), -2048.0, None, A.add), "pg", "PT PT1 zo", 256, GA)
+        V(lambda: TS(T.w5h[:], w1, 5.0, None, A.mult), "w5h", "w1", 16)
+        PM([(T.b3[:, 48:64], x, y, n == 0, False) for n, (x, y) in enumerate(((Ib, T.k16[:, 16:32]), (I4n, fin[:]), (In, T.uh[:]), (Ib, T.w5h[:])))] +
+           [(T.b3[:, 48:64], row("Wb", j), T.pg[:, j:256:16], False, j == 15) for j in R16], 16, "b3.d", "Wb Ib In I4n k16 uh w5h pg " + fi)
+        V(lambda: TT(ph, ps, nh, A.is_gt), "ph", "ps.0 nh", 16)
+        V(lambda: TT(pdh, ph, T.b3[:, 48:64], A.mult), "pdh", "ph b3.d", 16)
+        WB = T.b5[:, 256:272]
+        first("EQ", "b5", lambda x, y: T.rows[:, x:y], "rows", lambda b: T.kf[:, b:b + 1], "kf", "ps", ALL)
+        V(lambda: TT(rr, WB, pdh, A.mult), "rr", "b5.w pdh", 16)
+        V(lambda: TT(fr, rr, T.b3[:, 64:80], A.add), "fr", "rr b3.f", 16)
         V(lambda: TS(fr2, fr, 4095, None, A.bitwise_and), "fr2", "fr", 16)
         V(lambda fout=fout: TS(fout[:], fr2, -2048.0, None, A.add), fo, "fr2", 16)
         send("f", fo, "fin%d" % (t + 1), t)
-        V(lambda: TT(T.acc[:, 0:16], WB, ps, A.mult), "acc", "b5 ps", 16)
-        V(lambda: TT(T.acc[:, 16:32], WB, ps, A.mult), "acc2", "b5 ps", 16)
+        V(lambda: TT(acc, WB, ps, A.mult), "acc", "b5.w ps.0", 16)
         if t < NV - 1:
-            S_(lambda: ACT(T.accb[:], T.acc[:, 0:16], F.Copy, accum_out=af), "accb af", "acc", 16)
-            PM([(T.b3[:, 128:129], one, af, True, True)], 256, "b3", "one af")
-        S_(lambda: ACT(T.mM[:], T.b0[:, 0:256], F.Relu, bias=-64.0 * 16777216.0, scale=64.0), "mM", "b0", 256)
-        V(lambda: TT(T.kr[:], T.b0[:, 0:256], T.mM[:], A.subtract), "kr", "b0 mM", 256)
-        V(lambda: v.tensor_tensor_scan(T.sx[:], T.d0x[:], T.kr[:], 0.0, A.add, A.max), "sx", "d0x kr", 256)
-        sxl = T.sx[:, 15:256:16]
-        V(lambda: TC(fI, sxl), "fI", "sx", 16)
-        V(lambda: TS(foe, sxl, T.hc[:, 2:3], None, A.is_ge), "foe", "sx hs", 16)
+            S_(lambda: ACT(T.accb[:], acc, F.Copy, accum_out=af), "accb af", "acc", 16)
+            PM([(T.b3[:, 128:129], one, af, True, True)], 256, "b3.a", "one af")
+        for k, part in enumerate(EM):
+            records(part, "su2", "eg", "ea", k, "b2")
+        if KMAX == "p":
+            V(lambda: v.transpose(T.tx[:], dd), "tx", "dd", 256, 0.5)
+            PM([(T.b0[:, 256:512], Ib, T.ck[:, 256:512], True, False)], 256, "b0.x b0.w b0.n b0.g", "Ib ck")
+            for dst, k0, key in (("ts", 0, "W4"), ("td", 4, "W4d"), ("tx", 8, "W4x")):
+                turn(dst, k0, key, k0 == 8, 256, "b0.x")
+            V(lambda: v.tensor_tensor_scan(T.sx[:], T.d0x[:], T.b0[:, 256:512], 0.0, A.add, A.max), "sx", "d0x b0.x b0.w b0.n", 256)
+        else:
+            S_(lambda: ACT(T.mM[:], T.b0[:, 0:256], F.Relu, bias=-64.0 * 16000000.0, scale=64.0), "mM", "b0.k", 256)
+            V(lambda: TT(T.kr[:], T.b0[:, 0:256], T.mM[:], A.subtract), "kr", "b0.k mM", 256)
+            V(lambda: v.tensor_tensor_scan(T.sx[:], T.d0x[:], T.kr[:], 0.0, A.add, A.max), "sx", "d0x kr", 256)
+        add("v", [(lambda r=r: TC(T.li[:, LI.index("fI"), r:16:2], T.sx[:, 128 * r + 15:128 * r + 128:16])) for r in range(2)], "fI", "sx", 2 * dv(8))
+        V(lambda: TS(foe, fI, 2.0 ** -16, T.hc[:, 3:4], A.mult, A.is_ge), "foe", "fI h", 16)
         V(lambda: TS(vs, fI, 4095, None, A.bitwise_and), "vs", "fI", 16)
         V(lambda: TS(vk, vs, -2048.0, None, A.add), "vk", "vs", 16)
         V(lambda: TS(T.v16[:], vs, -2048.0, None, A.add), "v16", "vs", 16)
         V(lambda: TT(vrm, vs, tr, A.subtract), "vrm", "vs tr", 16)
-        spread("b4", 0, "v16", 0, 16)
-        V(lambda: TC(T.vrow[:], T.b4[:, 0:256]), "vrow", "b4", 256)
-        V(lambda: TT(flg, foe, T.acc[:, 0:16], A.mult), "flg", "foe acc", 16)
-        dedupe("EQv", "b5", "v", T.vrow, "vrow", "vk", "flg")
-        V(lambda: TT(unq, WB, flg, A.mult), "unq", "b5 flg", 16)
-        V(lambda: TT(dl, unq, vrm, A.mult), "dl", "unq vrm", 16)
+        spread("b4", 0, "v16", 16, "b4.0")
+        evac(T.vrow[:], T.b4[:, 0:256], "vrow", "b4.0", 256)
+        V(lambda: TT(flg, foe, acc, A.mult), "flg.0", "foe acc", 16)
+        V(lambda: TT(fv, flg, vrm, A.mult), "fv", "flg.0 vrm", 16)
+        first("EQv", "b5", lambda x, y: T.vrow[:, x:y], "vrow", lambda b: lfc("vk", b), "vk", "flg", ALL)
+        V(lambda: TT(dl, WB, fv, A.mult), "dl", "b5.w fv", 16)
         V(lambda: TT(dl, dl, tr, A.add), "dl", "dl tr", 16)
         V(lambda: TC(dlu, dl), "dlu", "dl", 16)
-        V(lambda: TC(T.R[:, 0:4352].indirect(dlu), T.s64[:]), "R", "dlu s64", 256, 3.5)
-        V(lambda: TT(T.la[:], T.acc[:], T.RM[:, 0:32], A.mult), "la", "acc acc2 RM", 32)
-        V(lambda: TT(T.la[:], T.la[:], T.T2c[:], A.add), "la", "la T2c", 32)
-        V(lambda: TC(T.lau[:], T.la[:]), "lau", "la", 32)
-        V(lambda zout=zout: TC(T.R[:, 0:4352].indirect(T.lau[:, 0:16]), zout[:]), "R", "lau " + zo_, 256, 3.5)
-        PM([(T.b4[:, 256 + j:512:16], T.Sp[:, j, :], fout[:], True, True) for j in R16], 16, "b4", "Sp " + fo)
-        S_(lambda: ACT(T.phr[:], T.b4[:, 256:512], F.Copy, bias=2048.0), "phr", "b4", 256)
-        V(lambda: TC(T.PT[:].indirect(T.lau[:, 0:16]), T.phr[:]), "PT", "lau phr", 256, 3.5)
-        S_(lambda: ACT(T.sg[:], T.b1[:, 0:256], F.Sign, bias=-511.5), "sg", "b1", 256)
-        PM([(T.b1[:, 256:512], Y1, T.sg[:], True, True)], 256, "b1", "Y1 sg")
-        S_(lambda: ACT(T.b1[:, 256:512], T.b1[:, 256:512], F.Relu, bias=bn), "b1", "bn", 256)
-        V(lambda: TT(T.nd[:], T.b0[:, 256:512], T.sF[:], A.subtract), "nd", "b0 sF", 256)
-        V(lambda: TT(T.nd[:], T.nd[:], T.b1[:, 256:512], A.mult), "nd", "nd b1", 256)
-        V(lambda: TT(T.C[:].indirect(T.lau[:, 16:32]), T.nd[:], T.sF[:], A.add), "C", "lau nd sF", 256, 3.5)
-        S_(lambda: ACT(T.sup[:], T.b2[:, 0:256], F.Relu, bias=T.hc[:, 0:1], scale=-1.0), "sup", "b2 h", 256)
-        S_(lambda: ACT(T.sg2[:], T.b2[:, 0:256], F.Sign, bias=-511.5), "sg2", "b2", 256)
-        PM([(T.b2[:, 256:512], Y2, T.sg2[:], True, True)], 256, "b2", "Y2 sg2")
-        S_(lambda: ACT(T.b2[:, 256:512], T.b2[:, 256:512], F.Relu, bias=bx), "b2", "bx", 256)
-        PM([(T.b7[:, 0:16], T.Sb[:, j, :], T.sup[:, j:256:16], j == 0, j == 15) for j in R16], 16, "b7", "Sb sup")
-        V(lambda: TS(cn0, T.b7[:, 0:16], 0.0, None, A.is_equal), "cn0", "b7", 16)
-        V(lambda: TT(cnd, cn0, T.acc[:, 0:16], A.mult), "cnd", "cn0 acc", 16)
-        dedupe("EQe", "b6", "a", T.erF, "erF", "nek", "cnd")
-        V(lambda: TT(w2, T.b6[:, 256:272], cnd, A.mult), "w2", "b6 cnd", 16)
-        V(lambda: TT(l2, w2, T.RM[:, 32:48], A.mult), "l2", "w2 RM", 16)
+        V(lambda: TC(T.R[:].indirect(dlu), T.s64[:]), "R Rd", "dlu s64", 256, SC)
+        V(lambda: TT(T.la[:, 0:16], acc, T.RM[:, 0:16], A.mult), "la0", "acc RM", 16)
+        V(lambda: TT(T.la[:, 16:32], acc, T.RM[:, 16:32], A.mult), "la1", "acc RM", 16)
+        V(lambda: TT(T.la[:], T.la[:], T.T2c[:], A.add), "la0 la1", "la0 la1 T2c", 32)
+        V(lambda: TC(T.lau[:], T.la[:]), "lau", "la0 la1", 32)
+        V(lambda zout=zout: TC(T.R[:].indirect(T.lau[:, 0:16]), zout[:]), "R Rd", "lau " + zo_, 256, SC)
+        spread("b4", 256, fo, 16, "b4.1")
+        S_(lambda: ACT(T.phr[:], T.b4[:, 256:512], F.Identity, bias=k2, scale=lfc("I16", 0)), "phr", "b4.1 k2", 256)
+        V(lambda: TC(T.PT[:].indirect(T.lau[:, 0:16]), T.phr[:]), "PT PT1", "lau phr", 256, SC)
+        Q = T.b1[:, 256:512]
+        if OWN == "p":
+            own, ok = [(T.b1[:, 256 + j:512:16], T.Sp[:, j, :], T.mneg[:], False, False) for j in R16], "Sp mneg"
+        else:
+            own, ok = [(Q, Ib, T.nrow[:], False, False)], "Ib nrow"
+        PM([(Q, I6, T.on[:], True, False)] + own + [(Q, Y1, dd, False, True)], 85 if OWN == "p" else 256, "b1.q b1.g", "I6 on Y1 dd " + ok)
+        S_(lambda: ACT(T.n1[:], Q, F.Copy, bias=-8192.0, scale=-1.0), "n1", "b1.q", 256)
+        V(lambda: TT(T.a1[:], Q, T.sF[:], A.min), "a1", "b1.q sF", 256)
+        V(lambda: TT(T.C[:].indirect(T.lau[:, 16:32]), T.a1[:], T.n1[:], A.max), "C", "lau a1 n1", 256, SC)
+        for k, (x, y) in enumerate(EP):
+            dk = " ".join("b2.%d" % z for z, (l0, nl, m) in enumerate(EM) if l0 < 16 * y and 16 * x < l0 + nl)
+            S_(lambda x=x, y=y: ACT(T.sup[:, 16 * x:16 * y], T.b2[:, 16 * x:16 * y], F.Relu, bias=T.hc[:, 0:1], scale=-1.0), "sup.%d" % k, dk + " h", 16 * (y - x))
+            PM([(T.b3[:, 80 + x:80 + y], row("Wb", j), T.sup[:, 16 * x + j:16 * y:16], j == 0, j == 15) for j in R16], 16, "b3.c%d" % k, "Wb sup.%d" % k)
+            V(lambda x=x, y=y: TT(lfc("cnd", x, y), lfc("acc", x, y), T.b3[:, 80 + x:80 + y], A.is_gt), "cnd.%d" % k, "acc b3.c%d" % k, 16)
+        S_(lambda: ACT(T.sg2[:], T.b2[:, 0:256], F.Sign, bias=-511.5), "sg2", " ".join("b2.%d" % z for z in range(len(EM))), 256)
+        PM([(Q, Y2c, T.on[:], True, False)] + own, 75 if OWN == "p" else 256, "b1.q b1.g", "Y2c on " + ok)
+        PM([(Q, Y2, T.sg2[:], False, True)], 256, "b1.q b1.g", "Y2 sg2")
+        S_(lambda: ACT(T.n2[:], Q, F.Copy, bias=-8192.0, scale=-1.0), "n2", "b1.q", 256)
+        S_(lambda: ACT(T.sF2[:], T.C[:, 0:1024].indirect(eu), F.Copy), "sF2", "C eu", 256, GA)
+        V(lambda: TT(T.a2[:], Q, T.sF2[:], A.min), "a2", "b1.q sF2", 256)
+        V(lambda: TT(cr, cnd, T.RM[:, 32:48], A.mult), "cr", "RM " + " ".join("cnd.%d" % k for k in range(len(EP))), 16)
+        first("EQe", "b0", lambda x, y: T.rows[:, 256 + x:256 + y], "rows", lambda b: T.kf[:, 16 + b:17 + b], "kf", "cnd", EP)
+        V(lambda: TT(l2, T.b0[:, 256:272], cr, A.mult), "l2", "b0.w cr", 16)
         V(lambda: TT(l2, l2, tc, A.add), "l2", "l2 tc", 16)
         V(lambda: TC(l2u, l2), "l2u", "l2", 16)
-        S_(lambda: ACT(T.sF2[:], T.C[:, 0:1024].indirect(eu), F.Copy), "sF2", "C eu", 256, 1.5)
-        V(lambda: TT(T.nd2[:], T.b0[:, 256:512], T.sF2[:], A.subtract), "nd2", "b0 sF2", 256)
-        V(lambda: TT(T.nd2[:], T.nd2[:], T.b2[:, 256:512], A.mult), "nd2", "nd2 b2", 256)
-        V(lambda: TT(T.C[:].indirect(l2u), T.nd2[:], T.sF2[:], A.add), "C", "l2u nd2 sF2", 256, 3.5)
-    D("yrec", T.yrec[:], T.R[:, 0:4096], "", "R", 6.0)
-    D("ycel", T.ycel[:], T.C[:, 0:1024], "", "C", 4.0, "a")
-    D("ypo", T.ypo[:], T.PT[0:128:16, 0:4096], "", "PT", 3.0)
+        V(lambda: TT(T.C[:].indirect(l2u), T.a2[:], T.n2[:], A.max), "C", "l2u a2 n2", 256, SC)
+    now[0] = -2
+    D("yrec", T.yrec[:], T.R[:, 0:4096], "", "R", 7.0)
+    D("ycel", T.ycel[:], T.C[:, 0:1024], "", "C", 4.5, "a")
+    D("ypo", T.ypo[:], T.PT[0:128:16, 0:4096], "", "PT PT1", 3.0)
     zl, fl = "zin%d" % NV, "fin%d" % NV
     D("ypat", T.ypat[:], T[zl][:], "", zl, 2.0)
-    spread("b4", 0, fl, 0, 16)
-    V(lambda: TS(T.phr[:], T.b4[:, 0:256], 2048.0, None, A.add), "phr", "b4", 256)
+    spread("b4", 0, fl, 16, "b4.0")
+    S_(lambda: ACT(T.phr[:], T.b4[:, 0:256], F.Copy, bias=2048.0), "phr", "b4.0", 256)
     D("yphi", T.yphi[:], T.phr[0:128:16, :], "", "phr", 2.0)
     return ops
 
 
 def schedule(ops):
     n = len(ops)
-    succ = [[] for _ in ops]
-    need = [0] * n
-    for o in ops:
-        deps = o["wait"] | o["ord"] | ({o["net"]} if o["net"] is not None else set())
-        need[o["i"]] = len(deps)
-        for x in sorted(deps):
-            succ[x].append(o["i"])
-    pri = [0.0] * n
-    for i in range(n - 1, -1, -1):
-        pri[i] = ops[i]["d"] + max([pri[k] + 0.1 for k in succ[i]] or [0.0])
-    free = {q: 0.0 for q in "vapgs"}
-    ready = {q: [] for q in "vapgsn"}
-    at = [0.0] * n
-    for i in range(n):
-        if need[i] == 0:
-            ready[ops[i]["q"]].append(i)
-    order = []
-    while len(order) < n:
-        st, q = min((max(free.get(q, 0.0), min(at[i] for i in L)), q) for q, L in ready.items() if L)
-        i = max((i for i in ready[q] if at[i] <= st + 1e-9), key=lambda i: pri[i])
-        ready[q].remove(i)
-        o = ops[i]
-        if q != "n":
-            free[q] = st + (o["d"] if o["sem"] is None else 0.1)
-        end = st + o["d"]
-        order.append(i)
-        for k in succ[i]:
-            need[k] -= 1
-            same = ops[k]["q"] == q
-            at[k] = max(at[k], st if same and i not in ops[k]["wait"] else end + (0.03 if same else 0.1))
-            if need[k] == 0:
-                ready[ops[k]["q"]].append(k)
+    occ = [0.0 if o["q"] == "n" else 0.1 if o["sem"] and o["sem"][0] == "d" else o["d"] for o in ops]
+    fwd, bwd = [[] for _ in ops], [[] for _ in ops]
+    for k, o in enumerate(ops):
+        for x in o["wait"] | o["ord"] | ({o["net"]} if o["net"] is not None else set()):
+            lag = ops[x]["d"] + WAKE if x in o["wait"] else occ[x]
+            fwd[k].append((x, lag))
+            bwd[x].append((k, lag + occ[k] - occ[x]))
+
+    def place(rank, before, after, first):
+        at, need = [0.0] * n, [len(x) for x in before]
+        lines = {}
+        ready = [i for i in range(n) if not need[i]]
+        while ready:
+            i = min(ready, key=lambda i: rank[i])
+            ready.remove(i)
+            o = ops[i]
+            t = max([first[i]] + [at[x] + lag for x, lag in before[i]])
+            held = [(o["q"], 0.0)] * (o["q"] != "n") + [(b, WAKE) for b in o["bank"]]
+            moved = True
+            while moved:
+                moved = False
+                for key, gap in held:
+                    line = lines.setdefault(key, [])
+                    k = len(line)
+                    while k and line[k - 1][1] + gap > t + 1e-9:
+                        k -= 1
+                    for s, e, q in line[k:]:
+                        if s >= t + occ[i] + gap - 1e-9:
+                            break
+                        if gap == 0.0 or q != o["q"]:
+                            t, moved = e + gap, len(held) > 1
+            for key, gap in held:
+                line = lines[key]
+                k = len(line)
+                while k and line[k - 1][0] > t:
+                    k -= 1
+                line.insert(k, (t, t + occ[i], o["q"]))
+            at[i] = t
+            for k, lag in after[i]:
+                need[k] -= 1
+                if not need[k]:
+                    ready.append(k)
+        return at
+
+    if not ORDER:
+        rank, best, seed = list(range(n)), None, 1
+        same = {o["tag"]: o["i"] for o in ops}
+        for _ in range(ROUNDS):
+            at = place(rank, fwd, bwd, [0.0] * n)
+            end = max(at[i] + ops[i]["d"] for i in range(n))
+            if best is None or end <= best[0]:
+                best = (end, at)
+            end, at = best
+            rank = []
+            seed = seed * 16807 % 2147483647
+            if _ % 8 == 7:
+                m = seed % NV
+                t0 = [at[same["su", t]] for t in range(NV)]
+                rank = [t0[o["tag"][1]] + at[same[o["tag"][0], m]] - t0[m] if (o["tag"][0], m) in same and o["tag"][1] >= 0 else at[o["i"]] for o in ops]
+                continue
+            lo, amp = (seed % 1000) * 1e-3 * end - SPAN / 2, (seed // 1000 % 1000) * 1e-3 * JIT
+            for i in range(n):
+                seed = seed * 16807 % 2147483647
+                rank.append(-(at[i] + occ[i]) + (amp * seed / 2147483647 if lo <= at[i] < lo + SPAN else 0.0))
+            back = place(rank, bwd, fwd, [ops[i]["d"] - occ[i] for i in range(n)])
+            rank = [-(back[i] + occ[i]) for i in range(n)]
+        ORDER.append(sorted(range(n), key=lambda i: (best[1][i], i)))
+        ORDER.append(best[0])
+    order = ORDER[0]
+    held = {}
+    for i in order:
+        for b in ops[i]["bank"]:
+            if b in held and ops[held[b]]["q"] != ops[i]["q"]:
+                ops[i]["wait"].add(held[b])
+            held[b] = i
     return order
 
 

@@ -1,41 +1,50 @@
+import numpy as np
+from concourse.bass import DstId, RemoteDMATransfer
 from concourse.mybir import AluOpType as A, AxisListType, ActivationFunctionType as F
 
 NV = 4
 CM = [(0, 64, "c"), (64, 64, "c"), (128, 64, "b"), (192, 64, "b")]
-EM = [(0, 64, "c"), (64, 64, "c"), (128, 64, "c"), (192, 64, "c")]
-VP = 32
+EM = [(0, 64, "c"), (64, 64, "c"), (128, 64, "c"), (192, 64, "a")]
+VP = 64
 EP = [(0, 12), (12, 16)]
-ZE0, ZE = "va" * 8, "ga" * 8
+ZE0, ZE = "va" * 4, "ga" * 4
 EVAC = "a"
 PTG = 2816
-TRN = 4.5
-KMAX, OWN = "v", "a"
-ROUNDS, SPAN, JIT = 1500, 12.0, 4.0
+TRF = 5.0
+TRN = 4.2
+KMAX, SPLIT, SU = "v", False, 8
+LATE = ("EQe",)
+ONA = "xr u32 u2 uh h".split()
+ROUNDS, HEAT, SEED = 12000, 0.5, 1
 ORDER = []
-CY, PE, WAKE = 0.9e-3, 0.45e-3, 0.25
+CY, PE, WAKE = 0.95e-3, 0.49e-3, 0.25
 GA, SC = 1.56, 3.8
 BIG = 16384.0
+PRE = True
+ZO = 192.0
+OFF = 64.0
 
 B, H, F4, I4, U2 = "bfloat16", "float16", "float32", "int32", "uint16"
 SHAPES = {
-    B: "R:4352 xg:4096 xa:4096 eg:4096 ea:4096 sup:256 mM:256 sg2:256 xs:256 x4:256 ck:512 s64:256 on:256 accb:16 k16:32 "
-       "Wb:144 W2:144 Wn:144 W3:144 Ww:144 Vs:240",
-    H: "rows:512 vrow:256 s16:256 nrow:256 pg:256 phh:256 thh:4 L3:32 v16:16 mneg:16 uh:16 w5h:16",
+    B: "R:4352 xg:4096 xa:4096 eg:4096 ea:4096 sup:256 mM:256 sg2:256 xs:256 zof:256 ck:256 s64:256 on:512 accb:16 k16:32 "
+       "Wb:144 W2:144 Wn:144 W3:144 Ww:144 Vs:240 VsB:240",
+    H: "sp:32 rows:512 vrow:512 s16:256 pg:256 phh:256 thh:4 L3:32 L2:32 uh:16 w5h:16",
     F4: "C:1280 PT:4352 posf:256 sF:256 sF2:256 a1:256 a2:256 n1:256 n2:256 phr:256 thf:4 hc:4 hB:4 kr:256 Iw:160 thr:128 "
         "B8a:8 B8:8 g16:8 g16b:8 K3:48 rc:2 d0n:256 d0x:256 RM:48 kf:32 T2c:32 la:32 col:16",
     I4: "Ci:1024 pos:256 phl:256 thl:4 wl:1 ai:1 CI:48",
     U2: "su:256 su2:256 lau:32",
 }
 LF = "u32 nh t3 t4 tq ps ph pdh rr acc dl l2 foe flg vk fv cnd cr vrm jr I16 b256 i16 iL tr tc pw pwb hf".split()
-LI = "ui u2 xq xr ye kI ny w1 fI vs fr fr2".split()
+LI = "ui u2 xq xr ye kI ny w1 fI vs fr fr2 yf".split()
 LU = "cu eu zo dlu l2u".split()
-MB = "Ib In I5 I4n I6 Y1 Y2 Y2c".split()
+MB = "Ib In I5 I4n I6 Y1 Y2 Y2c Zb".split()
 MF = "one Bba Bta Bt Utf Ulf".split()
 SCRATCH = {}
 for _d, _l in SHAPES.items():
     for _x in _l.split():
         SCRATCH[_x.split(":")[0]] = ("sbuf", [128, int(_x.split(":")[1])], _d)
-for _x, _s, _d in (("EQ", [16, 256], B), ("EQe", [16, 256], B), ("EQv", [16, 256], B), ("ze", [4096], B), ("Sp", [16, 128], B),
+for _x, _s, _d in (("EQ", [16, 256], B), ("EQe", [16, 256], B), ("EQv", [16, 256], B), ("ze", [4096], B),
+                   ("WEQ", [16, 8, 16], B), ("WEQe", [16, 8, 16], B), ("WEQv", [16, 8, 16], B), ("Sp", [16, 128], B), ("hT", [NV, 4], F4),
                    ("Bf", [8, 16], F4), ("Wt", [8, 16], B), ("Xm", [2, 8, 8], B), ("W4", [12, 128], B), ("T2", [3, 256], H),
                    ("ts", [8, 32], H), ("td", [8, 32], H), ("tx", [8, 32], H), ("sm", [256], F4), ("sx", [256], F4),
                    ("lf", [len(LF), 16], F4), ("li", [len(LI), 16], I4), ("lu", [len(LU), 16], U2), ("mb", [len(MB), 128], B),
@@ -49,8 +58,14 @@ for _t in range(NV):
     SCRATCH["fout%d" % _t] = ("sbuf", [128, 16], H)
 for _b in range(8):
     SCRATCH["b%d" % _b] = ("psum", [128, 512], F4)
-DMAS = ["rec", "cel", "wt", "pat", "phi", "th", "po", "pt", "yrec", "ycel", "ypo", "ypat", "yphi"]
+DMAS = ["rec", "cel", "wt", "pat", "phi", "th", "po", "pt", "pb", "yrec", "ycel", "ypo", "ypat", "yphi"]
 SEMAPHORES = ["qv", "qa", "qp", "qg"] + ["d" + n for n in DMAS] + ["%s%d" % (k, t) for k in ("zr", "zl", "fr", "fl") for t in range(NV)]
+SEMAPHORES += ["%s%d%d" % (x, t, k) for x in ("ho", "hl", "hb", "hk") for t in range(NV) for k in range(4)]
+LAND = ["xg", "xa", "eg", "ea"]
+
+
+def helper(core, T, topo):
+    return [c for c in topo.cores_of(core) if T.rank_of(c) is None and topo.die(c) == topo.die(core)][0]
 
 
 def dv(n, rate=1.0):
@@ -59,14 +74,14 @@ def dv(n, rate=1.0):
 
 def program(T, g, me, nxt, topo):
     v, a, p, s = g.vector, g.scalar, g.tensor, g.sync
-    ops = []
+    ops, aid = [], helper(me, T, topo)
     last, tags, now = {}, set(), [-1]
 
     def add(q, fns, w, r, d, sem=None, val=0, net=None):
         rs, ws = r.split(), w.split()
         o = {"q": q, "f": fns, "d": d, "sem": sem, "val": val, "i": len(ops), "wait": set(), "ord": set(), "net": net,
              "bank": sorted(set(k[:2] for k in rs + ws if k[0] == "b" and k[2:3] == "."))}
-        name = "".join(c for c in w if c != str(now[0]) and c != str(now[0] + 1)) if "in" in w or "out" in w else w or "send " + r[0]
+        name = "".join(c for c in w if c != str(now[0]) and c != str(now[0] + 1)) if "in" in w or "out" in w else w or "send " + r[:1]
         while (name, now[0]) in tags:
             name += "+"
         o["tag"] = (name, now[0])
@@ -77,7 +92,7 @@ def program(T, g, me, nxt, topo):
                 o["wait"].add(L[0])
             if key in ws:
                 for x in ([L[0]] if L[0] is not None else []) + L[1]:
-                    o["ord" if ops[x]["q"] == q and ops[x]["sem"] is None and (x != L[0] or q == "p") else "wait"].add(x)
+                    o["ord" if ops[x]["q"] == q == "p" else "wait"].add(x)
                 last[key] = [o["i"], []]
             else:
                 L[1].append(o["i"])
@@ -90,6 +105,13 @@ def program(T, g, me, nxt, topo):
 
     def S_(fn, w, r, n, rate=1.0):
         return add("a", [fn], w, r, dv(n, rate))
+
+    def AF(out, in_, w, r, n, scale=1.0, bias=0.0, rate=1.0):
+        if w.split(".")[0].rstrip("0123") in ONA or w in ONA:
+            return S_(lambda: ACT(out, in_, F.Copy, bias=bias, scale=scale), w, r, n, max(rate, 1.0))
+        if scale == 1.0:
+            return V((lambda: TS(out, in_, bias, None, A.add)) if bias else (lambda: TC(out, in_)), w, r, n, rate)
+        return V(lambda: TS(out, in_, scale, bias, A.mult, A.add), w, r, n, rate)
 
     def G(fn, w, r, n):
         return add("g", [fn], w, r, 0.17 + 2 * n * CY)
@@ -105,11 +127,11 @@ def program(T, g, me, nxt, topo):
     R16 = range(16)
     (u32, nh, t3, t4, tq, ps, ph, pdh, rr, acc, dl, l2, foe, flg, vk, fv, cnd, cr, vrm, jr, I16, b256, i16, iL, tr, tc, pw, pwb,
      hf) = [T.lf[:, k, :] for k in range(len(LF))]
-    ui, u2, xq, xr, ye, kI, ny, w1, fI, vs, fr, fr2 = [T.li[:, k, :] for k in range(len(LI))]
+    ui, u2, xq, xr, ye, kI, ny, w1, fI, vs, fr, fr2, yf = [T.li[:, k, :] for k in range(len(LI))]
     cu, eu, zo, dlu, l2u = [T.lu[:, k, :] for k in range(len(LU))]
-    Ib, In, I5, I4n, I6, Y1, Y2, Y2c = [T.mb[:, k, :] for k in range(len(MB))]
+    Ib, In, I5, I4n, I6, Y1, Y2, Y2c, Zb = [T.mb[:, k, :] for k in range(len(MB))]
     one, Bba, Bta, Bt, Utf, Ulf = [T.mf[:, k, :] for k in range(len(MF))]
-    pc, gs, jc, j16, p2, p3, wf, af, am, k2 = [T.col[:, k:k + 1] for k in range(10)]
+    pc, gs, jc, j16, p2, p3, wf, af, am, k2, a0, k3, ws = [T.col[:, k:k + 1] for k in range(13)]
     lfc = lambda name, lo, hi=None: T.lf[:, LF.index(name), lo:hi or lo + 1]
     row = lambda name, j: T[name][:, 15 - j:143 - j]
     idf = T.Iw[:, 16:144]
@@ -122,15 +144,18 @@ def program(T, g, me, nxt, topo):
     def spread(bank, off, src, n, key):
         PM([(T[bank][:, off + j:off + 16 * n:16], T.Sp[:, j, :], T[src][:, 0:n], True, True) for j in R16], n, key, "Sp " + src)
 
-    V(lambda: MS(T.phl[:], 0), "phl", "", 256)
+    V(lambda: MS(T.phl[:], 2048), "phl", "", 256)
     V(lambda: MS(T.thl[:], 0), "thl", "", 4)
     D("rec", T.R[:, 0:4096], T.rec[:], "R", "", 7.0, "a")
-    D("pat", T.zin0[:], T.pat[:], "zin0", "", 2.0)
+    D("pat", T.xs[:], T.pat[:], "xs", "", 2.0)
+    V(lambda: TS(T.zin0[:], T.xs[:], ZO, None, A.add), "zin0", "xs", 256, 0.5)
+    V(lambda: MS(T.zof[:], -ZO), "zof", "", 256, 0.5)
+    V(lambda: MS(Zb, 0.0), "Zb", "", 128, 0.5)
     D("wt", T.wl[:], T.wt[:], "wl", "", 2.0)
     D("phi", T.phl[0:128:16, :], T.phi[:], "phl", "", 2.0)
     D("cel", T.Ci[:], T.cel[:], "Ci", "", 4.0)
     D("th", T.thl[0:128:16, :], T.th[:], "thl", "", 2.0)
-    D("po", T.pos[:], T.po[:], "pos", "", 2.5)
+    D("po", T.pos[:], T.po[:], "pos", "R", 2.5)
     iota = lambda out, pat, base=0, cm=0: g.iota(out, pat, base, cm, allow_small_or_imprecise_dtypes=True)
     sel = lambda out, in_, pat, op, base, cm: g.affine_select(out, in_, pat, op, 0.0, base, cm)
     V(lambda: MS(one, 1.0), "one", "", 128)
@@ -148,46 +173,41 @@ def program(T, g, me, nxt, topo):
     G(lambda: sel(Bt, Bta, [[0, 16], [16, 8]], A.is_ge, 15, -1), "Bt", "Bta", 128)
     G(lambda: sel(Utf, T.Bf[:], [[1, 128]], A.is_gt, 0, -1), "Utf", "Bf", 128)
     G(lambda: sel(Ulf, T.Bf[:], [[-1, 128]], A.is_gt, 0, 1), "Ulf", "Bf", 128)
-    G(lambda: iota(T.ck[:, 0:256], [[0, 16], [4096, 16]], 2048), "ck0", "", 256)
-    V(lambda: TS(T.ck[:, 256:512], T.ck[:, 0:256], -1.0, 65536.0, A.mult, A.add), "ck", "ck0", 256, 0.5)
-    G(lambda: iota(T.PT[:, 0:PTG], [[0, PTG]]), "PT", "B8 Iw Bf Bt Utf Ulf ck0 jr pc g16 b256", PTG)
+    G(lambda: iota(T.ck[:, 0:256], [[0, 16], [4096, 16]], 2048), "ck", "", 256)
+    G(lambda: iota(T.PT[:, 0:PTG], [[0, PTG]]), "PT", "B8 Iw Bf Bt Utf Ulf ck jr pc g16 b256", PTG)
     V(lambda: MS(T.PT[:, PTG:4352], 0.0), "PT1", "", 4352 - PTG)
     V(lambda: MS(T.Wb[:], 0.0), "Wb", "", 144, 0.5)
     V(lambda: TC(T.Wb[:, 15:128:16], T.B8[:]), "Wb", "B8", 8)
     V(lambda: TC(wf, T.wl[:]), "wf", "wl", 1)
-    for name, x in (("Ww", wf), ("W2", 2.0), ("Wn", -1.0), ("W3", 3.0)):
+    for name, x in (("Ww", wf), ("W2", 2.0), ("Wn", -1.0)):
         V(lambda name=name, x=x: TS(T[name][:], T.Wb[:], x, None, A.mult), name, "Wb wf" if name == "Ww" else "Wb", 144, 0.5)
-    V(lambda: TC(T.C[:, 0:1024], T.Ci[:]), "C", "Ci", 1024)
     V(lambda: MS(T.C[:, 1024:1280], 0.0), "C", "", 256)
+    AF(T.C[:, 0:1024], T.Ci[:], "C", "Ci", 1024)
     V(lambda: TT(T.g16b[:], T.g16[:], T.B8[:], A.mult), "g16b", "g16 B8", 8)
     V(lambda: RED(gs, T.g16b[:]), "gs", "g16b", 8)
     V(lambda: TT(jc, pc, gs, A.subtract), "jc", "pc gs", 1)
     V(lambda: TS(I16, jr, jc, None, A.is_equal), "I16", "jr jc", 16)
-    V(lambda: TS(k2, lfc("I16", 0), 2048.0, None, A.mult), "k2", "I16", 1)
+    V(lambda: TS(k2, lfc("I16", 0), 2048.0 + OFF, None, A.mult), "k2", "I16", 1)
+    V(lambda: TS(k3, lfc("I16", 0), -2048.0 - OFF, None, A.mult), "k2", "I16", 1)
     V(lambda: TS(j16, jc, 16.0, None, A.mult), "j16", "jc", 1)
     V(lambda: TS(i16, b256, j16, None, A.add), "i16", "b256 j16", 16)
     V(lambda: TS(tr, i16, 0.0625, 4096.0, A.mult, A.add), "tr", "i16", 16)
     V(lambda: TS(tc, i16, 0.0625, 1024.0, A.mult, A.add), "tc", "i16", 16)
     V(lambda: TS(iL, i16, -1.0, 2048.0, A.mult, A.add), "iL", "i16", 16)
-    V(lambda: TT(T.K3[:, 0:16], tr, i16, A.subtract), "K3", "i16 tr", 16)
-    V(lambda: TC(T.K3[:, 16:32], tc), "K3", "tc", 16)
-    V(lambda: TC(T.K3[:, 32:48], tc), "K3", "tc", 16)
-    V(lambda: TC(T.T2c[:, 0:16], tr), "T2c", "tr", 16)
-    V(lambda: TC(T.T2c[:, 16:32], tc), "T2c", "tc", 16)
-    for k, y in enumerate((0.0, -512.0, -256.0, -256.0 if KMAX == "p" else -255.0625)):
-        V(lambda k=k, y=y: MS(T.hB[:, k:k + 1], y), "hB", "", 1)
+    add("v", [lambda: TT(T.K3[:, 0:16], tr, i16, A.subtract), lambda: TC(T.K3[:, 16:32], tc), lambda: TC(T.K3[:, 32:48], tc),
+              lambda: TC(T.T2c[:, 0:16], tr), lambda: TC(T.T2c[:, 16:32], tc)], "K3 T2c", "i16 tr tc", 5 * dv(16))
+    add("v", [(lambda k=k, y=y: MS(T.hB[:, k:k + 1], y)) for k, y in enumerate((0.0, -512.0, -256.0, -255.0625))], "hB", "", 4 * dv(1))
     add("a", [(lambda j=j: ACT(T.Sp[:, j, :], T.Bf[:], F.Copy, scale=lfc("I16", j))) for j in R16], "Sp", "Bf I16", 16 * dv(128))
     V(lambda: RED(T.rc[:, 0:1], T.B8[:, 0:8:2]), "rc", "B8", 4)
     V(lambda: RED(T.rc[:, 1:2], T.B8[:, 1:8:2]), "rc", "B8", 4)
-    for k, (x, r) in enumerate(((16, 0), (0, 0), (32, 1), (16, 1))):
-        V(lambda k=k, x=x, r=r: TS(T.W4[:, k, :], T.Iw[:, x:x + 128], T.rc[:, r:r + 1], None, A.mult), "W4", "Iw rc", 128)
+    add("a", [(lambda k=k, x=x, r=r: ACT(T.W4[:, k, :], T.Iw[:, x:x + 128], F.Copy, scale=T.rc[:, r:r + 1]))
+              for k, (x, r) in enumerate(((16, 0), (0, 0), (32, 1), (16, 1)))], "W4", "Iw rc", 4 * dv(128))
     V(lambda: TS(T.W4[:, 4:8, :], T.W4[:, 0:4, :], 65536.0, None, A.mult), "W4d", "W4", 512, 0.5)
-    V(lambda: TS(T.W4[:, 8:12, :], T.W4[:, 0:4, :], 67108864.0, None, A.mult), "W4x", "W4", 512, 0.5)
     for m, name, x in ((Ib, "Ib", 1.0), (In, "In", -1.0), (I5, "I5", 5.0), (I4n, "I4n", -4.0), (I6, "I6", 6144.0)):
         S_(lambda m=m, x=x: ACT(m, idf, F.Copy, scale=x), name, "Iw", 128)
     V(lambda: MS(T.d0n[:], 0.0), "d0n", "", 256)
     V(lambda: MS(T.d0n[:, 0:256:16], 134217728.0), "d0n", "", 16)
-    V(lambda: MS(T.d0x[:], 0.0 if KMAX == "p" else 8192.0), "d0x", "", 256)
+    V(lambda: MS(T.d0x[:], 8192.0), "d0x", "", 256)
     V(lambda: MS(T.d0x[:, 0:256:16], -268435456.0), "d0x", "", 16)
     V(lambda: MS(hf, 0.5), "hf", "", 16)
     V(lambda: v.tensor_tensor_scan(pw, hf, hf, 65536.0, A.mult, A.max), "pw", "hf", 16)
@@ -200,10 +220,14 @@ def program(T, g, me, nxt, topo):
     V(lambda: TS(T.Wt[:, :, 8:16], T.Bf[:, :, 0:8], 65536.0, None, A.mult), "Wt", "Bf", 64)
     V(lambda: MS(T.Vs[:], 0.0), "Vs", "", 240, 0.5)
     V(lambda: TC(T.Vs[:, 112:128], I16), "Vs", "I16", 16)
+    V(lambda: TS(T.VsB[:], T.Vs[:], -8192.0, None, A.mult), "VsB", "Vs", 240, 0.5)
+    V(lambda: TS(T.sp[:, 0:16], tr, -2304.0, None, A.add), "sp", "tr", 16)
+    V(lambda: TC(T.sp[:, 16:32], tc), "sp", "tc", 16)
     V(lambda: MS(T.s64[:], 64.0), "s64", "", 256, 0.5)
-    V(lambda: MS(T.on[:], 1.0), "on", "", 256, 0.5)
-    V(lambda: MS(T.k16[:, 0:16], -16384.0), "k16", "", 16)
-    V(lambda: MS(T.k16[:, 16:32], 3328.0), "k16", "", 16)
+    V(lambda: MS(T.on[:], 1.0), "on", "", 512, 0.5)
+    PM([(T.b3[:, 136:137], row("Ww", j), T.zof[:, 0:1], j == 0, j == 15) for j in R16], 1, "b3.ws", "Ww zof")
+    V(lambda: TC(ws, T.b3[:, 136:137]), "ws", "b3.ws", 1)
+    add("v", [lambda: MS(T.k16[:, 0:16], -16384.0), lambda: MS(T.k16[:, 16:32], 1280.0)], "k16", "", 2 * dv(16))
     V(lambda: TT(Utf, idf, Utf, A.subtract), "Utf", "Iw Utf", 128, 2)
     V(lambda: TT(Ulf, idf, Ulf, A.subtract), "Ulf", "Iw Ulf", 128, 2)
     for m, name, src, key, x in ((Y1, "Y1", Utf, "Utf", BIG), (Y2, "Y2", Ulf, "Ulf", -BIG / 2)):
@@ -212,35 +236,51 @@ def program(T, g, me, nxt, topo):
     V(lambda: TC(T.thh[:], T.thl[:]), "thh", "thl", 4)
     PM([(T.b3[:, 132:136], T.Sp[:, 0, :], T.thh[:], True, True)], 4, "b3.th", "Sp thh")
     V(lambda: TC(T.thf[:], T.b3[:, 132:136]), "thf", "b3.th", 4)
-    V(lambda: TS(T.phh[:], T.phl[:], -2048.0, lfc("I16", 0), A.add, A.mult), "phh", "phl I16", 256)
-    PM([(T.b5[:, 256:272], row("Wb", j), T.phh[:, j:256:16], j == 0, j == 15) for j in R16], 16, "b5.w", "Wb phh")
-    V(lambda: TC(T.fin0[:], T.b5[:, 256:272]), "fin0", "b5.w", 16)
-    V(lambda: TC(T.posf[:], T.pos[:]), "posf", "pos", 256)
+    add("a", [(lambda t=t: ACT(T.hT[:, t, :], T.hB[:], F.Identity, bias=T.thf[:, t:t + 1])) for t in range(1, NV)], "hT", "hB thf", 3 * dv(4))
+    V(lambda: TS(T.phh[:], T.phl[:], -2048.0, None, A.add), "phh", "phl", 256)
+    PM([(T.b5[:, 256:272], row("Wb", j), T.phh[:, j:256:16], j == 0, j == 15) for j in R16], 16, "b5.w0", "Wb phh")
+    V(lambda: TC(T.fin0[:], T.b5[:, 256:272]), "fin0", "b5.w0", 16)
+    V(lambda: TS(T.posf[:], T.pos[:], OFF, None, A.add), "posf", "pos", 256)
     D("pt", T.PT[0:128:16, 0:4096], T.posf[:], "PT PT1", "posf", 2.5)
 
-    def first(eq, bank, rows, rkey, key, kkey, flag, parts):
+    def first(eq, bank, rows, rkey, key, kkey, flag, parts, spare=None, split=False):
         lo = lambda b: 64 * (b // 4)
         part = lambda b: [k for k, (x, y) in enumerate(parts) if x <= b < y][0]
-        for b in R16:
-            V(lambda b=b: TS(T[eq][:, b, lo(b):256], rows(lo(b), 256), key(b), lfc(flag, b), A.is_equal, A.mult),
-              "%s.%d" % (eq, b), "%s %s %s.%d" % (rkey, kkey, flag, part(b)), 256 - lo(b), 0.5)
+        late = eq in LATE
+        for bs in ((0, 1), (2, 3), (4, 5), (6, 7), (8, 9, 10, 11), (12, 13, 14, 15)):
+            fk, ks, d = "%s.%d" % (flag, part(bs[0])), lambda k: " ".join("%s.%d" % (k, b) for b in bs), len(bs) * dv(256 - lo(bs[0]), 0.5)
+            if late:
+                add("v", [(lambda b=b: TS(T[eq][:, b, lo(b):256], rows(lo(b), 256), key(b), None, A.is_equal)) for b in bs], ks(eq), rkey + " " + kkey, d)
+                xy = [(b, 7 - b % 8, 16 if b < 8 else 15 - b % 8) for b in bs]
+                add("a", [(lambda b=b, x=x, y=y: ACT(T["W" + eq][:, b, :, x:y], T.Wt[:, :, x:y], F.Copy, scale=lfc(flag, b))) for b, x, y in xy],
+                    ks("W" + eq), "Wt " + fk, sum(dv(8 * (y - x)) for b, x, y in xy))
+            else:
+                add("v", [(lambda b=b: TS(T[eq][:, b, lo(b):256], rows(lo(b), 256), key(b), lfc(flag, b), A.is_equal, A.mult)) for b in bs],
+                    ks(eq), "%s %s %s" % (rkey, kkey, fk), d)
         for h, bs in ((0, (0, 1, 2)), (0, (4, 5, 6, 7, 3)), (1, (0, 1, 2, 3)), (1, (4, 5, 6, 7)), (1, (8, 9, 10)), (1, (12, 13, 14, 15, 11))):
             ms = []
             for b in bs:
                 x = max(lo(b), 128 * h)
-                w = T.Wt[:, :, 7 - b % 8:15 - b % 8] if b // 8 == h else T.Wt[:, :, 8:16]
+                y = 7 - b % 8 if b // 8 == h else 8
+                w = T["W" + eq][:, b, :, y:y + 8] if late else T.Wt[:, :, y:y + 8]
                 ms.append((T[bank][x - 128 * h:128, 384 + 64 * h:448 + 64 * h], T[eq][:, b, x:128 * h + 128], w, b == 0, b == 8 * h + 3))
-            PM(ms, 64, "%s.n %s.g" % (bank, bank), "Wt " + " ".join("%s.%d" % (eq, b) for b in bs))
-        V(lambda: TT(T.Xm[:], T[bank][:, 384:512], T.thr[:], A.is_lt), "Xm", bank + ".n thr", 128)
-        PM([(T[bank][:, 256:272], T.Vs[:, 112 - 16 * k:240 - 16 * k], T.Xm[:, :, k, :], k == 0, k == 7) for k in range(8)], 16,
-           "%s.w %s.g" % (bank, bank), "Vs Xm")
+            PM(ms, 64, "%s.n%d %s.g" % (bank, h, bank), "Wt " + " ".join("%s.%d" % (eq, b) + " W%s.%d" % (eq, b) * late for b in bs))
+            if bs[-1] != 11 and not (split and bs[-1] == 3 and h == 0):
+                continue
+            h0 = h if split else 0
+            V(lambda h=h, h0=h0: TT(T.Xm[:, h0:h + 1, :, :], T[bank][:, 384 + 64 * h0:448 + 64 * h], T.thr[:, 64 * h0:64 * h + 64], A.is_lt),
+              "Xm.%d" % h0, "%s.n%d %s.n%d thr" % (bank, h0, bank, h), 64 * (h + 1 - h0))
+            o = T[bank][:, 256 + 8 * h0:264 + 8 * h]
+            PM(([] if spare is None else [(o, Ib, T.sp[:, spare + 8 * h0:spare + 8 * h + 8], True, False)]) +
+               [(o, T["Vs" if spare is None else "VsB"][:, 112 - 16 * k:240 - 16 * k], T.Xm[:, h0:h + 1, k, :], k == 0 and spare is None, k == 7)
+                for k in range(8)], 16, "%s.w%d %s.g" % (bank, h0, bank), "Ib sp Vs VsB Xm.%d" % h0)
 
     def send(key, src, dst, t):
         rid, pid, _ = topo.addr(nxt)
         m, n = topo.mask(me, nxt), len(topo.engines(me, nxt))
         i = add("g", [lambda: g.remote_dma(T[dst][:], T[src][:], T.sem["%sr%d" % (key, t)], T.sem["%sl%d" % (key, t)], pid, rid, m)],
                 "", src, 0.3, "%sl%d" % (key, t), n)
-        add("n", [], dst, "", TRN, "%sr%d" % (key, t), n, i)
+        add("n", [], dst, "", TRN - (key == "f"), "%sr%d" % (key, t), n, i)
 
     ALL = [(0, 16)]
     for t in range(NV):
@@ -248,48 +288,47 @@ def program(T, g, me, nxt, topo):
         zi, fi, zo_, fo = "zin%d" % t, "fin%d" % t, "zout%d" % t, "fout%d" % t
         zin, fin, zout, fout = T[zi], T[fi], T[zo_], T[fo]
         PM([(T.b3[:, 0:16], row("Ww", j), zin[:, j:256:16], j == 0, j == 15) for j in R16], 16, "b3.u", "Ww " + zi)
-        V(lambda: TC(xr, T.b3[:, 0:16]), "xr", "b3.u", 16)
+        if "xr" in ONA:
+            S_(lambda: ACT(xr, T.b3[:, 0:16], F.Identity, bias=ws), "xr", "b3.u ws", 16)
+        else:
+            V(lambda: TS(xr, T.b3[:, 0:16], ws, None, A.add), "xr", "b3.u ws", 16)
         V(lambda: TS(ui, xr, 4095, None, A.bitwise_and), "ui", "xr", 16)
         V(lambda: TS(T.CI[:, 0:16], xr, 15, None, A.bitwise_and), "mi", "xr", 16)
-        V(lambda: TS(u32, ui, 32.0, None, A.add), "u32", "ui", 16)
-        V(lambda t=t: TS(u2, T.CI[:, 0:16], 2048.0, 2464.0 * t, A.mult, A.add), "u2", "mi", 16)
+        AF(u32, ui, "u32", "ui", 16, bias=32.0)
+        AF(u2, T.CI[:, 0:16], "u2", "mi", 16, 2048.0, 2464.0 * t)
         z0 = min(x for x, n, m in CM + EM if m != "c")
-        for k in R16:
-            out, in_, n = T.ze[:, 16 * z0 + k:4096:16], zin[:, z0:256], 256 - z0
+        for k in range(8):
+            outs, in_, n = [T.ze[:, 16 * z0 + x:4096:16] for x in (2 * k, 2 * k + 1)], zin[:, z0:256], 256 - z0
             eng = (ZE if t else ZE0)[k]
-            if eng == "g":
-                G(lambda out=out, in_=in_, n=n: sel(out, in_, [[0, n]], A.is_gt, 1, 0), "ze.%d" % k, zi, n)
-            elif eng == "a":
-                S_(lambda out=out, in_=in_: ACT(out, in_, F.Copy), "ze.%d" % k, zi, n)
-            else:
-                V(lambda out=out, in_=in_: TC(out, in_), "ze.%d" % k, zi, n, 0.5)
-        G(lambda zin=zin: sel(T.R[:, 4096:4352], zin[:], [[0, 256]], A.is_gt, 1, 0), "Rd", zi, 256)
+            fn = {"g": lambda o, i, n=n: sel(o, i, [[0, n]], A.is_gt, 1, 0), "a": lambda o, i: ACT(o, i, F.Copy), "v": TC}[eng]
+            add(eng, [(lambda o=o, in_=in_, fn=fn: fn(o, in_)) for o in outs], "ze.%d" % k, zi,
+                2 * (0.17 + 2 * n * CY if eng == "g" else dv(n, 1.0 if eng == "a" else 0.5)))
+        S_(lambda zin=zin: ACT(T.R[:, 4096:4352], zin[:], F.Copy, bias=-ZO), "Rd", zi, 256)
         V(lambda fin=fin: TT(xq, u32, fin[:], A.mult), "xq", "u32 " + fi, 16)
         V(lambda: TT(xq, xq, u2, A.add), "xq", "xq u2", 16)
         V(lambda: TS(T.CI[:, 16:32], xq, 5, 1023, A.arith_shift_right, A.bitwise_and), "ci", "xq", 16)
-        V(lambda: TC(cu, T.CI[:, 16:32]), "cu", "ci", 16)
-        V(lambda: TC(T.su[:], T.C[:, 0:1024].indirect(cu)), "su", "C cu", 256, GA)
+        AF(cu, T.CI[:, 16:32], "cu", "ci", 16)
+        cells, ck_ = (T.C[:, 0:1024], "C") if t else (T.Ci[:], "Ci")
+        for w, x, y in (("sa", 0, SU), ("su", SU, 16)):
+            AF(T.su[:, 16 * x:16 * y], cells.indirect(T.lu[:, 0, x:y]), w, ck_ + " cu", 16 * (y - x), rate=GA)
         S_(lambda: ACT(T.sF[:], T.C[:, 0:1024].indirect(cu), F.Copy), "sF", "C cu", 256, GA)
         V(lambda: TT(ye, T.CI[:, 16:32], u32, A.mult), "ye", "ci u32", 16)
-        V(lambda: TS(ye, ye, 32.0, None, A.add), "ye", "ye", 16)
-        V(lambda: TS(T.CI[:, 32:48], ye, 5, 1023, A.arith_shift_right, A.bitwise_and), "ei", "ye", 16)
-        V(lambda: TC(eu, T.CI[:, 32:48]), "eu", "ei", 16)
-        V(lambda: TC(T.su2[:], T.C[:, 0:1024].indirect(eu)), "su2", "C eu", 256, GA)
-        V(lambda: TC(T.L3[:], T.CI[:, 16:48]), "L3", "ci ei", 32)
-        V(lambda: TC(T.kf[:], T.CI[:, 16:48]), "kf", "ci ei", 32)
+        AF(yf, ye, "yf", "ye", 16, bias=32.0)
+        V(lambda: TS(T.CI[:, 32:48], yf, 5, 1023, A.arith_shift_right, A.bitwise_and), "ei", "yf", 16)
+        AF(eu, T.CI[:, 32:48], "eu", "ei", 16)
+        AF(T.su2[:], T.C[:, 0:1024].indirect(eu), "su2", "C eu", 256, rate=GA)
+        AF(T.L3[:], T.CI[:, 16:48], "L3", "ci ei", 32)
+        AF(T.kf[:], T.CI[:, 16:48], "kf", "ci ei", 32)
         V(lambda: TT(T.RM[:], T.CI[:], T.K3[:], A.subtract), "RM", "ci mi ei K3", 48)
-        V(lambda: TT(T.mneg[:], iL, T.CI[:, 0:16], A.subtract), "mneg", "iL mi", 16)
-        V(lambda: TS(T.uh[:], ui, -2048.0, None, A.add), "uh", "ui", 16)
+        V(lambda: TT(T.L2[:, 16:32], iL, T.CI[:, 0:16], A.subtract), "mneg", "iL mi", 16)
+        AF(T.uh[:], ui, "uh", "ui", 16, bias=-2048.0)
         spread("b4", 0, "L3", 32, "b4.0 b4.1")
         evac(T.rows[:], T.b4[:], "rows", "b4.0 b4.1", 512)
-        if OWN != "p":
-            spread("b4", 0, "mneg", 16, "b4.0")
-            evac(T.nrow[:], T.b4[:, 0:256], "nrow", "b4.0", 256)
         PM([(T.b3[:, 64:80], I5, fin[:], True, False), (T.b3[:, 64:80], Ib, T.uh[:], False, True)], 16, "b3.f", "I5 Ib uh " + fi)
         def turn(dst, k0, key, stop, off=0, out="b0.k"):
             PM([(T.b0[:, off + 128 * r:off + 128 * r + 128], T.W4[:, k0 + 2 * r + h, :], T[dst][:, :, 16 * h:16 * h + 16], False, stop and r + h == 2)
                 for r in range(2) for h in range(2)], 128, out + " b0.g", key + " " + dst)
-        V(lambda: TS(T.s16[:], T.su[:], -2048.0, None, A.add), "s16", "su", 256, 0.5)
+        AF(T.s16[:], T.su[:], "s16", "sa su", 256, bias=-2048.0, rate=0.5)
         V(lambda: v.transpose(T.ts[:], T.s16[:]), "ts", "s16", 256, 0.5)
         PM([(T.b0[:, 0:256], Ib, T.ck[:, 0:256], True, False)], 256, "b0.k b0.g", "Ib ck")
         turn("ts", 0, "W4", False)
@@ -298,29 +337,48 @@ def program(T, g, me, nxt, topo):
             l0, nl, mode = part
             lo, hi = 16 * l0, 16 * (l0 + nl)
             gk, ak, out = "%s.%d" % (xg, k), "%s.%d" % (xa, k), T[bank][:, l0:l0 + nl]
+            sk = lambda x, y: su if su == "su2" else "sa " * (x < 16 * SU) + "su" * (y > 16 * SU)
             if mode == "c":
-                S_(lambda: ACT(T[xg][:, lo:hi], T.R[:, 0:4096].indirect(T[su][:, l0:l0 + nl]), F.Copy), gk, "R " + su, hi - lo, GA)
+                banks = (("b6", "b6.x"), ("b7", "b7.x"))
+                if su == "su" and k and PRE:
+                    banks = (("b2", "b2.0 b2.1 b2.2 b2.3 b2.g"), ("b4", "b4.0 b4.1"))
+                S_(lambda: ACT(T[xg][:, lo:hi], T.R[:, 0:4096].indirect(T[su][:, l0:l0 + nl]), F.Copy), gk, "R " + sk(l0, l0 + nl), hi - lo, GA)
                 for y in range(2):
-                    bk = "b%d" % (6 + y)
-                    ms = []
-                    for j in range(8):
-                        o = T[bk][:, nl * j:nl * j + nl]
-                        ms += [(o, Ib, T[xg][:, lo + 8 * y + j:hi:16], True, False), (o, In, zin[:, l0:l0 + nl], False, True)]
-                    PM(ms, nl, bk + ".x", "Ib In %s %s" % (gk, zi))
-                    S_(lambda bk=bk, y=y: ACT(T[xa][:, lo + 8 * nl * y:lo + 8 * nl * (y + 1)], T[bk][:, 0:8 * nl], F.Abs), "%s.%d" % (ak, y), bk + ".x", 8 * nl)
+                    bk, key = banks[y]
+                    os_ = [T[bk][:, nl * j:nl * j + nl] for j in range(8)]
+                    rs_ = [T[xg][:, lo + 8 * y + j:hi:16] for j in range(8)]
+                    if su == "su" and PRE:
+                        PM([(T[bk][:, 0:8 * nl], Zb, T.on[:, 0:8 * nl], True, False)] + [(o, In, zin[:, l0:l0 + nl], False, False) for o in os_],
+                           114, key, "Zb on In " + zi)
+                        PM([(o, Ib, r, False, j == 7) for j, (o, r) in enumerate(zip(os_, rs_))], nl, key, "Ib " + gk)
+                    else:
+                        PM([m for o, r in zip(os_, rs_) for m in ((o, Ib, r, True, False), (o, In, zin[:, l0:l0 + nl], False, True))], nl, key,
+                           "Ib In %s %s" % (gk, zi))
+                    S_(lambda bk=bk, y=y: ACT(T[xa][:, lo + 8 * nl * y:lo + 8 * nl * (y + 1)], T[bk][:, 0:8 * nl], F.Abs, bias=ZO), "%s.%d" % (ak, y), key, 8 * nl)
                 PM([(out, row("Wb", j), T[xa][:, lo + nl * j:lo + nl * j + nl], j == 0, j == 15) for j in R16], nl, "%s.%d" % (bank, k), "Wb %s.0 %s.1" % (ak, ak))
                 return
-            zk = " ".join("ze.%d" % z for z in R16)
+            zk = " ".join("ze.%d" % z for z in range(8))
+            if mode == "f":
+                rid, pid, _ = topo.addr(aid)
+                m, n = topo.mask(me, aid), len(topo.engines(me, aid))
+                S_(lambda: ACT(T[xg][:, lo:hi], T.R[:, 0:4096].indirect(T[su][:, l0:l0 + nl]), F.Copy), gk, "R " + sk(l0, l0 + nl), hi - lo, GA)
+                tr_ = RemoteDMATransfer(dst_ids=[DstId(rid=rid, pnc=pid)], dma_engine_mask=m, remote_sem=T.sem["ho%d%d" % (t, k)],
+                                        srcs=[T[xg][:, lo:hi], T.ze[:, lo:hi]], dsts=[T[LAND[t]][:, lo:hi]], alu_op=2)
+                i = add("g", [lambda ls=T.sem["hl%d%d" % (t, k)]: g.remote_dma_fused([tr_], local_sem=ls)], "", "%s %s" % (gk, zk), 0.5, "hl%d%d" % (t, k), n)
+                add("n", [], ak, "", TRF, "hb%d%d" % (t, k), len(topo.engines(aid, me)), i)
+                PM([(out, Bn, zin[:, l0:l0 + nl], True, False)] + [(out, row("Wn", j), T[xg][:, lo + j:hi:16], False, False) for j in R16] +
+                   [(out, row("W2", j), T[xa][:, lo + j:hi:16], False, j == 15) for j in R16], nl, "%s.%d" % (bank, k), "Bn Wn W2 %s %s %s" % (zi, gk, ak))
+                return
             ys = range(l0, l0 + nl, VP)
             for y in ys:
                 ye_ = min(y + VP, l0 + nl)
                 x, xa_ = T[xg][:, 16 * y:16 * ye_], T[xa][:, 16 * y:16 * ye_]
                 V(lambda x=x, y=y, ye_=ye_: TT(x, T.R[:, 0:4096].indirect(T[su][:, y:ye_]), T.ze[:, 16 * y:16 * ye_], A.subtract),
-                  "%s.%d" % (gk, y), "R %s %s" % (su, zk), 16 * (ye_ - y), GA)
+                  "%s.%d" % (gk, y), "R %s %s" % (sk(y, ye_), zk), 16 * (ye_ - y), GA)
                 if mode == "a":
-                    S_(lambda x=x, xa_=xa_: ACT(xa_, x, F.Abs), "%s.%d" % (ak, y), "%s.%d" % (gk, y), 16 * (ye_ - y))
+                    S_(lambda x=x, xa_=xa_: ACT(xa_, x, F.Abs, bias=ZO), "%s.%d" % (ak, y), "%s.%d" % (gk, y), 16 * (ye_ - y))
                 else:
-                    V(lambda x=x, xa_=xa_: TS(xa_, x, 0.0, None, A.max), "%s.%d" % (ak, y), "%s.%d" % (gk, y), 16 * (ye_ - y), 0.5)
+                    V(lambda x=x, xa_=xa_: TS(xa_, x, ZO, 0.0, A.add, A.max), "%s.%d" % (ak, y), "%s.%d" % (gk, y), 16 * (ye_ - y), 0.5)
             ks = lambda key: " ".join("%s.%d" % (key, y) for y in ys)
             if mode == "b":
                 PM([(out, row("Wn", j), T[xg][:, lo + j:hi:16], j == 0, False) for j in R16], nl, "%s.%d %s.g" % (bank, k, bank), "Wn " + ks(gk))
@@ -331,6 +389,11 @@ def program(T, g, me, nxt, topo):
             records(part, "su", "xg", "xa", k, "b5" if part[2] == "b" else "b1")
         if t == 0:
             V(lambda: TS(T.hc[:], T.hB[:], T.thf[:, 0:1], None, A.add), "h", "hB thf", 4)
+        elif "h" in ONA:
+            S_(lambda: ACT(a0, T.b3[:, 128:129], F.Copy), "a0", "b3.a", 1)
+            S_(lambda: ACT(T.ai[:], a0, F.Copy, bias=-0.484375, scale=0.03125), "ai", "a0", 1)
+            S_(lambda: ACT(am, T.ai[:], F.Identity, bias=a0, scale=-32.0), "am", "ai a0", 1)
+            S_(lambda t=t: ACT(T.hc[:], T.hT[:, t, :], F.Identity, bias=am), "h", "hT am", 4)
         else:
             V(lambda: TS(T.ai[:], T.b3[:, 128:129], 0.03125, -0.484375, A.mult, A.add), "ai", "b3.a", 1)
             V(lambda: TS(am, T.ai[:], -32.0, T.b3[:, 128:129], A.mult, A.add), "am", "ai b3.a", 1)
@@ -340,7 +403,7 @@ def program(T, g, me, nxt, topo):
             ks = [k for k, part in enumerate(CM) if (part[2] == "b") == (bk == "b5")]
             if ks:
                 x, y = CM[ks[0]][0], CM[ks[-1]][0] + CM[ks[-1]][1]
-                V(lambda bk=bk, x=x, y=y: TS(T.T2[:, 0, x:y], T[bk][:, x:y], -256.0, 256.0, A.add, A.min), "dn" + bk, " ".join("%s.%d" % (bk, k) for k in ks), y - x)
+                V(lambda bk=bk, x=x, y=y: TS(T.T2[:, 0, x:y], T[bk][:, x:y], -256.0 - 16 * ZO * (bk == "b5"), 256.0, A.add, A.min), "dn" + bk, " ".join("%s.%d" % (bk, k) for k in ks), y - x)
         DN = "dnb1 dnb5"
         V(lambda: v.transpose(T.td[:], dn), "td", DN, 256, 0.5)
         turn("td", 4, "W4d", True)
@@ -355,75 +418,66 @@ def program(T, g, me, nxt, topo):
         add("v", [(lambda r=r: TC(T.li[:, LI.index("kI"), r:16:2], T.sm[:, 128 * r + 15:128 * r + 128:16])) for r in range(2)], "kI", "sm", 2 * dv(8))
         V(lambda: TS(w1, kI, 16, None, A.arith_shift_right), "w1", "kI", 16)
         V(lambda: TS(ny, kI, 4095, None, A.bitwise_and), "ny", "kI", 16)
-        V(lambda: TS(nh, w1, T.hc[:, 2:3], 8192.0, A.is_ge, A.mult), "nh", "w1 h", 16)
-        V(lambda: TT(t3, ny, nh, A.add), "t3", "ny nh", 16)
-        V(lambda: TT(t4, t3, tr, A.min), "t4", "t3 tr", 16)
-        V(lambda: TC(zo, t4), "zo", "t4", 16)
+        add("v", [(lambda r=r: TS(T.lf[:, LF.index("nh"), r:16:2], T.sm[:, 128 * r + 15:128 * r + 128:16], 2.0 ** -16, T.hc[:, 2:3], A.mult, A.is_ge))
+                  for r in range(2)], "nh", "sm h", 2 * dv(8))
+        V(lambda: TT(t3, nh, tr, A.mult), "t3", "nh tr", 16)
+        V(lambda: TT(t4, t3, ny, A.max), "t4", "t3 ny", 16)
+        AF(zo, t4, "zo", "t4", 16)
         V(lambda zin=zin: TT(T.xs[:], T.R[:].indirect(zo), zin[:], A.add), "xs", "R Rd zo " + zi, 256, GA)
-        V(lambda: TS(T.x4[:], T.xs[:], 0.5, 191.75, A.mult, A.add), "x4", "xs", 256, 0.5)
-        V(lambda zout=zout: TS(zout[:], T.x4[:], -192.0, None, A.add), zo_, "x4", 256, 0.5)
+        V(lambda zout=zout: TS(zout[:], T.xs[:], 0.5, ZO / 2 - 0.25, A.mult, A.add), zo_, "xs", 256, 0.5)
         send("z", zo_, "zin%d" % (t + 1), t)
-        if EVAC == "a":
-            S_(lambda: ACT(T.pg[:], T.PT[:].indirect(zo), F.Copy, bias=-2048.0), "pg", "PT PT1 zo", 256, GA)
-        else:
-            V(lambda: TS(T.pg[:], T.PT[:].indirect(zo), -2048.0, None, A.add), "pg", "PT PT1 zo", 256, GA)
-        V(lambda: TS(T.w5h[:], w1, 5.0, None, A.mult), "w5h", "w1", 16)
+        S_(lambda: ACT(T.pg[:], T.PT[:].indirect(zo), F.Identity, bias=k3), "pg", "PT PT1 zo k2", 256, GA)
+        AF(T.w5h[:], w1, "w5h", "w1", 16, 5.0)
         PM([(T.b3[:, 48:64], x, y, n == 0, False) for n, (x, y) in enumerate(((Ib, T.k16[:, 16:32]), (I4n, fin[:]), (In, T.uh[:]), (Ib, T.w5h[:])))] +
            [(T.b3[:, 48:64], row("Wb", j), T.pg[:, j:256:16], False, j == 15) for j in R16], 16, "b3.d", "Wb Ib In I4n k16 uh w5h pg " + fi)
         V(lambda: TT(ph, ps, nh, A.is_gt), "ph", "ps.0 nh", 16)
         V(lambda: TT(pdh, ph, T.b3[:, 48:64], A.mult), "pdh", "ph b3.d", 16)
         WB = T.b5[:, 256:272]
         first("EQ", "b5", lambda x, y: T.rows[:, x:y], "rows", lambda b: T.kf[:, b:b + 1], "kf", "ps", ALL)
-        V(lambda: TT(rr, WB, pdh, A.mult), "rr", "b5.w pdh", 16)
+        V(lambda: TT(rr, WB, pdh, A.mult), "rr", "b5.w0 pdh", 16)
         V(lambda: TT(fr, rr, T.b3[:, 64:80], A.add), "fr", "rr b3.f", 16)
         V(lambda: TS(fr2, fr, 4095, None, A.bitwise_and), "fr2", "fr", 16)
-        V(lambda fout=fout: TS(fout[:], fr2, -2048.0, None, A.add), fo, "fr2", 16)
+        AF(fout[:], fr2, fo, "fr2", 16, bias=-2048.0)
         send("f", fo, "fin%d" % (t + 1), t)
-        V(lambda: TT(acc, WB, ps, A.mult), "acc", "b5.w ps.0", 16)
+        V(lambda: TT(acc, WB, ps, A.mult), "acc", "b5.w0 ps.0", 16)
         if t < NV - 1:
             S_(lambda: ACT(T.accb[:], acc, F.Copy, accum_out=af), "accb af", "acc", 16)
             PM([(T.b3[:, 128:129], one, af, True, True)], 256, "b3.a", "one af")
         for k, part in enumerate(EM):
             records(part, "su2", "eg", "ea", k, "b2")
-        if KMAX == "p":
-            V(lambda: v.transpose(T.tx[:], dd), "tx", "dd", 256, 0.5)
-            PM([(T.b0[:, 256:512], Ib, T.ck[:, 256:512], True, False)], 256, "b0.x b0.w b0.n b0.g", "Ib ck")
-            for dst, k0, key in (("ts", 0, "W4"), ("td", 4, "W4d"), ("tx", 8, "W4x")):
-                turn(dst, k0, key, k0 == 8, 256, "b0.x")
-            V(lambda: v.tensor_tensor_scan(T.sx[:], T.d0x[:], T.b0[:, 256:512], 0.0, A.add, A.max), "sx", "d0x b0.x b0.w b0.n", 256)
-        else:
-            S_(lambda: ACT(T.mM[:], T.b0[:, 0:256], F.Relu, bias=-64.0 * 16000000.0, scale=64.0), "mM", "b0.k", 256)
-            V(lambda: TT(T.kr[:], T.b0[:, 0:256], T.mM[:], A.subtract), "kr", "b0.k mM", 256)
-            V(lambda: v.tensor_tensor_scan(T.sx[:], T.d0x[:], T.kr[:], 0.0, A.add, A.max), "sx", "d0x kr", 256)
+        S_(lambda: ACT(T.mM[:], T.b0[:, 0:256], F.Relu, bias=-64.0 * 16000000.0, scale=64.0), "mM", "b0.k", 256)
+        V(lambda: TT(T.kr[:], T.b0[:, 0:256], T.mM[:], A.subtract), "kr", "b0.k mM", 256)
+        V(lambda: v.tensor_tensor_scan(T.sx[:], T.d0x[:], T.kr[:], 0.0, A.add, A.max), "sx", "d0x kr", 256)
         add("v", [(lambda r=r: TC(T.li[:, LI.index("fI"), r:16:2], T.sx[:, 128 * r + 15:128 * r + 128:16])) for r in range(2)], "fI", "sx", 2 * dv(8))
         V(lambda: TS(foe, fI, 2.0 ** -16, T.hc[:, 3:4], A.mult, A.is_ge), "foe", "fI h", 16)
         V(lambda: TS(vs, fI, 4095, None, A.bitwise_and), "vs", "fI", 16)
-        V(lambda: TS(vk, vs, -2048.0, None, A.add), "vk", "vs", 16)
-        V(lambda: TS(T.v16[:], vs, -2048.0, None, A.add), "v16", "vs", 16)
+        AF(vk, vs, "vk", "vs", 16, bias=-2048.0)
+        AF(T.L2[:, 0:16], vs, "v16", "vs", 16, bias=-2048.0)
         V(lambda: TT(vrm, vs, tr, A.subtract), "vrm", "vs tr", 16)
-        spread("b4", 0, "v16", 16, "b4.0")
-        evac(T.vrow[:], T.b4[:, 0:256], "vrow", "b4.0", 256)
+        PM([(T.b4[:, j:512:16], T.Sp[:, j, :], T.L2[:], True, True) for j in R16], 32, "b4.0 b4.1", "Sp v16 mneg")
+        evac(T.vrow[:, 0:256], T.b4[:, 0:256], "vrow", "b4.0", 256)
+        evac(T.vrow[:, 256:512], T.b4[:, 256:512], "nrow", "b4.1", 256)
         V(lambda: TT(flg, foe, acc, A.mult), "flg.0", "foe acc", 16)
         V(lambda: TT(fv, flg, vrm, A.mult), "fv", "flg.0 vrm", 16)
-        first("EQv", "b5", lambda x, y: T.vrow[:, x:y], "vrow", lambda b: lfc("vk", b), "vk", "flg", ALL)
-        V(lambda: TT(dl, WB, fv, A.mult), "dl", "b5.w fv", 16)
-        V(lambda: TT(dl, dl, tr, A.add), "dl", "dl tr", 16)
-        V(lambda: TC(dlu, dl), "dlu", "dl", 16)
+        V(lambda: TT(fv, fv, T.sp[:, 0:16], A.add), "fv", "fv sp", 16)
+        first("EQv", "b5", lambda x, y: T.vrow[:, x:y], "vrow", lambda b: lfc("vk", b), "vk", "flg", ALL, 0)
+        V(lambda: TT(dl, WB, fv, A.max), "dl", "b5.w0 fv", 16)
+        AF(dlu, dl, "dlu", "dl", 16, bias=2304.0)
         V(lambda: TC(T.R[:].indirect(dlu), T.s64[:]), "R Rd", "dlu s64", 256, SC)
         V(lambda: TT(T.la[:, 0:16], acc, T.RM[:, 0:16], A.mult), "la0", "acc RM", 16)
         V(lambda: TT(T.la[:, 16:32], acc, T.RM[:, 16:32], A.mult), "la1", "acc RM", 16)
         V(lambda: TT(T.la[:], T.la[:], T.T2c[:], A.add), "la0 la1", "la0 la1 T2c", 32)
-        V(lambda: TC(T.lau[:], T.la[:]), "lau", "la0 la1", 32)
-        V(lambda zout=zout: TC(T.R[:].indirect(T.lau[:, 0:16]), zout[:]), "R Rd", "lau " + zo_, 256, SC)
+        AF(T.lau[:], T.la[:], "lau", "la0 la1", 32)
+        V(lambda zout=zout: TT(T.R[:].indirect(T.lau[:, 0:16]), zout[:], T.zof[:], A.add), "R Rd", "zof lau " + zo_, 256, SC)
         spread("b4", 256, fo, 16, "b4.1")
         S_(lambda: ACT(T.phr[:], T.b4[:, 256:512], F.Identity, bias=k2, scale=lfc("I16", 0)), "phr", "b4.1 k2", 256)
-        V(lambda: TC(T.PT[:].indirect(T.lau[:, 0:16]), T.phr[:]), "PT PT1", "lau phr", 256, SC)
-        Q = T.b1[:, 256:512]
-        if OWN == "p":
-            own, ok = [(T.b1[:, 256 + j:512:16], T.Sp[:, j, :], T.mneg[:], False, False) for j in R16], "Sp mneg"
+        if OFF:
+            S_(lambda: ACT(T.PT[:].indirect(T.lau[:, 0:16]), T.phr[:], F.Silu), "PT PT1", "lau phr", 256, SC if t else SC + 6)
         else:
-            own, ok = [(Q, Ib, T.nrow[:], False, False)], "Ib nrow"
-        PM([(Q, I6, T.on[:], True, False)] + own + [(Q, Y1, dd, False, True)], 85 if OWN == "p" else 256, "b1.q b1.g", "I6 on Y1 dd " + ok)
+            V(lambda: TC(T.PT[:].indirect(T.lau[:, 0:16]), T.phr[:]), "PT PT1", "lau phr", 256, SC)
+        Q = T.b1[:, 256:512]
+        own = (Q, Ib, T.vrow[:, 256:512], False, False)
+        PM([(Q, I6, T.on[:, 0:256], True, False), (Q, Y1, dd, False, False), own[:4] + (True,)], 256, "b1.q b1.g", "I6 on Y1 dd Ib nrow")
         S_(lambda: ACT(T.n1[:], Q, F.Copy, bias=-8192.0, scale=-1.0), "n1", "b1.q", 256)
         V(lambda: TT(T.a1[:], Q, T.sF[:], A.min), "a1", "b1.q sF", 256)
         V(lambda: TT(T.C[:].indirect(T.lau[:, 16:32]), T.a1[:], T.n1[:], A.max), "C", "lau a1 n1", 256, SC)
@@ -433,23 +487,34 @@ def program(T, g, me, nxt, topo):
             PM([(T.b3[:, 80 + x:80 + y], row("Wb", j), T.sup[:, 16 * x + j:16 * y:16], j == 0, j == 15) for j in R16], 16, "b3.c%d" % k, "Wb sup.%d" % k)
             V(lambda x=x, y=y: TT(lfc("cnd", x, y), lfc("acc", x, y), T.b3[:, 80 + x:80 + y], A.is_gt), "cnd.%d" % k, "acc b3.c%d" % k, 16)
         S_(lambda: ACT(T.sg2[:], T.b2[:, 0:256], F.Sign, bias=-511.5), "sg2", " ".join("b2.%d" % z for z in range(len(EM))), 256)
-        PM([(Q, Y2c, T.on[:], True, False)] + own, 75 if OWN == "p" else 256, "b1.q b1.g", "Y2c on " + ok)
+        PM([(Q, Y2c, T.on[:, 0:256], True, False), own], 256, "b1.q b1.g", "Y2c on Ib nrow")
         PM([(Q, Y2, T.sg2[:], False, True)], 256, "b1.q b1.g", "Y2 sg2")
         S_(lambda: ACT(T.n2[:], Q, F.Copy, bias=-8192.0, scale=-1.0), "n2", "b1.q", 256)
         S_(lambda: ACT(T.sF2[:], T.C[:, 0:1024].indirect(eu), F.Copy), "sF2", "C eu", 256, GA)
         V(lambda: TT(T.a2[:], Q, T.sF2[:], A.min), "a2", "b1.q sF2", 256)
-        V(lambda: TT(cr, cnd, T.RM[:, 32:48], A.mult), "cr", "RM " + " ".join("cnd.%d" % k for k in range(len(EP))), 16)
-        first("EQe", "b0", lambda x, y: T.rows[:, 256 + x:256 + y], "rows", lambda b: T.kf[:, 16 + b:17 + b], "kf", "cnd", EP)
-        V(lambda: TT(l2, T.b0[:, 256:272], cr, A.mult), "l2", "b0.w cr", 16)
-        V(lambda: TT(l2, l2, tc, A.add), "l2", "l2 tc", 16)
-        V(lambda: TC(l2u, l2), "l2u", "l2", 16)
-        V(lambda: TT(T.C[:].indirect(l2u), T.a2[:], T.n2[:], A.max), "C", "l2u a2 n2", 256, SC)
+        first("EQe", "b0", lambda x, y: T.rows[:, 256 + x:256 + y], "rows", lambda b: T.kf[:, 16 + b:17 + b], "kf", "cnd", EP, 16, SPLIT)
+        for h, (x, y) in enumerate(((0, 8), (8, 16)) if SPLIT else ALL):
+            c_, l_, u_ = lfc("cr", x, y), lfc("l2", x, y), T.lu[:, LU.index("l2u"), x:y]
+            V(lambda x=x, y=y, c_=c_: TT(c_, lfc("cnd", x, y), T.RM[:, 32 + x:32 + y], A.mult), "cr.%d" % h,
+              "RM " + " ".join("cnd.%d" % k for k, (x1, y1) in enumerate(EP) if x1 < y and x < y1), 16)
+            V(lambda x=x, y=y, c_=c_: TT(c_, c_, lfc("tc", x, y), A.add), "cr.%d" % h, "cr.%d tc" % h, 16)
+            V(lambda x=x, y=y, c_=c_, l_=l_: TT(l_, T.b0[:, 256 + x:256 + y], c_, A.max), "l2.%d" % h, "b0.w%d cr.%d" % (h, h), 16)
+            AF(u_, l_, "l2u.%d" % h, "l2.%d" % h, 16)
+            V(lambda x=x, y=y, u_=u_: TT(T.C[:].indirect(u_), T.a2[:, 16 * x:16 * y], T.n2[:, 16 * x:16 * y], A.max), "C", "l2u.%d a2 n2" % h, 16 * (y - x), SC)
     now[0] = -2
-    D("yrec", T.yrec[:], T.R[:, 0:4096], "", "R", 7.0)
+    i = D("yrec", T.yrec[:], T.R[:, 0:4096], "", "R", 7.0)
+    add("n", [], "", "", 9.5, None, 0, i)
     D("ycel", T.ycel[:], T.C[:, 0:1024], "", "C", 4.5, "a")
-    D("ypo", T.ypo[:], T.PT[0:128:16, 0:4096], "", "PT PT1", 3.0)
+    if OFF:
+        D("pb", T.posf[:], T.PT[0:128:16, 0:4096], "posf", "PT PT1", 2.5)
+        V(lambda: TS(T.pos[:], T.posf[:], -OFF, None, A.add), "pos", "posf", 256)
+        V(lambda: TC(T.posf[:], T.pos[:]), "posf", "pos", 256)
+        D("ypo", T.ypo[:], T.posf[:], "", "posf", 2.5)
+    else:
+        D("ypo", T.ypo[:], T.PT[0:128:16, 0:4096], "", "PT PT1", 3.0)
     zl, fl = "zin%d" % NV, "fin%d" % NV
-    D("ypat", T.ypat[:], T[zl][:], "", zl, 2.0)
+    S_(lambda: ACT(T.xs[:], T[zl][:], F.Copy, bias=-ZO), "xs", zl, 256)
+    D("ypat", T.ypat[:], T.xs[:], "", "xs", 2.0)
     spread("b4", 0, fl, 16, "b4.0")
     S_(lambda: ACT(T.phr[:], T.b4[:, 0:256], F.Copy, bias=2048.0), "phr", "b4.0", 256)
     D("yphi", T.yphi[:], T.phr[0:128:16, :], "", "phr", 2.0)
@@ -466,66 +531,106 @@ def schedule(ops):
             fwd[k].append((x, lag))
             bwd[x].append((k, lag + occ[k] - occ[x]))
 
-    def place(rank, before, after, first):
-        at, need = [0.0] * n, [len(x) for x in before]
-        lines = {}
-        ready = [i for i in range(n) if not need[i]]
-        while ready:
-            i = min(ready, key=lambda i: rank[i])
-            ready.remove(i)
-            o = ops[i]
-            t = max([first[i]] + [at[x] + lag for x, lag in before[i]])
-            held = [(o["q"], 0.0)] * (o["q"] != "n") + [(b, WAKE) for b in o["bank"]]
+    holds = [[(o["q"], 0.0)] * (o["q"] != "n") + [(b, WAKE) for b in o["bank"]] for o in ops]
+
+    queue, zero, tail = [o["q"] for o in ops], [0.0] * n, [o["d"] - occ[o["i"]] for o in ops]
+
+    def place(order, before, first):
+        at, lines = [0.0] * n, {key: [] for held in holds for key, gap in held}
+        for i in order:
+            t, d, me, held = first[i], occ[i] - 1e-9, queue[i], holds[i]
+            for x, lag in before[i]:
+                if at[x] + lag > t:
+                    t = at[x] + lag
             moved = True
             while moved:
                 moved = False
                 for key, gap in held:
-                    line = lines.setdefault(key, [])
-                    k = len(line)
-                    while k and line[k - 1][1] + gap > t + 1e-9:
+                    line = lines[key]
+                    m = k = len(line)
+                    lim = t - gap + 1e-9
+                    while k and line[k - 1][1] > lim:
                         k -= 1
-                    for s, e, q in line[k:]:
-                        if s >= t + occ[i] + gap - 1e-9:
+                    while k < m:
+                        s, e, q = line[k]
+                        if s >= t + d + gap:
                             break
-                        if gap == 0.0 or q != o["q"]:
+                        if gap == 0.0 or q != me:
                             t, moved = e + gap, len(held) > 1
+                        k += 1
             for key, gap in held:
                 line = lines[key]
                 k = len(line)
                 while k and line[k - 1][0] > t:
                     k -= 1
-                line.insert(k, (t, t + occ[i], o["q"]))
+                line.insert(k, (t, t + occ[i], me))
             at[i] = t
-            for k, lag in after[i]:
-                need[k] -= 1
-                if not need[k]:
-                    ready.append(k)
         return at
 
+    def run(order):
+        at, why, last, end, final = [0.0] * n, [None] * n, {}, 0.0, 0
+        for i in order:
+            t, w = 0.0, None
+            for x, lag in fwd[i]:
+                if at[x] + lag > t:
+                    t, w = at[x] + lag, (x, False)
+            for key, gap in holds[i]:
+                x = last.get(key)
+                if x is not None and (gap == 0.0 or queue[x] != queue[i]) and at[x] + occ[x] + gap > t + 1e-9:
+                    t, w = at[x] + occ[x] + gap, (x, True)
+                last[key] = i
+            at[i], why[i] = t, w
+            if t + ops[i]["d"] > end:
+                end, final = t + ops[i]["d"], i
+        return at, why, final, end
+
+    def tighten(at):
+        back = place(sorted(range(n), key=lambda i: (-at[i] - occ[i], -i)), bwd, tail)
+        at = place(sorted(range(n), key=lambda i: (-back[i] - occ[i], i)), fwd, zero)
+        order = sorted(range(n), key=lambda i: (at[i], i))
+        at, why, final, end = run(order)
+        return end + 0.1 * sum(at) / n, order, why, final, end
+
+    def swap(order, x, i, up):
+        lo, hi = order.index(x), order.index(i)
+        if lo > hi:
+            return False
+        part, moved = order[lo:hi + 1], {i if up else x}
+        for y in part[-2::-1] if up else part[1:]:
+            if any(z in moved for z, lag in (bwd if up else fwd)[y]):
+                if y in (x, i):
+                    return False
+                moved.add(y)
+        order[lo:hi + 1] = sorted(part, key=lambda y: (y in moved) != up)
+        return True
+
     if not ORDER:
-        rank, best, seed = list(range(n)), None, 1
-        same = {o["tag"]: o["i"] for o in ops}
-        for _ in range(ROUNDS):
-            at = place(rank, fwd, bwd, [0.0] * n)
-            end = max(at[i] + ops[i]["d"] for i in range(n))
-            if best is None or end <= best[0]:
-                best = (end, at)
-            end, at = best
-            rank = []
-            seed = seed * 16807 % 2147483647
-            if _ % 8 == 7:
-                m = seed % NV
-                t0 = [at[same["su", t]] for t in range(NV)]
-                rank = [t0[o["tag"][1]] + at[same[o["tag"][0], m]] - t0[m] if (o["tag"][0], m) in same and o["tag"][1] >= 0 else at[o["i"]] for o in ops]
-                continue
-            lo, amp = (seed % 1000) * 1e-3 * end - SPAN / 2, (seed // 1000 % 1000) * 1e-3 * JIT
-            for i in range(n):
-                seed = seed * 16807 % 2147483647
-                rank.append(-(at[i] + occ[i]) + (amp * seed / 2147483647 if lo <= at[i] < lo + SPAN else 0.0))
-            back = place(rank, bwd, fwd, [ops[i]["d"] - occ[i] for i in range(n)])
-            rank = [-(back[i] + occ[i]) for i in range(n)]
-        ORDER.append(sorted(range(n), key=lambda i: (best[1][i], i)))
-        ORDER.append(best[0])
+        rng, same = np.random.default_rng(SEED), {o["tag"]: o["i"] for o in ops}
+        now = best = tighten(place(range(n), fwd, zero))
+        for k in range(ROUNDS):
+            order, why, i = now[1][:], now[2], now[3]
+            pairs = []
+            while why[i]:
+                if why[i][1]:
+                    pairs.append((why[i][0], i))
+                i = why[i][0]
+            j, up = int(rng.integers(len(pairs))), rng.random() < 0.5
+            x, i = pairs[j]
+            for _ in range(int(rng.integers(4))):
+                if up and j + 1 < len(pairs) and pairs[j + 1][1] == x:
+                    j, x = j + 1, pairs[j + 1][0]
+                if not up and j and pairs[j - 1][0] == i:
+                    j, i = j - 1, pairs[j - 1][1]
+            (a, ta), (b, tb) = ops[x]["tag"], ops[i]["tag"]
+            todo = [(x, i)]
+            if rng.random() < 0.8 and min(ta, tb) >= 0:
+                todo = [(same[a, ta + d], same[b, tb + d]) for d in range(-min(ta, tb), NV) if (a, ta + d) in same and (b, tb + d) in same]
+            if any([swap(order, x, i, up) for x, i in todo]):
+                new = tighten(run(order)[0])
+                if new[0] <= now[0] + HEAT * (1 - k / ROUNDS) * rng.random():
+                    now = new
+                    best = min(best, now, key=lambda y: y[4])
+        ORDER.extend([best[1], best[4]])
     order = ORDER[0]
     held = {}
     for i in order:
@@ -539,6 +644,16 @@ def schedule(ops):
 def rank_program(g, core, T, topo):
     rank = T.rank_of(core)
     if rank is None:
+        for c in T.cores:
+            if helper(c, T, topo) == core:
+                rid, pid, _ = topo.addr(c)
+                parts = [(t, k, x, n) for t in range(NV) for k, (x, n, m) in enumerate(EM) if m == "f"]
+                for t, k, x, n in parts:
+                    g.wait_ge(T.sem["ho%d%d" % (t, k)], len(topo.engines(c, core)))
+                    g.remote_dma(T.ea[:, 16 * x:16 * (x + n)], T[LAND[t]][:, 16 * x:16 * (x + n)], T.sem["hb%d%d" % (t, k)], T.sem["hk%d%d" % (t, k)],
+                                 pid, rid, topo.mask(core, c))
+                for t, k, x, n in parts:
+                    g.wait_ge(T.sem["hk%d%d" % (t, k)], len(topo.engines(core, c)))
         return
     nxt = T.cores[(rank + 1) % len(T.cores)]
     ops = program(T, g, core, nxt, topo)
@@ -550,6 +665,8 @@ def rank_program(g, core, T, topo):
         o = ops[i]
         q = o["q"]
         if q == "n":
+            if o["sem"] is None:
+                continue
             ev[i] = (o["sem"], o["val"])
             clock[i] = {o["sem"]: o["val"]}
             final[o["sem"]] = o["val"]

@@ -1,43 +1,41 @@
 import numpy as np
-from concourse.bass import DstId, RemoteDMATransfer
 from concourse.mybir import AluOpType as A, AxisListType, ActivationFunctionType as F
 
 NV = 4
 CM = [(0, 64, "c"), (64, 64, "c"), (128, 64, "b"), (192, 64, "b")]
-EM = [(0, 64, "c"), (64, 64, "c"), (128, 64, "c"), (192, 64, "a")]
-VP = 64
-EP = [(0, 12), (12, 16)]
+EMS = [[(192, 64, "a"), (128, 64, "c"), (0, 64, "c"), (64, 64, "c")]] * NV
+VP, VE = 64, 32
+EP = [(0, 8), (8, 16)]
 ZE0, ZE = "va" * 4, "ga" * 4
 EVAC = "a"
-PTG = 2816
-TRF = 5.0
+PTG = 4352
 TRN = 4.2
-KMAX, SPLIT, SU = "v", False, 8
-LATE = ("EQe",)
-ONA = "xr u32 u2 uh h".split()
-ROUNDS, HEAT, SEED = 12000, 0.5, 1
+KMAX, SPLIT, SU = "v", True, 8
+LATE, XA, S2 = ("EQe0", "EQe1"), ("EQe", "EQv"), False
+ONA = "xr u32 u2 uh h C sa l2u dlu lau fout".split()
+ROUNDS, HEAT, SEED = 14000, 1.0, 2
 ORDER = []
-CY, PE, WAKE = 0.95e-3, 0.49e-3, 0.25
+CY, PE, WAKE = 0.92e-3, 0.49e-3, 0.25
 GA, SC = 1.56, 3.8
 BIG = 16384.0
-PRE = True
+PRE, SHARE = True, 40
 ZO = 192.0
 OFF = 64.0
 
 B, H, F4, I4, U2 = "bfloat16", "float16", "float32", "int32", "uint16"
 SHAPES = {
-    B: "R:4352 xg:4096 xa:4096 eg:4096 ea:4096 sup:256 mM:256 sg2:256 xs:256 zof:256 ck:256 s64:256 on:512 accb:16 k16:32 "
+    B: "R:4352 xg:4096 xa:4096 eg:4096 ea:4096 sup:256 mM:256 sg2:256 xs:256 zof:256 ck:512 d0n:256 d0x:256 thb:64 s64:256 on:512 accb:32 k16:32 "
        "Wb:144 W2:144 Wn:144 W3:144 Ww:144 Vs:240 VsB:240",
     H: "sp:32 rows:512 vrow:512 s16:256 pg:256 phh:256 thh:4 L3:32 L2:32 uh:16 w5h:16",
     F4: "C:1280 PT:4352 posf:256 sF:256 sF2:256 a1:256 a2:256 n1:256 n2:256 phr:256 thf:4 hc:4 hB:4 kr:256 Iw:160 thr:128 "
-        "B8a:8 B8:8 g16:8 g16b:8 K3:48 rc:2 d0n:256 d0x:256 RM:48 kf:32 T2c:32 la:32 col:16",
+        "B8a:8 B8:8 g16:8 g16b:8 K3:48 rc:2 RM:48 kf:32 T2c:32 la:32 col:16",
     I4: "Ci:1024 pos:256 phl:256 thl:4 wl:1 ai:1 CI:48",
     U2: "su:256 su2:256 lau:32",
 }
 LF = "u32 nh t3 t4 tq ps ph pdh rr acc dl l2 foe flg vk fv cnd cr vrm jr I16 b256 i16 iL tr tc pw pwb hf".split()
 LI = "ui u2 xq xr ye kI ny w1 fI vs fr fr2 yf".split()
 LU = "cu eu zo dlu l2u".split()
-MB = "Ib In I5 I4n I6 Y1 Y2 Y2c Zb".split()
+MB = "Ib In I5 I4n I6 Y1 Y2 Y2c Zb Ix".split()
 MF = "one Bba Bta Bt Utf Ulf".split()
 SCRATCH = {}
 for _d, _l in SHAPES.items():
@@ -60,21 +58,15 @@ for _b in range(8):
     SCRATCH["b%d" % _b] = ("psum", [128, 512], F4)
 DMAS = ["rec", "cel", "wt", "pat", "phi", "th", "po", "pt", "pb", "yrec", "ycel", "ypo", "ypat", "yphi"]
 SEMAPHORES = ["qv", "qa", "qp", "qg"] + ["d" + n for n in DMAS] + ["%s%d" % (k, t) for k in ("zr", "zl", "fr", "fl") for t in range(NV)]
-SEMAPHORES += ["%s%d%d" % (x, t, k) for x in ("ho", "hl", "hb", "hk") for t in range(NV) for k in range(4)]
-LAND = ["xg", "xa", "eg", "ea"]
-
-
-def helper(core, T, topo):
-    return [c for c in topo.cores_of(core) if T.rank_of(c) is None and topo.die(c) == topo.die(core)][0]
 
 
 def dv(n, rate=1.0):
-    return 0.055 + n * rate * CY if rate > 1.2 else max(64, n * rate) * CY
+    return 0.055 + n * rate * CY if rate > 1.2 else max(64, n * rate) * CY + 0.015
 
 
 def program(T, g, me, nxt, topo):
     v, a, p, s = g.vector, g.scalar, g.tensor, g.sync
-    ops, aid = [], helper(me, T, topo)
+    ops = []
     last, tags, now = {}, set(), [-1]
 
     def add(q, fns, w, r, d, sem=None, val=0, net=None):
@@ -129,12 +121,12 @@ def program(T, g, me, nxt, topo):
      hf) = [T.lf[:, k, :] for k in range(len(LF))]
     ui, u2, xq, xr, ye, kI, ny, w1, fI, vs, fr, fr2, yf = [T.li[:, k, :] for k in range(len(LI))]
     cu, eu, zo, dlu, l2u = [T.lu[:, k, :] for k in range(len(LU))]
-    Ib, In, I5, I4n, I6, Y1, Y2, Y2c, Zb = [T.mb[:, k, :] for k in range(len(MB))]
+    Ib, In, I5, I4n, I6, Y1, Y2, Y2c, Zb, Ix = [T.mb[:, k, :] for k in range(len(MB))]
     one, Bba, Bta, Bt, Utf, Ulf = [T.mf[:, k, :] for k in range(len(MF))]
     pc, gs, jc, j16, p2, p3, wf, af, am, k2, a0, k3, ws = [T.col[:, k:k + 1] for k in range(13)]
     lfc = lambda name, lo, hi=None: T.lf[:, LF.index(name), lo:hi or lo + 1]
     row = lambda name, j: T[name][:, 15 - j:143 - j]
-    idf = T.Iw[:, 16:144]
+    idf, acc = T.Iw[:, 16:144], T.accb[:, 0:16]
 
     def evac(out, in_, w, r, n, bias=0.0):
         if EVAC == "a":
@@ -175,7 +167,8 @@ def program(T, g, me, nxt, topo):
     G(lambda: sel(Ulf, T.Bf[:], [[-1, 128]], A.is_gt, 0, 1), "Ulf", "Bf", 128)
     G(lambda: iota(T.ck[:, 0:256], [[0, 16], [4096, 16]], 2048), "ck", "", 256)
     G(lambda: iota(T.PT[:, 0:PTG], [[0, PTG]]), "PT", "B8 Iw Bf Bt Utf Ulf ck jr pc g16 b256", PTG)
-    V(lambda: MS(T.PT[:, PTG:4352], 0.0), "PT1", "", 4352 - PTG)
+    if PTG < 4352:
+        V(lambda: MS(T.PT[:, PTG:4352], 0.0), "PT1", "", 4352 - PTG)
     V(lambda: MS(T.Wb[:], 0.0), "Wb", "", 144, 0.5)
     V(lambda: TC(T.Wb[:, 15:128:16], T.B8[:]), "Wb", "B8", 8)
     V(lambda: TC(wf, T.wl[:]), "wf", "wl", 1)
@@ -196,18 +189,22 @@ def program(T, g, me, nxt, topo):
     V(lambda: TS(iL, i16, -1.0, 2048.0, A.mult, A.add), "iL", "i16", 16)
     add("v", [lambda: TT(T.K3[:, 0:16], tr, i16, A.subtract), lambda: TC(T.K3[:, 16:32], tc), lambda: TC(T.K3[:, 32:48], tc),
               lambda: TC(T.T2c[:, 0:16], tr), lambda: TC(T.T2c[:, 16:32], tc)], "K3 T2c", "i16 tr tc", 5 * dv(16))
-    add("v", [(lambda k=k, y=y: MS(T.hB[:, k:k + 1], y)) for k, y in enumerate((0.0, -512.0, -256.0, -255.0625))], "hB", "", 4 * dv(1))
+    add("v", [(lambda k=k, y=y: MS(T.hB[:, k:k + 1], y)) for k, y in enumerate((0.0, -512.0, -256.0, -256.0 if KMAX == "p" else -255.0625))], "hB", "", 4 * dv(1))
     add("a", [(lambda j=j: ACT(T.Sp[:, j, :], T.Bf[:], F.Copy, scale=lfc("I16", j))) for j in R16], "Sp", "Bf I16", 16 * dv(128))
     V(lambda: RED(T.rc[:, 0:1], T.B8[:, 0:8:2]), "rc", "B8", 4)
     V(lambda: RED(T.rc[:, 1:2], T.B8[:, 1:8:2]), "rc", "B8", 4)
     add("a", [(lambda k=k, x=x, r=r: ACT(T.W4[:, k, :], T.Iw[:, x:x + 128], F.Copy, scale=T.rc[:, r:r + 1]))
               for k, (x, r) in enumerate(((16, 0), (0, 0), (32, 1), (16, 1)))], "W4", "Iw rc", 4 * dv(128))
     V(lambda: TS(T.W4[:, 4:8, :], T.W4[:, 0:4, :], 65536.0, None, A.mult), "W4d", "W4", 512, 0.5)
-    for m, name, x in ((Ib, "Ib", 1.0), (In, "In", -1.0), (I5, "I5", 5.0), (I4n, "I4n", -4.0), (I6, "I6", 6144.0)):
+    if KMAX == "p":
+        V(lambda: TS(T.W4[:, 8:12, :], T.W4[:, 0:4, :], 67108864.0, None, A.mult), "W4x", "W4", 512, 0.5)
+        V(lambda: TS(T.ck[:, 256:512], T.ck[:, 0:256], -1.0, 65536.0, A.mult, A.add), "ck2", "ck", 256, 0.5)
+    for m, name, x in ((Ib, "Ib", 1.0), (In, "In", -1.0), (I5, "I5", 5.0), (I4n, "I4n", -4.0), (Ix, "Ix", 16.0)):
         S_(lambda m=m, x=x: ACT(m, idf, F.Copy, scale=x), name, "Iw", 128)
-    V(lambda: MS(T.d0n[:], 0.0), "d0n", "", 256)
+    add("a", [lambda: ACT(I6, idf, F.Silu, scale=6144.0)], "I6", "Iw", 1.45)
+    V(lambda: MS(T.d0n[:], 0.0), "d0n", "", 256, 0.5)
     V(lambda: MS(T.d0n[:, 0:256:16], 134217728.0), "d0n", "", 16)
-    V(lambda: MS(T.d0x[:], 8192.0), "d0x", "", 256)
+    V(lambda: MS(T.d0x[:], 0.0 if KMAX == "p" else 8192.0), "d0x", "", 256, 0.5)
     V(lambda: MS(T.d0x[:, 0:256:16], -268435456.0), "d0x", "", 16)
     V(lambda: MS(hf, 0.5), "hf", "", 16)
     V(lambda: v.tensor_tensor_scan(pw, hf, hf, 65536.0, A.mult, A.max), "pw", "hf", 16)
@@ -215,6 +212,8 @@ def program(T, g, me, nxt, topo):
     V(lambda: RED(p2, pwb), "p2", "pwb", 16)
     V(lambda: TS(p3, p2, 2.0, 1.0, A.mult, A.add), "p3", "p2", 1)
     V(lambda: TS(T.thr[:], Bt, p3, -1.0, A.mult, A.add), "thr", "Bt p3", 128)
+    if XA:
+        S_(lambda: ACT(T.thb[:], T.thr[:, 0:64], F.Copy), "thb", "thr", 64)
     V(lambda: MS(T.Wt[:, :, 0:7], 0.0), "Wt", "", 56, 0.5)
     V(lambda: TS(T.Wt[:, :, 7], T.B8[:], p2, None, A.mult), "Wt", "B8 p2", 8)
     V(lambda: TS(T.Wt[:, :, 8:16], T.Bf[:, :, 0:8], 65536.0, None, A.mult), "Wt", "Bf", 64)
@@ -243,33 +242,43 @@ def program(T, g, me, nxt, topo):
     V(lambda: TS(T.posf[:], T.pos[:], OFF, None, A.add), "posf", "pos", 256)
     D("pt", T.PT[0:128:16, 0:4096], T.posf[:], "PT PT1", "posf", 2.5)
 
-    def first(eq, bank, rows, rkey, key, kkey, flag, parts, spare=None, split=False):
+    def first(eq, bank, rows, rkey, key, kkey, flag, parts, spare=None, within=False, split=False):
         lo = lambda b: 64 * (b // 4)
         part = lambda b: [k for k, (x, y) in enumerate(parts) if x <= b < y][0]
-        late = eq in LATE
-        for bs in ((0, 1), (2, 3), (4, 5), (6, 7), (8, 9, 10, 11), (12, 13, 14, 15)):
-            fk, ks, d = "%s.%d" % (flag, part(bs[0])), lambda k: " ".join("%s.%d" % (k, b) for b in bs), len(bs) * dv(256 - lo(bs[0]), 0.5)
-            if late:
-                add("v", [(lambda b=b: TS(T[eq][:, b, lo(b):256], rows(lo(b), 256), key(b), None, A.is_equal)) for b in bs], ks(eq), rkey + " " + kkey, d)
-                xy = [(b, 7 - b % 8, 16 if b < 8 else 15 - b % 8) for b in bs]
+        late = lambda b: "%s%d" % (eq, b // 8) in LATE
+        hi = lambda b: 128 * (b // 8 + 1) if within else 256
+        for bs in ((0, 1, 2, 3), (4, 5, 6, 7), (8, 9, 10, 11), (12, 13, 14, 15)) if within else ((0, 1), (2, 3), (4, 5), (6, 7), (8, 9, 10, 11), (12, 13, 14, 15)):
+            fk, ks, d = "%s.%d" % (flag, part(bs[0])), lambda k: " ".join("%s.%d" % (k, b) for b in bs), len(bs) * dv(hi(bs[0]) - lo(bs[0]), 0.5)
+            if late(bs[0]):
+                add("v", [(lambda b=b: TS(T[eq][:, b, lo(b):hi(b)], rows(lo(b), hi(b)), key(b), None, A.is_equal)) for b in bs], ks(eq), rkey + " " + kkey, d)
+                xy = [(b, 7 - b % 8, 16 if b < 8 and not within else 15 - b % 8) for b in bs]
                 add("a", [(lambda b=b, x=x, y=y: ACT(T["W" + eq][:, b, :, x:y], T.Wt[:, :, x:y], F.Copy, scale=lfc(flag, b))) for b, x, y in xy],
                     ks("W" + eq), "Wt " + fk, sum(dv(8 * (y - x)) for b, x, y in xy))
             else:
-                add("v", [(lambda b=b: TS(T[eq][:, b, lo(b):256], rows(lo(b), 256), key(b), lfc(flag, b), A.is_equal, A.mult)) for b in bs],
+                add("v", [(lambda b=b: TS(T[eq][:, b, lo(b):hi(b)], rows(lo(b), hi(b)), key(b), lfc(flag, b), A.is_equal, A.mult)) for b in bs],
                     ks(eq), "%s %s %s" % (rkey, kkey, fk), d)
-        for h, bs in ((0, (0, 1, 2)), (0, (4, 5, 6, 7, 3)), (1, (0, 1, 2, 3)), (1, (4, 5, 6, 7)), (1, (8, 9, 10)), (1, (12, 13, 14, 15, 11))):
+        steps = ((1, (8, 12, 13, 14, 15, 9, 10, 11)), (0, (0, 4, 5, 6, 7, 1, 2, 3))) if within else \
+            ((0, (0, 1, 2)), (0, (4, 5, 6, 7, 3)), (1, (0, 1, 2, 3, 4, 5, 6, 7)), (1, (8, 9, 10, 12, 13, 14, 15, 11)))
+        for n_, (h, bs) in enumerate(steps):
             ms = []
             for b in bs:
                 x = max(lo(b), 128 * h)
                 y = 7 - b % 8 if b // 8 == h else 8
-                w = T["W" + eq][:, b, :, y:y + 8] if late else T.Wt[:, :, y:y + 8]
-                ms.append((T[bank][x - 128 * h:128, 384 + 64 * h:448 + 64 * h], T[eq][:, b, x:128 * h + 128], w, b == 0, b == 8 * h + 3))
-            PM(ms, 64, "%s.n%d %s.g" % (bank, h, bank), "Wt " + " ".join("%s.%d" % (eq, b) + " W%s.%d" % (eq, b) * late for b in bs))
-            if bs[-1] != 11 and not (split and bs[-1] == 3 and h == 0):
+                w = T["W" + eq][:, b, :, y:y + 8] if late(b) else T.Wt[:, :, y:y + 8]
+                ms.append((T[bank][x - 128 * h:128, 384 + 64 * h:448 + 64 * h], T[eq][:, b, x:128 * h + 128], w,
+                           b == (8 * h if within else 0), b == 8 * h + 3))
+            if eq in XA and ms[0][3]:
+                ms.insert(1, (T[bank][:, 384 + 64 * h:448 + 64 * h], In, T.thb[:], False, False))
+            PM(ms, 64, "%s.n%d %s.g" % (bank, h, bank), "In thb Wt " + " ".join("%s.%d" % (eq, b) + " W%s.%d" % (eq, b) * late(b) for b in bs))
+            if not split and n_ < len(steps) - 1:
                 continue
-            h0 = h if split else 0
-            V(lambda h=h, h0=h0: TT(T.Xm[:, h0:h + 1, :, :], T[bank][:, 384 + 64 * h0:448 + 64 * h], T.thr[:, 64 * h0:64 * h + 64], A.is_lt),
-              "Xm.%d" % h0, "%s.n%d %s.n%d thr" % (bank, h0, bank, h), 64 * (h + 1 - h0))
+            h0, h = (h, h) if split else (0, 1)
+            if eq in XA:
+                S_(lambda h=h, h0=h0: ACT(T.Xm[:, h0:h + 1, :, :], T[bank][:, 384 + 64 * h0:448 + 64 * h], F.Relu, scale=-1.0),
+                   "Xm.%d" % h0, "%s.n%d %s.n%d" % (bank, h0, bank, h), 64 * (h + 1 - h0))
+            else:
+                V(lambda h=h, h0=h0: TT(T.Xm[:, h0:h + 1, :, :], T[bank][:, 384 + 64 * h0:448 + 64 * h], T.thr[:, 64 * h0:64 * h + 64], A.is_lt),
+                  "Xm.%d" % h0, "%s.n%d %s.n%d thr" % (bank, h0, bank, h), 64 * (h + 1 - h0))
             o = T[bank][:, 256 + 8 * h0:264 + 8 * h]
             PM(([] if spare is None else [(o, Ib, T.sp[:, spare + 8 * h0:spare + 8 * h + 8], True, False)]) +
                [(o, T["Vs" if spare is None else "VsB"][:, 112 - 16 * k:240 - 16 * k], T.Xm[:, h0:h + 1, k, :], k == 0 and spare is None, k == 7)
@@ -285,6 +294,7 @@ def program(T, g, me, nxt, topo):
     ALL = [(0, 16)]
     for t in range(NV):
         now[0] = t
+        EM = EMS[t]
         zi, fi, zo_, fo = "zin%d" % t, "fin%d" % t, "zout%d" % t, "fout%d" % t
         zin, fin, zout, fout = T[zi], T[fi], T[zo_], T[fo]
         PM([(T.b3[:, 0:16], row("Ww", j), zin[:, j:256:16], j == 0, j == 15) for j in R16], 16, "b3.u", "Ww " + zi)
@@ -330,8 +340,6 @@ def program(T, g, me, nxt, topo):
                 for r in range(2) for h in range(2)], 128, out + " b0.g", key + " " + dst)
         AF(T.s16[:], T.su[:], "s16", "sa su", 256, bias=-2048.0, rate=0.5)
         V(lambda: v.transpose(T.ts[:], T.s16[:]), "ts", "s16", 256, 0.5)
-        PM([(T.b0[:, 0:256], Ib, T.ck[:, 0:256], True, False)], 256, "b0.k b0.g", "Ib ck")
-        turn("ts", 0, "W4", False)
 
         def records(part, su, xg, xa, k, bank):
             l0, nl, mode = part
@@ -341,7 +349,7 @@ def program(T, g, me, nxt, topo):
             if mode == "c":
                 banks = (("b6", "b6.x"), ("b7", "b7.x"))
                 if su == "su" and k and PRE:
-                    banks = (("b2", "b2.0 b2.1 b2.2 b2.3 b2.g"), ("b4", "b4.0 b4.1"))
+                    banks = (("b2", "b2.0 b2.1 b2.2 b2.3 b2.4 b2.g"), ("b0", "b0.k b0.n0 b0.n1 b0.w0 b0.w1 b0.g"))
                 S_(lambda: ACT(T[xg][:, lo:hi], T.R[:, 0:4096].indirect(T[su][:, l0:l0 + nl]), F.Copy), gk, "R " + sk(l0, l0 + nl), hi - lo, GA)
                 for y in range(2):
                     bk, key = banks[y]
@@ -355,23 +363,13 @@ def program(T, g, me, nxt, topo):
                         PM([m for o, r in zip(os_, rs_) for m in ((o, Ib, r, True, False), (o, In, zin[:, l0:l0 + nl], False, True))], nl, key,
                            "Ib In %s %s" % (gk, zi))
                     S_(lambda bk=bk, y=y: ACT(T[xa][:, lo + 8 * nl * y:lo + 8 * nl * (y + 1)], T[bk][:, 0:8 * nl], F.Abs, bias=ZO), "%s.%d" % (ak, y), key, 8 * nl)
-                PM([(out, row("Wb", j), T[xa][:, lo + nl * j:lo + nl * j + nl], j == 0, j == 15) for j in R16], nl, "%s.%d" % (bank, k), "Wb %s.0 %s.1" % (ak, ak))
+                PM([(out, row("Wb", j), T[xa][:, lo + nl * j:lo + nl * j + nl], j == 0, j == 15) for j in R16], nl, "%s.%d" % (bank, k) + " b2.g" * (bank == "b2" and "b" in [m for x, n, m in EM]), "Wb %s.0 %s.1" % (ak, ak))
                 return
             zk = " ".join("ze.%d" % z for z in range(8))
-            if mode == "f":
-                rid, pid, _ = topo.addr(aid)
-                m, n = topo.mask(me, aid), len(topo.engines(me, aid))
-                S_(lambda: ACT(T[xg][:, lo:hi], T.R[:, 0:4096].indirect(T[su][:, l0:l0 + nl]), F.Copy), gk, "R " + sk(l0, l0 + nl), hi - lo, GA)
-                tr_ = RemoteDMATransfer(dst_ids=[DstId(rid=rid, pnc=pid)], dma_engine_mask=m, remote_sem=T.sem["ho%d%d" % (t, k)],
-                                        srcs=[T[xg][:, lo:hi], T.ze[:, lo:hi]], dsts=[T[LAND[t]][:, lo:hi]], alu_op=2)
-                i = add("g", [lambda ls=T.sem["hl%d%d" % (t, k)]: g.remote_dma_fused([tr_], local_sem=ls)], "", "%s %s" % (gk, zk), 0.5, "hl%d%d" % (t, k), n)
-                add("n", [], ak, "", TRF, "hb%d%d" % (t, k), len(topo.engines(aid, me)), i)
-                PM([(out, Bn, zin[:, l0:l0 + nl], True, False)] + [(out, row("Wn", j), T[xg][:, lo + j:hi:16], False, False) for j in R16] +
-                   [(out, row("W2", j), T[xa][:, lo + j:hi:16], False, j == 15) for j in R16], nl, "%s.%d" % (bank, k), "Bn Wn W2 %s %s %s" % (zi, gk, ak))
-                return
-            ys = range(l0, l0 + nl, VP)
+            vp = VP if su == "su" else VE
+            ys = range(l0, l0 + nl, vp)
             for y in ys:
-                ye_ = min(y + VP, l0 + nl)
+                ye_ = min(y + vp, l0 + nl)
                 x, xa_ = T[xg][:, 16 * y:16 * ye_], T[xa][:, 16 * y:16 * ye_]
                 V(lambda x=x, y=y, ye_=ye_: TT(x, T.R[:, 0:4096].indirect(T[su][:, y:ye_]), T.ze[:, 16 * y:16 * ye_], A.subtract),
                   "%s.%d" % (gk, y), "R %s %s" % (sk(y, ye_), zk), 16 * (ye_ - y), GA)
@@ -381,23 +379,22 @@ def program(T, g, me, nxt, topo):
                     V(lambda x=x, xa_=xa_: TS(xa_, x, ZO, 0.0, A.add, A.max), "%s.%d" % (ak, y), "%s.%d" % (gk, y), 16 * (ye_ - y), 0.5)
             ks = lambda key: " ".join("%s.%d" % (key, y) for y in ys)
             if mode == "b":
-                PM([(out, row("Wn", j), T[xg][:, lo + j:hi:16], j == 0, False) for j in R16], nl, "%s.%d %s.g" % (bank, k, bank), "Wn " + ks(gk))
+                PM([(out, row("Wn", j), T[xg][:, lo + j:hi:16], j == 0, False) for j in R16] + [(out, Ix, T.zof[:, 0:nl], False, False)] * (su == "su2"),
+                   nl, "%s.%d %s.g" % (bank, k, bank), "Wn Ix zof " + ks(gk))
             PM([(out, row("Wb" if mode == "a" else "W2", j), T[xa][:, lo + j:hi:16], j == 0 and mode == "a", j == 15) for j in R16], nl,
                "%s.%d %s.g" % (bank, k, bank), "Wb W2 " + ks(ak))
 
         for k, part in enumerate(CM):
             records(part, "su", "xg", "xa", k, "b5" if part[2] == "b" else "b1")
+        PM([(T.b0[:, 0:256], Ib, T.ck[:, 0:256], True, False)], 256, "b0.k b0.g", "Ib ck")
+        turn("ts", 0, "W4", False)
         if t == 0:
             V(lambda: TS(T.hc[:], T.hB[:], T.thf[:, 0:1], None, A.add), "h", "hB thf", 4)
-        elif "h" in ONA:
-            S_(lambda: ACT(a0, T.b3[:, 128:129], F.Copy), "a0", "b3.a", 1)
+        else:
+            S_(lambda: ACT(T.accb[:, 16:32], T.b3[:, 112:128], F.Copy, accum_out=a0), "a0", "b3.a", 16)
             S_(lambda: ACT(T.ai[:], a0, F.Copy, bias=-0.484375, scale=0.03125), "ai", "a0", 1)
             S_(lambda: ACT(am, T.ai[:], F.Identity, bias=a0, scale=-32.0), "am", "ai a0", 1)
             S_(lambda t=t: ACT(T.hc[:], T.hT[:, t, :], F.Identity, bias=am), "h", "hT am", 4)
-        else:
-            V(lambda: TS(T.ai[:], T.b3[:, 128:129], 0.03125, -0.484375, A.mult, A.add), "ai", "b3.a", 1)
-            V(lambda: TS(am, T.ai[:], -32.0, T.b3[:, 128:129], A.mult, A.add), "am", "ai b3.a", 1)
-            V(lambda t=t: TS(T.hc[:], T.hB[:], am, T.thf[:, t:t + 1], A.add, A.add), "h", "hB am thf", 4)
         dn, dd = T.T2[:, 0, :], T.T2[:, 1, :]
         for bk in ("b1", "b5"):
             ks = [k for k, part in enumerate(CM) if (part[2] == "b") == (bk == "b5")]
@@ -409,11 +406,17 @@ def program(T, g, me, nxt, topo):
         turn("td", 4, "W4d", True)
         V(lambda: TS(dd, dn, 256.0, -1.0, A.is_ge, A.mult), "dd", DN, 256, 0.5)
         V(lambda: TS(T.T2[:, 2, :], dn, T.hc[:, 2:3], 3.0, A.min, A.mult), "mn", DN + " h", 256, 0.5)
-        PM([(T.b3[:, 144:192], row("Wb", j), T.T2[:, :, j:256:16], j == 0, False) for j in range(15)] + [(T.b3[:, 144:160], Ib, T.k16[:, 0:16], False, False)] +
-           [(T.b3[:, 144:192], row("Wb", 15), T.T2[:, :, 15:256:16], False, True)], 16, "b3.s", "Wb Ib k16 dd mn " + DN)
-        V(lambda: TS(tq, T.b3[:, 160:176], 64.0, T.hc[:, 1:2], A.add, A.mult), "tq", "b3.s h", 16)
-        V(lambda: TT(tq, tq, T.b3[:, 144:160], A.subtract), "tq", "b3.s tq", 16)
-        V(lambda: TT(ps, tq, T.b3[:, 176:192], A.is_ge), "ps.0", "b3.s tq", 16)
+        if S2:
+            PM([(T.b3[:, 144:176], row("Wb", j), T.T2[:, 0:2, j:256:16], j == 0, False) for j in R16] + [(T.b3[:, 144:160], Ib, T.k16[:, 0:16], False, False)] +
+               [(T.b3[:, 144:160], row("Wb", j), T.T2[:, 2, j:256:16], False, j == 15) for j in R16], 16, "b3.s", "Wb Ib k16 dd mn " + DN)
+            V(lambda: TS(tq, T.b3[:, 160:176], 64.0, T.hc[:, 1:2], A.add, A.mult), "tq", "b3.s h", 16)
+            V(lambda: TT(ps, tq, T.b3[:, 144:160], A.is_ge), "ps.0", "b3.s tq", 16)
+        else:
+            PM([(T.b3[:, 144:192], row("Wb", j), T.T2[:, :, j:256:16], j == 0, False) for j in range(15)] + [(T.b3[:, 144:160], Ib, T.k16[:, 0:16], False, False)] +
+               [(T.b3[:, 144:192], row("Wb", 15), T.T2[:, :, 15:256:16], False, True)], 16, "b3.s", "Wb Ib k16 dd mn " + DN)
+            V(lambda: TS(tq, T.b3[:, 160:176], 64.0, T.hc[:, 1:2], A.add, A.mult), "tq", "b3.s h", 16)
+            V(lambda: TT(tq, tq, T.b3[:, 144:160], A.subtract), "tq", "b3.s tq", 16)
+            V(lambda: TT(ps, tq, T.b3[:, 176:192], A.is_ge), "ps.0", "b3.s tq", 16)
         V(lambda: v.tensor_tensor_scan(T.sm[:], T.d0n[:], T.b0[:, 0:256], 0.0, A.add, A.min), "sm", "d0n b0.k", 256)
         add("v", [(lambda r=r: TC(T.li[:, LI.index("kI"), r:16:2], T.sm[:, 128 * r + 15:128 * r + 128:16])) for r in range(2)], "kI", "sm", 2 * dv(8))
         V(lambda: TS(w1, kI, 16, None, A.arith_shift_right), "w1", "kI", 16)
@@ -423,8 +426,13 @@ def program(T, g, me, nxt, topo):
         V(lambda: TT(t3, nh, tr, A.mult), "t3", "nh tr", 16)
         V(lambda: TT(t4, t3, ny, A.max), "t4", "t3 ny", 16)
         AF(zo, t4, "zo", "t4", 16)
-        V(lambda zin=zin: TT(T.xs[:], T.R[:].indirect(zo), zin[:], A.add), "xs", "R Rd zo " + zi, 256, GA)
-        V(lambda zout=zout: TS(zout[:], T.xs[:], 0.5, ZO / 2 - 0.25, A.mult, A.add), zo_, "xs", 256, 0.5)
+        if "xs" in ONA:
+            S_(lambda: ACT(T.xs[:], T.R[:].indirect(zo), F.Copy), "xs", "R Rd zo", 256, GA)
+            PM([(T.b1[:, 0:256], Ib, zin[:], True, False), (T.b1[:, 0:256], Ib, T.xs[:], False, True)], 256, "b1.0 b1.1 b1.2 b1.3 b1.g", "Ib xs " + zi)
+            AF(zout[:], T.b1[:, 0:256], zo_, "b1.0 b1.1 b1.2 b1.3", 256, 0.5, ZO / 2 - 0.25)
+        else:
+            V(lambda zin=zin: TT(T.xs[:], T.R[:].indirect(zo), zin[:], A.add), "xs", "R Rd zo " + zi, 256, GA)
+            V(lambda zout=zout: TS(zout[:], T.xs[:], 0.5, ZO / 2 - 0.25, A.mult, A.add), zo_, "xs", 256, 0.5)
         send("z", zo_, "zin%d" % (t + 1), t)
         S_(lambda: ACT(T.pg[:], T.PT[:].indirect(zo), F.Identity, bias=k3), "pg", "PT PT1 zo k2", 256, GA)
         AF(T.w5h[:], w1, "w5h", "w1", 16, 5.0)
@@ -441,13 +449,19 @@ def program(T, g, me, nxt, topo):
         send("f", fo, "fin%d" % (t + 1), t)
         V(lambda: TT(acc, WB, ps, A.mult), "acc", "b5.w0 ps.0", 16)
         if t < NV - 1:
-            S_(lambda: ACT(T.accb[:], acc, F.Copy, accum_out=af), "accb af", "acc", 16)
-            PM([(T.b3[:, 128:129], one, af, True, True)], 256, "b3.a", "one af")
+            PM([(T.b3[:, 112:128], T.on[:, 0:128], acc, True, True)], 16, "b3.a", "on acc")
         for k, part in enumerate(EM):
             records(part, "su2", "eg", "ea", k, "b2")
-        S_(lambda: ACT(T.mM[:], T.b0[:, 0:256], F.Relu, bias=-64.0 * 16000000.0, scale=64.0), "mM", "b0.k", 256)
-        V(lambda: TT(T.kr[:], T.b0[:, 0:256], T.mM[:], A.subtract), "kr", "b0.k mM", 256)
-        V(lambda: v.tensor_tensor_scan(T.sx[:], T.d0x[:], T.kr[:], 0.0, A.add, A.max), "sx", "d0x kr", 256)
+        if KMAX == "p":
+            V(lambda: v.transpose(T.tx[:], dd), "tx", "dd", 256, 0.5)
+            PM([(T.b0[:, 256:512], Ib, T.ck[:, 256:512], True, False)], 256, "b0.x b0.w0 b0.w1 b0.n0 b0.n1 b0.g", "Ib ck2")
+            for dst, k0, key in (("ts", 0, "W4"), ("td", 4, "W4d"), ("tx", 8, "W4x")):
+                turn(dst, k0, key, k0 == 8, 256, "b0.x")
+            V(lambda: v.tensor_tensor_scan(T.sx[:], T.d0x[:], T.b0[:, 256:512], 0.0, A.add, A.max), "sx", "d0x b0.x b0.w0 b0.w1 b0.n0 b0.n1", 256)
+        else:
+            S_(lambda: ACT(T.mM[:], T.b0[:, 0:256], F.Relu, bias=-64.0 * 16000000.0, scale=64.0), "mM", "b0.k", 256)
+            V(lambda: TT(T.kr[:], T.b0[:, 0:256], T.mM[:], A.subtract), "kr", "b0.k mM", 256)
+            V(lambda: v.tensor_tensor_scan(T.sx[:], T.d0x[:], T.kr[:], 0.0, A.add, A.max), "sx", "d0x kr", 256)
         add("v", [(lambda r=r: TC(T.li[:, LI.index("fI"), r:16:2], T.sx[:, 128 * r + 15:128 * r + 128:16])) for r in range(2)], "fI", "sx", 2 * dv(8))
         V(lambda: TS(foe, fI, 2.0 ** -16, T.hc[:, 3:4], A.mult, A.is_ge), "foe", "fI h", 16)
         V(lambda: TS(vs, fI, 4095, None, A.bitwise_and), "vs", "fI", 16)
@@ -460,10 +474,11 @@ def program(T, g, me, nxt, topo):
         V(lambda: TT(flg, foe, acc, A.mult), "flg.0", "foe acc", 16)
         V(lambda: TT(fv, flg, vrm, A.mult), "fv", "flg.0 vrm", 16)
         V(lambda: TT(fv, fv, T.sp[:, 0:16], A.add), "fv", "fv sp", 16)
-        first("EQv", "b5", lambda x, y: T.vrow[:, x:y], "vrow", lambda b: lfc("vk", b), "vk", "flg", ALL, 0)
+        first("EQv", "b5", lambda x, y: T.vrow[:, x:y], "vrow", lambda b: lfc("vk", b), "vk", "flg", ALL, 0, True)
         V(lambda: TT(dl, WB, fv, A.max), "dl", "b5.w0 fv", 16)
         AF(dlu, dl, "dlu", "dl", 16, bias=2304.0)
-        V(lambda: TC(T.R[:].indirect(dlu), T.s64[:]), "R Rd", "dlu s64", 256, SC)
+        for x in (0, 8):
+            V(lambda x=x: TC(T.R[:].indirect(T.lu[:, LU.index("dlu"), x:x + 8]), T.s64[:, 0:128]), "R Rd", "dlu s64", 128, SC)
         V(lambda: TT(T.la[:, 0:16], acc, T.RM[:, 0:16], A.mult), "la0", "acc RM", 16)
         V(lambda: TT(T.la[:, 16:32], acc, T.RM[:, 16:32], A.mult), "la1", "acc RM", 16)
         V(lambda: TT(T.la[:], T.la[:], T.T2c[:], A.add), "la0 la1", "la0 la1 T2c", 32)
@@ -472,35 +487,40 @@ def program(T, g, me, nxt, topo):
         spread("b4", 256, fo, 16, "b4.1")
         S_(lambda: ACT(T.phr[:], T.b4[:, 256:512], F.Identity, bias=k2, scale=lfc("I16", 0)), "phr", "b4.1 k2", 256)
         if OFF:
-            S_(lambda: ACT(T.PT[:].indirect(T.lau[:, 0:16]), T.phr[:], F.Silu), "PT PT1", "lau phr", 256, SC if t else SC + 6)
+            S_(lambda: ACT(T.PT[:].indirect(T.lau[:, 0:16]), T.phr[:], F.Silu), "PT PT1", "lau phr", 256, SC)
         else:
             V(lambda: TC(T.PT[:].indirect(T.lau[:, 0:16]), T.phr[:]), "PT PT1", "lau phr", 256, SC)
         Q = T.b1[:, 256:512]
         own = (Q, Ib, T.vrow[:, 256:512], False, False)
-        PM([(Q, I6, T.on[:, 0:256], True, False), (Q, Y1, dd, False, False), own[:4] + (True,)], 256, "b1.q b1.g", "I6 on Y1 dd Ib nrow")
-        S_(lambda: ACT(T.n1[:], Q, F.Copy, bias=-8192.0, scale=-1.0), "n1", "b1.q", 256)
-        V(lambda: TT(T.a1[:], Q, T.sF[:], A.min), "a1", "b1.q sF", 256)
+        PM([(Q, I6, T.on[:, 0:256], True, False), (Q, Y1, dd, False, False), own[:4] + (True,)], 256, "b1.q0 b1.q1 b1.g", "I6 on Y1 dd Ib nrow")
+        S_(lambda: ACT(T.n1[:], Q, F.Copy, bias=-8192.0, scale=-1.0), "n1", "b1.q0 b1.q1", 256)
+        V(lambda: TT(T.a1[:], Q, T.sF[:], A.min), "a1", "b1.q0 b1.q1 sF", 256)
         V(lambda: TT(T.C[:].indirect(T.lau[:, 16:32]), T.a1[:], T.n1[:], A.max), "C", "lau a1 n1", 256, SC)
         for k, (x, y) in enumerate(EP):
             dk = " ".join("b2.%d" % z for z, (l0, nl, m) in enumerate(EM) if l0 < 16 * y and 16 * x < l0 + nl)
             S_(lambda x=x, y=y: ACT(T.sup[:, 16 * x:16 * y], T.b2[:, 16 * x:16 * y], F.Relu, bias=T.hc[:, 0:1], scale=-1.0), "sup.%d" % k, dk + " h", 16 * (y - x))
             PM([(T.b3[:, 80 + x:80 + y], row("Wb", j), T.sup[:, 16 * x + j:16 * y:16], j == 0, j == 15) for j in R16], 16, "b3.c%d" % k, "Wb sup.%d" % k)
-            V(lambda x=x, y=y: TT(lfc("cnd", x, y), lfc("acc", x, y), T.b3[:, 80 + x:80 + y], A.is_gt), "cnd.%d" % k, "acc b3.c%d" % k, 16)
-        S_(lambda: ACT(T.sg2[:], T.b2[:, 0:256], F.Sign, bias=-511.5), "sg2", " ".join("b2.%d" % z for z in range(len(EM))), 256)
-        PM([(Q, Y2c, T.on[:, 0:256], True, False), own], 256, "b1.q b1.g", "Y2c on Ib nrow")
-        PM([(Q, Y2, T.sg2[:], False, True)], 256, "b1.q b1.g", "Y2 sg2")
-        S_(lambda: ACT(T.n2[:], Q, F.Copy, bias=-8192.0, scale=-1.0), "n2", "b1.q", 256)
+            V(lambda x=x, y=y: TT(lfc("cnd", x, y), T.accb[:, x:y], T.b3[:, 80 + x:80 + y], A.is_gt), "cnd.%d" % k, "acc b3.c%d" % k, 16)
         S_(lambda: ACT(T.sF2[:], T.C[:, 0:1024].indirect(eu), F.Copy), "sF2", "C eu", 256, GA)
-        V(lambda: TT(T.a2[:], Q, T.sF2[:], A.min), "a2", "b1.q sF2", 256)
-        first("EQe", "b0", lambda x, y: T.rows[:, 256 + x:256 + y], "rows", lambda b: T.kf[:, 16 + b:17 + b], "kf", "cnd", EP, 16, SPLIT)
-        for h, (x, y) in enumerate(((0, 8), (8, 16)) if SPLIT else ALL):
+        first("EQe", "b0", lambda x, y: T.rows[:, 256 + x:256 + y], "rows", lambda b: T.kf[:, 16 + b:17 + b], "kf", "cnd", EP, 16, True, SPLIT)
+        for h, (x, y) in ((1, (8, 16)), (0, (0, 8))) if SPLIT else ((0, (0, 16)),):
+            ln, Qh = slice(16 * x, 16 * y), T.b1[:, 256 + 16 * x:256 + 16 * y]
+            S_(lambda ln=ln: ACT(T.sg2[:, ln], T.b2[:, ln], F.Sign, bias=-511.5), "sg2.%d" % h,
+               " ".join("b2.%d" % z for z, (l0, nl, m) in enumerate(EM) if l0 < 16 * y and 16 * x < l0 + nl), 16 * (y - x))
+            qk = "b1.q%d" % h if SPLIT else "b1.q0 b1.q1"
+            PM([(Qh, Y2c, T.on[:, ln], True, False), (Qh, Ib, T.vrow[:, 256 + 16 * x:256 + 16 * y], False, False), (Qh, Y2, T.sg2[:, ln], False, True)],
+               16 * (y - x), qk + " b1.g", "Y2c Y2 on Ib nrow sg2.%d" % h)
+            S_(lambda ln=ln, Qh=Qh: ACT(T.n2[:, ln], Qh, F.Copy, bias=-8192.0, scale=-1.0), "n2.%d" % h, qk, 16 * (y - x))
+            V(lambda ln=ln, Qh=Qh: TT(T.a2[:, ln], Qh, T.sF2[:, ln], A.min), "a2.%d" % h, qk + " sF2", 16 * (y - x))
             c_, l_, u_ = lfc("cr", x, y), lfc("l2", x, y), T.lu[:, LU.index("l2u"), x:y]
             V(lambda x=x, y=y, c_=c_: TT(c_, lfc("cnd", x, y), T.RM[:, 32 + x:32 + y], A.mult), "cr.%d" % h,
               "RM " + " ".join("cnd.%d" % k for k, (x1, y1) in enumerate(EP) if x1 < y and x < y1), 16)
             V(lambda x=x, y=y, c_=c_: TT(c_, c_, lfc("tc", x, y), A.add), "cr.%d" % h, "cr.%d tc" % h, 16)
             V(lambda x=x, y=y, c_=c_, l_=l_: TT(l_, T.b0[:, 256 + x:256 + y], c_, A.max), "l2.%d" % h, "b0.w%d cr.%d" % (h, h), 16)
             AF(u_, l_, "l2u.%d" % h, "l2.%d" % h, 16)
-            V(lambda x=x, y=y, u_=u_: TT(T.C[:].indirect(u_), T.a2[:, 16 * x:16 * y], T.n2[:, 16 * x:16 * y], A.max), "C", "l2u.%d a2 n2" % h, 16 * (y - x), SC)
+            for x in range(y - 8, x - 8, -8):
+                V(lambda x=x: TT(T.C[:].indirect(T.lu[:, LU.index("l2u"), x:x + 8]), T.a2[:, 16 * x:16 * x + 128], T.n2[:, 16 * x:16 * x + 128], A.max),
+                  "C", "l2u.@ a2.@ n2.@".replace("@", str(h)), 128, SC)
     now[0] = -2
     i = D("yrec", T.yrec[:], T.R[:, 0:4096], "", "R", 7.0)
     add("n", [], "", "", 9.5, None, 0, i)
@@ -542,6 +562,17 @@ def schedule(ops):
             for x, lag in before[i]:
                 if at[x] + lag > t:
                     t = at[x] + lag
+            if len(held) == 1:
+                line = lines[me]
+                m = k = len(line)
+                while k and line[k - 1][1] > t + 1e-9:
+                    k -= 1
+                while k < m and line[k][0] < t + d:
+                    t = line[k][1]
+                    k += 1
+                line.insert(k, (t, t + occ[i], me))
+                at[i] = t
+                continue
             moved = True
             while moved:
                 moved = False
@@ -585,9 +616,9 @@ def schedule(ops):
         return at, why, final, end
 
     def tighten(at):
-        back = place(sorted(range(n), key=lambda i: (-at[i] - occ[i], -i)), bwd, tail)
-        at = place(sorted(range(n), key=lambda i: (-back[i] - occ[i], i)), fwd, zero)
-        order = sorted(range(n), key=lambda i: (at[i], i))
+        back = place(np.argsort(np.add(at, occ), kind="stable")[::-1].tolist(), bwd, tail)
+        at = place(np.argsort(-np.add(back, occ), kind="stable").tolist(), fwd, zero)
+        order = np.argsort(at, kind="stable").tolist()
         at, why, final, end = run(order)
         return end + 0.1 * sum(at) / n, order, why, final, end
 
@@ -625,7 +656,14 @@ def schedule(ops):
             todo = [(x, i)]
             if rng.random() < 0.8 and min(ta, tb) >= 0:
                 todo = [(same[a, ta + d], same[b, tb + d]) for d in range(-min(ta, tb), NV) if (a, ta + d) in same and (b, tb + d) in same]
-            if any([swap(order, x, i, up) for x, i in todo]):
+            if k % SHARE == SHARE - 1:
+                at, m = run(order)[0], int(rng.integers(NV))
+                t0 = [at[same["su", t]] for t in range(NV)]
+                rank = [t0[t] + at[same[a, m]] - t0[m] if t >= 0 and (a, m) in same else at[i] for i, (a, t) in enumerate(o["tag"] for o in ops)]
+                for i in range(n):
+                    rank[i] = max([rank[i]] + [rank[x] + 1e-6 for x, lag in fwd[i]])
+                todo, order = [], sorted(range(n), key=lambda i: rank[i])
+            if not todo or any([swap(order, x, i, up) for x, i in todo]):
                 new = tighten(run(order)[0])
                 if new[0] <= now[0] + HEAT * (1 - k / ROUNDS) * rng.random():
                     now = new
@@ -644,16 +682,6 @@ def schedule(ops):
 def rank_program(g, core, T, topo):
     rank = T.rank_of(core)
     if rank is None:
-        for c in T.cores:
-            if helper(c, T, topo) == core:
-                rid, pid, _ = topo.addr(c)
-                parts = [(t, k, x, n) for t in range(NV) for k, (x, n, m) in enumerate(EM) if m == "f"]
-                for t, k, x, n in parts:
-                    g.wait_ge(T.sem["ho%d%d" % (t, k)], len(topo.engines(c, core)))
-                    g.remote_dma(T.ea[:, 16 * x:16 * (x + n)], T[LAND[t]][:, 16 * x:16 * (x + n)], T.sem["hb%d%d" % (t, k)], T.sem["hk%d%d" % (t, k)],
-                                 pid, rid, topo.mask(core, c))
-                for t, k, x, n in parts:
-                    g.wait_ge(T.sem["hk%d%d" % (t, k)], len(topo.engines(core, c)))
         return
     nxt = T.cores[(rank + 1) % len(T.cores)]
     ops = program(T, g, core, nxt, topo)
@@ -680,6 +708,8 @@ def rank_program(g, core, T, topo):
                         seen[q][k] = y
         for f in o["f"]:
             ins = f()
+            if f is not o["f"][-1]:
+                continue
             if o["sem"] is None:
                 ins.then_inc(T.sem["q" + q], 1)
                 cnt[q] += 1

import numpy as np
from concourse.mybir import AluOpType as A, AxisListType, ActivationFunctionType as F

NV = 4
CM = [(0, 64, "c"), (64, 64, "c"), (128, 64, "b"), (192, 64, "b")]
EMS = [[(192, 64, "a"), (128, 64, "c"), (0, 64, "c"), (64, 64, "c")]] * NV
VP, VE = 64, 32
EP = [(0, 8), (8, 16)]
ZE0, ZE = "va" * 4, "ga" * 4
EVAC = "a"
PTG = 4352
TRN = 4.2
KMAX, SPLIT, SU = "v", True, 8
LATE, XA, S2 = ("EQe0", "EQe1"), ("EQe", "EQv"), False
ONA = "xr u32 u2 uh h C sa l2u dlu lau fout".split()
ROUNDS, HEAT, SEED = 14000, 1.0, 2
ORDER = []
CY, PE, WAKE = 0.92e-3, 0.49e-3, 0.25
GA, SC = 1.56, 3.8
BIG = 16384.0
PRE, SHARE = True, 40
ZO = 192.0
OFF = 64.0

B, H, F4, I4, U2 = "bfloat16", "float16", "float32", "int32", "uint16"
SHAPES = {
    B: "R:4352 xg:4096 xa:4096 eg:4096 ea:4096 sup:256 mM:256 sg2:256 xs:256 zof:256 ck:512 d0n:256 d0x:256 thb:64 s64:256 on:512 accb:32 k16:32 "
       "Wb:144 W2:144 Wn:144 W3:144 Ww:144 Vs:240 VsB:240",
    H: "sp:32 rows:512 vrow:512 s16:256 pg:256 phh:256 thh:4 L3:32 L2:32 uh:16 w5h:16",
    F4: "C:1280 PT:4352 posf:256 sF:256 sF2:256 a1:256 a2:256 n1:256 n2:256 phr:256 thf:4 hc:4 hB:4 kr:256 Iw:160 thr:128 "
        "B8a:8 B8:8 g16:8 g16b:8 K3:48 rc:2 RM:48 kf:32 T2c:32 la:32 col:16",
    I4: "Ci:1024 pos:256 phl:256 thl:4 wl:1 ai:1 CI:48",
    U2: "su:256 su2:256 lau:32",
}
LF = "u32 nh t3 t4 tq ps ph pdh rr acc dl l2 foe flg vk fv cnd cr vrm jr I16 b256 i16 iL tr tc pw pwb hf".split()
LI = "ui u2 xq xr ye kI ny w1 fI vs fr fr2 yf".split()
LU = "cu eu zo dlu l2u".split()
MB = "Ib In I5 I4n I6 Y1 Y2 Y2c Zb Ix".split()
MF = "one Bba Bta Bt Utf Ulf".split()
SCRATCH = {}
for _d, _l in SHAPES.items():
    for _x in _l.split():
        SCRATCH[_x.split(":")[0]] = ("sbuf", [128, int(_x.split(":")[1])], _d)
for _x, _s, _d in (("EQ", [16, 256], B), ("EQe", [16, 256], B), ("EQv", [16, 256], B), ("ze", [4096], B),
                   ("WEQ", [16, 8, 16], B), ("WEQe", [16, 8, 16], B), ("WEQv", [16, 8, 16], B), ("Sp", [16, 128], B), ("hT", [NV, 4], F4),
                   ("Bf", [8, 16], F4), ("Wt", [8, 16], B), ("Xm", [2, 8, 8], B), ("W4", [12, 128], B), ("T2", [3, 256], H),
                   ("ts", [8, 32], H), ("td", [8, 32], H), ("tx", [8, 32], H), ("sm", [256], F4), ("sx", [256], F4),
                   ("lf", [len(LF), 16], F4), ("li", [len(LI), 16], I4), ("lu", [len(LU), 16], U2), ("mb", [len(MB), 128], B),
                   ("mf", [len(MF), 128], F4)):
    SCRATCH[_x] = ("sbuf", [128] + _s, _d)
for _t in range(NV + 1):
    SCRATCH["zin%d" % _t] = ("sbuf", [128, 256], B)
    SCRATCH["fin%d" % _t] = ("sbuf", [128, 16], H)
for _t in range(NV):
    SCRATCH["zout%d" % _t] = ("sbuf", [128, 256], B)
    SCRATCH["fout%d" % _t] = ("sbuf", [128, 16], H)
for _b in range(8):
    SCRATCH["b%d" % _b] = ("psum", [128, 512], F4)
DMAS = ["rec", "cel", "wt", "pat", "phi", "th", "po", "pt", "pb", "yrec", "ycel", "ypo", "ypat", "yphi"]
SEMAPHORES = ["qv", "qa", "qp", "qg"] + ["d" + n for n in DMAS] + ["%s%d" % (k, t) for k in ("zr", "zl", "fr", "fl") for t in range(NV)]


def dv(n, rate=1.0):
    return 0.055 + n * rate * CY if rate > 1.2 else max(64, n * rate) * CY + 0.015


def program(T, g, me, nxt, topo):
    v, a, p, s = g.vector, g.scalar, g.tensor, g.sync
    ops = []
    last, tags, now = {}, set(), [-1]

    def add(q, fns, w, r, d, sem=None, val=0, net=None):
        rs, ws = r.split(), w.split()
        o = {"q": q, "f": fns, "d": d, "sem": sem, "val": val, "i": len(ops), "wait": set(), "ord": set(), "net": net,
             "bank": sorted(set(k[:2] for k in rs + ws if k[0] == "b" and k[2:3] == "."))}
        name = "".join(c for c in w if c != str(now[0]) and c != str(now[0] + 1)) if "in" in w or "out" in w else w or "send " + r[:1]
        while (name, now[0]) in tags:
            name += "+"
        o["tag"] = (name, now[0])
        tags.add(o["tag"])
        for key in sorted(set(rs + ws)):
            L = last.setdefault(key, [None, []])
            if key in rs and L[0] is not None:
                o["wait"].add(L[0])
            if key in ws:
                for x in ([L[0]] if L[0] is not None else []) + L[1]:
                    o["ord" if ops[x]["q"] == q == "p" else "wait"].add(x)
                last[key] = [o["i"], []]
            else:
                L[1].append(o["i"])
        o["ord"] -= o["wait"]
        ops.append(o)
        return o["i"]

    def V(fn, w, r, n, rate=1.0):
        return add("v", [fn], w, r, dv(n, rate))

    def S_(fn, w, r, n, rate=1.0):
        return add("a", [fn], w, r, dv(n, rate))

    def AF(out, in_, w, r, n, scale=1.0, bias=0.0, rate=1.0):
        if w.split(".")[0].rstrip("0123") in ONA or w in ONA:
            return S_(lambda: ACT(out, in_, F.Copy, bias=bias, scale=scale), w, r, n, max(rate, 1.0))
        if scale == 1.0:
            return V((lambda: TS(out, in_, bias, None, A.add)) if bias else (lambda: TC(out, in_)), w, r, n, rate)
        return V(lambda: TS(out, in_, scale, bias, A.mult, A.add), w, r, n, rate)

    def G(fn, w, r, n):
        return add("g", [fn], w, r, 0.17 + 2 * n * CY)

    def PM(args, n, w, r):
        return add("p", [(lambda x=x: p.matmul(*x)) for x in args], w, r, len(args) * max(64, n) * PE)

    def D(name, out, in_, w, r, d, q="s"):
        return add(q, [lambda: (s if q == "s" else a).dma_start(out, in_)], w, r, d, "d" + name, 16)

    TS, TT, TC, MS, ACT = v.tensor_scalar, v.tensor_tensor, v.tensor_copy, v.memset, a.activation
    RED = lambda out, in_: v.tensor_reduce(out, in_, AxisListType.X, A.add)
    R16 = range(16)
    (u32, nh, t3, t4, tq, ps, ph, pdh, rr, acc, dl, l2, foe, flg, vk, fv, cnd, cr, vrm, jr, I16, b256, i16, iL, tr, tc, pw, pwb,
     hf) = [T.lf[:, k, :] for k in range(len(LF))]
    ui, u2, xq, xr, ye, kI, ny, w1, fI, vs, fr, fr2, yf = [T.li[:, k, :] for k in range(len(LI))]
    cu, eu, zo, dlu, l2u = [T.lu[:, k, :] for k in range(len(LU))]
    Ib, In, I5, I4n, I6, Y1, Y2, Y2c, Zb, Ix = [T.mb[:, k, :] for k in range(len(MB))]
    one, Bba, Bta, Bt, Utf, Ulf = [T.mf[:, k, :] for k in range(len(MF))]
    pc, gs, jc, j16, p2, p3, wf, af, am, k2, a0, k3, ws = [T.col[:, k:k + 1] for k in range(13)]
    lfc = lambda name, lo, hi=None: T.lf[:, LF.index(name), lo:hi or lo + 1]
    row = lambda name, j: T[name][:, 15 - j:143 - j]
    idf, acc = T.Iw[:, 16:144], T.accb[:, 0:16]

    def evac(out, in_, w, r, n, bias=0.0):
        if EVAC == "a":
            return S_(lambda: ACT(out, in_, F.Copy, bias=bias), w, r, n)
        return V(lambda: TS(out, in_, bias, None, A.add), w, r, n)

    def spread(bank, off, src, n, key):
        PM([(T[bank][:, off + j:off + 16 * n:16], T.Sp[:, j, :], T[src][:, 0:n], True, True) for j in R16], n, key, "Sp " + src)

    V(lambda: MS(T.phl[:], 2048), "phl", "", 256)
    V(lambda: MS(T.thl[:], 0), "thl", "", 4)
    D("rec", T.R[:, 0:4096], T.rec[:], "R", "", 7.0, "a")
    D("pat", T.xs[:], T.pat[:], "xs", "", 2.0)
    V(lambda: TS(T.zin0[:], T.xs[:], ZO, None, A.add), "zin0", "xs", 256, 0.5)
    V(lambda: MS(T.zof[:], -ZO), "zof", "", 256, 0.5)
    V(lambda: MS(Zb, 0.0), "Zb", "", 128, 0.5)
    D("wt", T.wl[:], T.wt[:], "wl", "", 2.0)
    D("phi", T.phl[0:128:16, :], T.phi[:], "phl", "", 2.0)
    D("cel", T.Ci[:], T.cel[:], "Ci", "", 4.0)
    D("th", T.thl[0:128:16, :], T.th[:], "thl", "", 2.0)
    D("po", T.pos[:], T.po[:], "pos", "R", 2.5)
    iota = lambda out, pat, base=0, cm=0: g.iota(out, pat, base, cm, allow_small_or_imprecise_dtypes=True)
    sel = lambda out, in_, pat, op, base, cm: g.affine_select(out, in_, pat, op, 0.0, base, cm)
    V(lambda: MS(one, 1.0), "one", "", 128)
    V(lambda: MS(T.Iw[:], 1.0), "Iw", "", 160)
    G(lambda: sel(T.B8a[:], T.mf[:, 0, 0:8], [[-16, 8]], A.is_ge, 0, 1), "B8a", "one", 8)
    G(lambda: sel(T.B8[:], T.B8a[:], [[16, 8]], A.is_ge, 15, -1), "B8", "B8a", 8)
    G(lambda: iota(T.g16[:], [[16, 8]]), "g16", "", 8)
    G(lambda: iota(pc, [[0, 1]], 0, 1), "pc", "", 1)
    G(lambda: iota(jr, [[1, 16]]), "jr", "", 16)
    G(lambda: iota(b256, [[256, 16]]), "b256", "", 16)
    G(lambda: sel(T.Iw[:], T.Iw[:], [[-1, 160]], A.is_equal, 16, 1), "Iw", "Iw", 160)
    G(lambda: sel(Bba, one, [[-16, 8], [0, 16]], A.is_ge, 0, 1), "Bba", "one", 128)
    G(lambda: sel(T.Bf[:], Bba, [[16, 8], [0, 16]], A.is_ge, 15, -1), "Bf", "Bba", 128)
    G(lambda: sel(Bta, one, [[0, 16], [-16, 8]], A.is_ge, 0, 1), "Bta", "one", 128)
    G(lambda: sel(Bt, Bta, [[0, 16], [16, 8]], A.is_ge, 15, -1), "Bt", "Bta", 128)
    G(lambda: sel(Utf, T.Bf[:], [[1, 128]], A.is_gt, 0, -1), "Utf", "Bf", 128)
    G(lambda: sel(Ulf, T.Bf[:], [[-1, 128]], A.is_gt, 0, 1), "Ulf", "Bf", 128)
    G(lambda: iota(T.ck[:, 0:256], [[0, 16], [4096, 16]], 2048), "ck", "", 256)
    G(lambda: iota(T.PT[:, 0:PTG], [[0, PTG]]), "PT", "B8 Iw Bf Bt Utf Ulf ck jr pc g16 b256", PTG)
    if PTG < 4352:
        V(lambda: MS(T.PT[:, PTG:4352], 0.0), "PT1", "", 4352 - PTG)
    V(lambda: MS(T.Wb[:], 0.0), "Wb", "", 144, 0.5)
    V(lambda: TC(T.Wb[:, 15:128:16], T.B8[:]), "Wb", "B8", 8)
    V(lambda: TC(wf, T.wl[:]), "wf", "wl", 1)
    for name, x in (("Ww", wf), ("W2", 2.0), ("Wn", -1.0)):
        V(lambda name=name, x=x: TS(T[name][:], T.Wb[:], x, None, A.mult), name, "Wb wf" if name == "Ww" else "Wb", 144, 0.5)
    V(lambda: MS(T.C[:, 1024:1280], 0.0), "C", "", 256)
    AF(T.C[:, 0:1024], T.Ci[:], "C", "Ci", 1024)
    V(lambda: TT(T.g16b[:], T.g16[:], T.B8[:], A.mult), "g16b", "g16 B8", 8)
    V(lambda: RED(gs, T.g16b[:]), "gs", "g16b", 8)
    V(lambda: TT(jc, pc, gs, A.subtract), "jc", "pc gs", 1)
    V(lambda: TS(I16, jr, jc, None, A.is_equal), "I16", "jr jc", 16)
    V(lambda: TS(k2, lfc("I16", 0), 2048.0 + OFF, None, A.mult), "k2", "I16", 1)
    V(lambda: TS(k3, lfc("I16", 0), -2048.0 - OFF, None, A.mult), "k2", "I16", 1)
    V(lambda: TS(j16, jc, 16.0, None, A.mult), "j16", "jc", 1)
    V(lambda: TS(i16, b256, j16, None, A.add), "i16", "b256 j16", 16)
    V(lambda: TS(tr, i16, 0.0625, 4096.0, A.mult, A.add), "tr", "i16", 16)
    V(lambda: TS(tc, i16, 0.0625, 1024.0, A.mult, A.add), "tc", "i16", 16)
    V(lambda: TS(iL, i16, -1.0, 2048.0, A.mult, A.add), "iL", "i16", 16)
    add("v", [lambda: TT(T.K3[:, 0:16], tr, i16, A.subtract), lambda: TC(T.K3[:, 16:32], tc), lambda: TC(T.K3[:, 32:48], tc),
              lambda: TC(T.T2c[:, 0:16], tr), lambda: TC(T.T2c[:, 16:32], tc)], "K3 T2c", "i16 tr tc", 5 * dv(16))
    add("v", [(lambda k=k, y=y: MS(T.hB[:, k:k + 1], y)) for k, y in enumerate((0.0, -512.0, -256.0, -256.0 if KMAX == "p" else -255.0625))], "hB", "", 4 * dv(1))
    add("a", [(lambda j=j: ACT(T.Sp[:, j, :], T.Bf[:], F.Copy, scale=lfc("I16", j))) for j in R16], "Sp", "Bf I16", 16 * dv(128))
    V(lambda: RED(T.rc[:, 0:1], T.B8[:, 0:8:2]), "rc", "B8", 4)
    V(lambda: RED(T.rc[:, 1:2], T.B8[:, 1:8:2]), "rc", "B8", 4)
    add("a", [(lambda k=k, x=x, r=r: ACT(T.W4[:, k, :], T.Iw[:, x:x + 128], F.Copy, scale=T.rc[:, r:r + 1]))
              for k, (x, r) in enumerate(((16, 0), (0, 0), (32, 1), (16, 1)))], "W4", "Iw rc", 4 * dv(128))
    V(lambda: TS(T.W4[:, 4:8, :], T.W4[:, 0:4, :], 65536.0, None, A.mult), "W4d", "W4", 512, 0.5)
    if KMAX == "p":
        V(lambda: TS(T.W4[:, 8:12, :], T.W4[:, 0:4, :], 67108864.0, None, A.mult), "W4x", "W4", 512, 0.5)
        V(lambda: TS(T.ck[:, 256:512], T.ck[:, 0:256], -1.0, 65536.0, A.mult, A.add), "ck2", "ck", 256, 0.5)
    for m, name, x in ((Ib, "Ib", 1.0), (In, "In", -1.0), (I5, "I5", 5.0), (I4n, "I4n", -4.0), (Ix, "Ix", 16.0)):
        S_(lambda m=m, x=x: ACT(m, idf, F.Copy, scale=x), name, "Iw", 128)
    add("a", [lambda: ACT(I6, idf, F.Silu, scale=6144.0)], "I6", "Iw", 1.45)
    V(lambda: MS(T.d0n[:], 0.0), "d0n", "", 256, 0.5)
    V(lambda: MS(T.d0n[:, 0:256:16], 134217728.0), "d0n", "", 16)
    V(lambda: MS(T.d0x[:], 0.0 if KMAX == "p" else 8192.0), "d0x", "", 256, 0.5)
    V(lambda: MS(T.d0x[:, 0:256:16], -268435456.0), "d0x", "", 16)
    V(lambda: MS(hf, 0.5), "hf", "", 16)
    V(lambda: v.tensor_tensor_scan(pw, hf, hf, 65536.0, A.mult, A.max), "pw", "hf", 16)
    V(lambda: TT(pwb, pw, I16, A.mult), "pwb", "pw I16", 16)
    V(lambda: RED(p2, pwb), "p2", "pwb", 16)
    V(lambda: TS(p3, p2, 2.0, 1.0, A.mult, A.add), "p3", "p2", 1)
    V(lambda: TS(T.thr[:], Bt, p3, -1.0, A.mult, A.add), "thr", "Bt p3", 128)
    if XA:
        S_(lambda: ACT(T.thb[:], T.thr[:, 0:64], F.Copy), "thb", "thr", 64)
    V(lambda: MS(T.Wt[:, :, 0:7], 0.0), "Wt", "", 56, 0.5)
    V(lambda: TS(T.Wt[:, :, 7], T.B8[:], p2, None, A.mult), "Wt", "B8 p2", 8)
    V(lambda: TS(T.Wt[:, :, 8:16], T.Bf[:, :, 0:8], 65536.0, None, A.mult), "Wt", "Bf", 64)
    V(lambda: MS(T.Vs[:], 0.0), "Vs", "", 240, 0.5)
    V(lambda: TC(T.Vs[:, 112:128], I16), "Vs", "I16", 16)
    V(lambda: TS(T.VsB[:], T.Vs[:], -8192.0, None, A.mult), "VsB", "Vs", 240, 0.5)
    V(lambda: TS(T.sp[:, 0:16], tr, -2304.0, None, A.add), "sp", "tr", 16)
    V(lambda: TC(T.sp[:, 16:32], tc), "sp", "tc", 16)
    V(lambda: MS(T.s64[:], 64.0), "s64", "", 256, 0.5)
    V(lambda: MS(T.on[:], 1.0), "on", "", 512, 0.5)
    PM([(T.b3[:, 136:137], row("Ww", j), T.zof[:, 0:1], j == 0, j == 15) for j in R16], 1, "b3.ws", "Ww zof")
    V(lambda: TC(ws, T.b3[:, 136:137]), "ws", "b3.ws", 1)
    add("v", [lambda: MS(T.k16[:, 0:16], -16384.0), lambda: MS(T.k16[:, 16:32], 1280.0)], "k16", "", 2 * dv(16))
    V(lambda: TT(Utf, idf, Utf, A.subtract), "Utf", "Iw Utf", 128, 2)
    V(lambda: TT(Ulf, idf, Ulf, A.subtract), "Ulf", "Iw Ulf", 128, 2)
    for m, name, src, key, x in ((Y1, "Y1", Utf, "Utf", BIG), (Y2, "Y2", Ulf, "Ulf", -BIG / 2)):
        S_(lambda m=m, src=src, x=x: ACT(m, src, F.Copy, scale=x), name, key, 128)
    V(lambda: TT(Y2c, Y2, I6, A.add), "Y2c", "Y2 I6", 128)
    V(lambda: TC(T.thh[:], T.thl[:]), "thh", "thl", 4)
    PM([(T.b3[:, 132:136], T.Sp[:, 0, :], T.thh[:], True, True)], 4, "b3.th", "Sp thh")
    V(lambda: TC(T.thf[:], T.b3[:, 132:136]), "thf", "b3.th", 4)
    add("a", [(lambda t=t: ACT(T.hT[:, t, :], T.hB[:], F.Identity, bias=T.thf[:, t:t + 1])) for t in range(1, NV)], "hT", "hB thf", 3 * dv(4))
    V(lambda: TS(T.phh[:], T.phl[:], -2048.0, None, A.add), "phh", "phl", 256)
    PM([(T.b5[:, 256:272], row("Wb", j), T.phh[:, j:256:16], j == 0, j == 15) for j in R16], 16, "b5.w0", "Wb phh")
    V(lambda: TC(T.fin0[:], T.b5[:, 256:272]), "fin0", "b5.w0", 16)
    V(lambda: TS(T.posf[:], T.pos[:], OFF, None, A.add), "posf", "pos", 256)
    D("pt", T.PT[0:128:16, 0:4096], T.posf[:], "PT PT1", "posf", 2.5)

    def first(eq, bank, rows, rkey, key, kkey, flag, parts, spare=None, within=False, split=False):
        lo = lambda b: 64 * (b // 4)
        part = lambda b: [k for k, (x, y) in enumerate(parts) if x <= b < y][0]
        late = lambda b: "%s%d" % (eq, b // 8) in LATE
        hi = lambda b: 128 * (b // 8 + 1) if within else 256
        for bs in ((0, 1, 2, 3), (4, 5, 6, 7), (8, 9, 10, 11), (12, 13, 14, 15)) if within else ((0, 1), (2, 3), (4, 5), (6, 7), (8, 9, 10, 11), (12, 13, 14, 15)):
            fk, ks, d = "%s.%d" % (flag, part(bs[0])), lambda k: " ".join("%s.%d" % (k, b) for b in bs), len(bs) * dv(hi(bs[0]) - lo(bs[0]), 0.5)
            if late(bs[0]):
                add("v", [(lambda b=b: TS(T[eq][:, b, lo(b):hi(b)], rows(lo(b), hi(b)), key(b), None, A.is_equal)) for b in bs], ks(eq), rkey + " " + kkey, d)
                xy = [(b, 7 - b % 8, 16 if b < 8 and not within else 15 - b % 8) for b in bs]
                add("a", [(lambda b=b, x=x, y=y: ACT(T["W" + eq][:, b, :, x:y], T.Wt[:, :, x:y], F.Copy, scale=lfc(flag, b))) for b, x, y in xy],
                    ks("W" + eq), "Wt " + fk, sum(dv(8 * (y - x)) for b, x, y in xy))
            else:
                add("v", [(lambda b=b: TS(T[eq][:, b, lo(b):hi(b)], rows(lo(b), hi(b)), key(b), lfc(flag, b), A.is_equal, A.mult)) for b in bs],
                    ks(eq), "%s %s %s" % (rkey, kkey, fk), d)
        steps = ((1, (8, 12, 13, 14, 15, 9, 10, 11)), (0, (0, 4, 5, 6, 7, 1, 2, 3))) if within else \
            ((0, (0, 1, 2)), (0, (4, 5, 6, 7, 3)), (1, (0, 1, 2, 3, 4, 5, 6, 7)), (1, (8, 9, 10, 12, 13, 14, 15, 11)))
        for n_, (h, bs) in enumerate(steps):
            ms = []
            for b in bs:
                x = max(lo(b), 128 * h)
                y = 7 - b % 8 if b // 8 == h else 8
                w = T["W" + eq][:, b, :, y:y + 8] if late(b) else T.Wt[:, :, y:y + 8]
                ms.append((T[bank][x - 128 * h:128, 384 + 64 * h:448 + 64 * h], T[eq][:, b, x:128 * h + 128], w,
                           b == (8 * h if within else 0), b == 8 * h + 3))
            if eq in XA and ms[0][3]:
                ms.insert(1, (T[bank][:, 384 + 64 * h:448 + 64 * h], In, T.thb[:], False, False))
            PM(ms, 64, "%s.n%d %s.g" % (bank, h, bank), "In thb Wt " + " ".join("%s.%d" % (eq, b) + " W%s.%d" % (eq, b) * late(b) for b in bs))
            if not split and n_ < len(steps) - 1:
                continue
            h0, h = (h, h) if split else (0, 1)
            if eq in XA:
                S_(lambda h=h, h0=h0: ACT(T.Xm[:, h0:h + 1, :, :], T[bank][:, 384 + 64 * h0:448 + 64 * h], F.Relu, scale=-1.0),
                   "Xm.%d" % h0, "%s.n%d %s.n%d" % (bank, h0, bank, h), 64 * (h + 1 - h0))
            else:
                V(lambda h=h, h0=h0: TT(T.Xm[:, h0:h + 1, :, :], T[bank][:, 384 + 64 * h0:448 + 64 * h], T.thr[:, 64 * h0:64 * h + 64], A.is_lt),
                  "Xm.%d" % h0, "%s.n%d %s.n%d thr" % (bank, h0, bank, h), 64 * (h + 1 - h0))
            o = T[bank][:, 256 + 8 * h0:264 + 8 * h]
            PM(([] if spare is None else [(o, Ib, T.sp[:, spare + 8 * h0:spare + 8 * h + 8], True, False)]) +
               [(o, T["Vs" if spare is None else "VsB"][:, 112 - 16 * k:240 - 16 * k], T.Xm[:, h0:h + 1, k, :], k == 0 and spare is None, k == 7)
                for k in range(8)], 16, "%s.w%d %s.g" % (bank, h0, bank), "Ib sp Vs VsB Xm.%d" % h0)

    def send(key, src, dst, t):
        rid, pid, _ = topo.addr(nxt)
        m, n = topo.mask(me, nxt), len(topo.engines(me, nxt))
        i = add("g", [lambda: g.remote_dma(T[dst][:], T[src][:], T.sem["%sr%d" % (key, t)], T.sem["%sl%d" % (key, t)], pid, rid, m)],
                "", src, 0.3, "%sl%d" % (key, t), n)
        add("n", [], dst, "", TRN - (key == "f"), "%sr%d" % (key, t), n, i)

    ALL = [(0, 16)]
    for t in range(NV):
        now[0] = t
        EM = EMS[t]
        zi, fi, zo_, fo = "zin%d" % t, "fin%d" % t, "zout%d" % t, "fout%d" % t
        zin, fin, zout, fout = T[zi], T[fi], T[zo_], T[fo]
        PM([(T.b3[:, 0:16], row("Ww", j), zin[:, j:256:16], j == 0, j == 15) for j in R16], 16, "b3.u", "Ww " + zi)
        if "xr" in ONA:
            S_(lambda: ACT(xr, T.b3[:, 0:16], F.Identity, bias=ws), "xr", "b3.u ws", 16)
        else:
            V(lambda: TS(xr, T.b3[:, 0:16], ws, None, A.add), "xr", "b3.u ws", 16)
        V(lambda: TS(ui, xr, 4095, None, A.bitwise_and), "ui", "xr", 16)
        V(lambda: TS(T.CI[:, 0:16], xr, 15, None, A.bitwise_and), "mi", "xr", 16)
        AF(u32, ui, "u32", "ui", 16, bias=32.0)
        AF(u2, T.CI[:, 0:16], "u2", "mi", 16, 2048.0, 2464.0 * t)
        z0 = min(x for x, n, m in CM + EM if m != "c")
        for k in range(8):
            outs, in_, n = [T.ze[:, 16 * z0 + x:4096:16] for x in (2 * k, 2 * k + 1)], zin[:, z0:256], 256 - z0
            eng = (ZE if t else ZE0)[k]
            fn = {"g": lambda o, i, n=n: sel(o, i, [[0, n]], A.is_gt, 1, 0), "a": lambda o, i: ACT(o, i, F.Copy), "v": TC}[eng]
            add(eng, [(lambda o=o, in_=in_, fn=fn: fn(o, in_)) for o in outs], "ze.%d" % k, zi,
                2 * (0.17 + 2 * n * CY if eng == "g" else dv(n, 1.0 if eng == "a" else 0.5)))
        S_(lambda zin=zin: ACT(T.R[:, 4096:4352], zin[:], F.Copy, bias=-ZO), "Rd", zi, 256)
        V(lambda fin=fin: TT(xq, u32, fin[:], A.mult), "xq", "u32 " + fi, 16)
        V(lambda: TT(xq, xq, u2, A.add), "xq", "xq u2", 16)
        V(lambda: TS(T.CI[:, 16:32], xq, 5, 1023, A.arith_shift_right, A.bitwise_and), "ci", "xq", 16)
        AF(cu, T.CI[:, 16:32], "cu", "ci", 16)
        cells, ck_ = (T.C[:, 0:1024], "C") if t else (T.Ci[:], "Ci")
        for w, x, y in (("sa", 0, SU), ("su", SU, 16)):
            AF(T.su[:, 16 * x:16 * y], cells.indirect(T.lu[:, 0, x:y]), w, ck_ + " cu", 16 * (y - x), rate=GA)
        S_(lambda: ACT(T.sF[:], T.C[:, 0:1024].indirect(cu), F.Copy), "sF", "C cu", 256, GA)
        V(lambda: TT(ye, T.CI[:, 16:32], u32, A.mult), "ye", "ci u32", 16)
        AF(yf, ye, "yf", "ye", 16, bias=32.0)
        V(lambda: TS(T.CI[:, 32:48], yf, 5, 1023, A.arith_shift_right, A.bitwise_and), "ei", "yf", 16)
        AF(eu, T.CI[:, 32:48], "eu", "ei", 16)
        AF(T.su2[:], T.C[:, 0:1024].indirect(eu), "su2", "C eu", 256, rate=GA)
        AF(T.L3[:], T.CI[:, 16:48], "L3", "ci ei", 32)
        AF(T.kf[:], T.CI[:, 16:48], "kf", "ci ei", 32)
        V(lambda: TT(T.RM[:], T.CI[:], T.K3[:], A.subtract), "RM", "ci mi ei K3", 48)
        V(lambda: TT(T.L2[:, 16:32], iL, T.CI[:, 0:16], A.subtract), "mneg", "iL mi", 16)
        AF(T.uh[:], ui, "uh", "ui", 16, bias=-2048.0)
        spread("b4", 0, "L3", 32, "b4.0 b4.1")
        evac(T.rows[:], T.b4[:], "rows", "b4.0 b4.1", 512)
        PM([(T.b3[:, 64:80], I5, fin[:], True, False), (T.b3[:, 64:80], Ib, T.uh[:], False, True)], 16, "b3.f", "I5 Ib uh " + fi)
        def turn(dst, k0, key, stop, off=0, out="b0.k"):
            PM([(T.b0[:, off + 128 * r:off + 128 * r + 128], T.W4[:, k0 + 2 * r + h, :], T[dst][:, :, 16 * h:16 * h + 16], False, stop and r + h == 2)
                for r in range(2) for h in range(2)], 128, out + " b0.g", key + " " + dst)
        AF(T.s16[:], T.su[:], "s16", "sa su", 256, bias=-2048.0, rate=0.5)
        V(lambda: v.transpose(T.ts[:], T.s16[:]), "ts", "s16", 256, 0.5)

        def records(part, su, xg, xa, k, bank):
            l0, nl, mode = part
            lo, hi = 16 * l0, 16 * (l0 + nl)
            gk, ak, out = "%s.%d" % (xg, k), "%s.%d" % (xa, k), T[bank][:, l0:l0 + nl]
            sk = lambda x, y: su if su == "su2" else "sa " * (x < 16 * SU) + "su" * (y > 16 * SU)
            if mode == "c":
                banks = (("b6", "b6.x"), ("b7", "b7.x"))
                if su == "su" and k and PRE:
                    banks = (("b2", "b2.0 b2.1 b2.2 b2.3 b2.4 b2.g"), ("b0", "b0.k b0.n0 b0.n1 b0.w0 b0.w1 b0.g"))
                S_(lambda: ACT(T[xg][:, lo:hi], T.R[:, 0:4096].indirect(T[su][:, l0:l0 + nl]), F.Copy), gk, "R " + sk(l0, l0 + nl), hi - lo, GA)
                for y in range(2):
                    bk, key = banks[y]
                    os_ = [T[bk][:, nl * j:nl * j + nl] for j in range(8)]
                    rs_ = [T[xg][:, lo + 8 * y + j:hi:16] for j in range(8)]
                    if su == "su" and PRE:
                        PM([(T[bk][:, 0:8 * nl], Zb, T.on[:, 0:8 * nl], True, False)] + [(o, In, zin[:, l0:l0 + nl], False, False) for o in os_],
                           114, key, "Zb on In " + zi)
                        PM([(o, Ib, r, False, j == 7) for j, (o, r) in enumerate(zip(os_, rs_))], nl, key, "Ib " + gk)
                    else:
                        PM([m for o, r in zip(os_, rs_) for m in ((o, Ib, r, True, False), (o, In, zin[:, l0:l0 + nl], False, True))], nl, key,
                           "Ib In %s %s" % (gk, zi))
                    S_(lambda bk=bk, y=y: ACT(T[xa][:, lo + 8 * nl * y:lo + 8 * nl * (y + 1)], T[bk][:, 0:8 * nl], F.Abs, bias=ZO), "%s.%d" % (ak, y), key, 8 * nl)
                PM([(out, row("Wb", j), T[xa][:, lo + nl * j:lo + nl * j + nl], j == 0, j == 15) for j in R16], nl, "%s.%d" % (bank, k) + " b2.g" * (bank == "b2" and "b" in [m for x, n, m in EM]), "Wb %s.0 %s.1" % (ak, ak))
                return
            zk = " ".join("ze.%d" % z for z in range(8))
            vp = VP if su == "su" else VE
            ys = range(l0, l0 + nl, vp)
            for y in ys:
                ye_ = min(y + vp, l0 + nl)
                x, xa_ = T[xg][:, 16 * y:16 * ye_], T[xa][:, 16 * y:16 * ye_]
                V(lambda x=x, y=y, ye_=ye_: TT(x, T.R[:, 0:4096].indirect(T[su][:, y:ye_]), T.ze[:, 16 * y:16 * ye_], A.subtract),
                  "%s.%d" % (gk, y), "R %s %s" % (sk(y, ye_), zk), 16 * (ye_ - y), GA)
                if mode == "a":
                    S_(lambda x=x, xa_=xa_: ACT(xa_, x, F.Abs, bias=ZO), "%s.%d" % (ak, y), "%s.%d" % (gk, y), 16 * (ye_ - y))
                else:
                    V(lambda x=x, xa_=xa_: TS(xa_, x, ZO, 0.0, A.add, A.max), "%s.%d" % (ak, y), "%s.%d" % (gk, y), 16 * (ye_ - y), 0.5)
            ks = lambda key: " ".join("%s.%d" % (key, y) for y in ys)
            if mode == "b":
                PM([(out, row("Wn", j), T[xg][:, lo + j:hi:16], j == 0, False) for j in R16] + [(out, Ix, T.zof[:, 0:nl], False, False)] * (su == "su2"),
                   nl, "%s.%d %s.g" % (bank, k, bank), "Wn Ix zof " + ks(gk))
            PM([(out, row("Wb" if mode == "a" else "W2", j), T[xa][:, lo + j:hi:16], j == 0 and mode == "a", j == 15) for j in R16], nl,
               "%s.%d %s.g" % (bank, k, bank), "Wb W2 " + ks(ak))

        for k, part in enumerate(CM):
            records(part, "su", "xg", "xa", k, "b5" if part[2] == "b" else "b1")
        PM([(T.b0[:, 0:256], Ib, T.ck[:, 0:256], True, False)], 256, "b0.k b0.g", "Ib ck")
        turn("ts", 0, "W4", False)
        if t == 0:
            V(lambda: TS(T.hc[:], T.hB[:], T.thf[:, 0:1], None, A.add), "h", "hB thf", 4)
        else:
            S_(lambda: ACT(T.accb[:, 16:32], T.b3[:, 112:128], F.Copy, accum_out=a0), "a0", "b3.a", 16)
            S_(lambda: ACT(T.ai[:], a0, F.Copy, bias=-0.484375, scale=0.03125), "ai", "a0", 1)
            S_(lambda: ACT(am, T.ai[:], F.Identity, bias=a0, scale=-32.0), "am", "ai a0", 1)
            S_(lambda t=t: ACT(T.hc[:], T.hT[:, t, :], F.Identity, bias=am), "h", "hT am", 4)
        dn, dd = T.T2[:, 0, :], T.T2[:, 1, :]
        for bk in ("b1", "b5"):
            ks = [k for k, part in enumerate(CM) if (part[2] == "b") == (bk == "b5")]
            if ks:
                x, y = CM[ks[0]][0], CM[ks[-1]][0] + CM[ks[-1]][1]
                V(lambda bk=bk, x=x, y=y: TS(T.T2[:, 0, x:y], T[bk][:, x:y], -256.0 - 16 * ZO * (bk == "b5"), 256.0, A.add, A.min), "dn" + bk, " ".join("%s.%d" % (bk, k) for k in ks), y - x)
        DN = "dnb1 dnb5"
        V(lambda: v.transpose(T.td[:], dn), "td", DN, 256, 0.5)
        turn("td", 4, "W4d", True)
        V(lambda: TS(dd, dn, 256.0, -1.0, A.is_ge, A.mult), "dd", DN, 256, 0.5)
        V(lambda: TS(T.T2[:, 2, :], dn, T.hc[:, 2:3], 3.0, A.min, A.mult), "mn", DN + " h", 256, 0.5)
        if S2:
            PM([(T.b3[:, 144:176], row("Wb", j), T.T2[:, 0:2, j:256:16], j == 0, False) for j in R16] + [(T.b3[:, 144:160], Ib, T.k16[:, 0:16], False, False)] +
               [(T.b3[:, 144:160], row("Wb", j), T.T2[:, 2, j:256:16], False, j == 15) for j in R16], 16, "b3.s", "Wb Ib k16 dd mn " + DN)
            V(lambda: TS(tq, T.b3[:, 160:176], 64.0, T.hc[:, 1:2], A.add, A.mult), "tq", "b3.s h", 16)
            V(lambda: TT(ps, tq, T.b3[:, 144:160], A.is_ge), "ps.0", "b3.s tq", 16)
        else:
            PM([(T.b3[:, 144:192], row("Wb", j), T.T2[:, :, j:256:16], j == 0, False) for j in range(15)] + [(T.b3[:, 144:160], Ib, T.k16[:, 0:16], False, False)] +
               [(T.b3[:, 144:192], row("Wb", 15), T.T2[:, :, 15:256:16], False, True)], 16, "b3.s", "Wb Ib k16 dd mn " + DN)
            V(lambda: TS(tq, T.b3[:, 160:176], 64.0, T.hc[:, 1:2], A.add, A.mult), "tq", "b3.s h", 16)
            V(lambda: TT(tq, tq, T.b3[:, 144:160], A.subtract), "tq", "b3.s tq", 16)
            V(lambda: TT(ps, tq, T.b3[:, 176:192], A.is_ge), "ps.0", "b3.s tq", 16)
        V(lambda: v.tensor_tensor_scan(T.sm[:], T.d0n[:], T.b0[:, 0:256], 0.0, A.add, A.min), "sm", "d0n b0.k", 256)
        add("v", [(lambda r=r: TC(T.li[:, LI.index("kI"), r:16:2], T.sm[:, 128 * r + 15:128 * r + 128:16])) for r in range(2)], "kI", "sm", 2 * dv(8))
        V(lambda: TS(w1, kI, 16, None, A.arith_shift_right), "w1", "kI", 16)
        V(lambda: TS(ny, kI, 4095, None, A.bitwise_and), "ny", "kI", 16)
        add("v", [(lambda r=r: TS(T.lf[:, LF.index("nh"), r:16:2], T.sm[:, 128 * r + 15:128 * r + 128:16], 2.0 ** -16, T.hc[:, 2:3], A.mult, A.is_ge))
                  for r in range(2)], "nh", "sm h", 2 * dv(8))
        V(lambda: TT(t3, nh, tr, A.mult), "t3", "nh tr", 16)
        V(lambda: TT(t4, t3, ny, A.max), "t4", "t3 ny", 16)
        AF(zo, t4, "zo", "t4", 16)
        if "xs" in ONA:
            S_(lambda: ACT(T.xs[:], T.R[:].indirect(zo), F.Copy), "xs", "R Rd zo", 256, GA)
            PM([(T.b1[:, 0:256], Ib, zin[:], True, False), (T.b1[:, 0:256], Ib, T.xs[:], False, True)], 256, "b1.0 b1.1 b1.2 b1.3 b1.g", "Ib xs " + zi)
            AF(zout[:], T.b1[:, 0:256], zo_, "b1.0 b1.1 b1.2 b1.3", 256, 0.5, ZO / 2 - 0.25)
        else:
            V(lambda zin=zin: TT(T.xs[:], T.R[:].indirect(zo), zin[:], A.add), "xs", "R Rd zo " + zi, 256, GA)
            V(lambda zout=zout: TS(zout[:], T.xs[:], 0.5, ZO / 2 - 0.25, A.mult, A.add), zo_, "xs", 256, 0.5)
        send("z", zo_, "zin%d" % (t + 1), t)
        S_(lambda: ACT(T.pg[:], T.PT[:].indirect(zo), F.Identity, bias=k3), "pg", "PT PT1 zo k2", 256, GA)
        AF(T.w5h[:], w1, "w5h", "w1", 16, 5.0)
        PM([(T.b3[:, 48:64], x, y, n == 0, False) for n, (x, y) in enumerate(((Ib, T.k16[:, 16:32]), (I4n, fin[:]), (In, T.uh[:]), (Ib, T.w5h[:])))] +
           [(T.b3[:, 48:64], row("Wb", j), T.pg[:, j:256:16], False, j == 15) for j in R16], 16, "b3.d", "Wb Ib In I4n k16 uh w5h pg " + fi)
        V(lambda: TT(ph, ps, nh, A.is_gt), "ph", "ps.0 nh", 16)
        V(lambda: TT(pdh, ph, T.b3[:, 48:64], A.mult), "pdh", "ph b3.d", 16)
        WB = T.b5[:, 256:272]
        first("EQ", "b5", lambda x, y: T.rows[:, x:y], "rows", lambda b: T.kf[:, b:b + 1], "kf", "ps", ALL)
        V(lambda: TT(rr, WB, pdh, A.mult), "rr", "b5.w0 pdh", 16)
        V(lambda: TT(fr, rr, T.b3[:, 64:80], A.add), "fr", "rr b3.f", 16)
        V(lambda: TS(fr2, fr, 4095, None, A.bitwise_and), "fr2", "fr", 16)
        AF(fout[:], fr2, fo, "fr2", 16, bias=-2048.0)
        send("f", fo, "fin%d" % (t + 1), t)
        V(lambda: TT(acc, WB, ps, A.mult), "acc", "b5.w0 ps.0", 16)
        if t < NV - 1:
            PM([(T.b3[:, 112:128], T.on[:, 0:128], acc, True, True)], 16, "b3.a", "on acc")
        for k, part in enumerate(EM):
            records(part, "su2", "eg", "ea", k, "b2")
        if KMAX == "p":
            V(lambda: v.transpose(T.tx[:], dd), "tx", "dd", 256, 0.5)
            PM([(T.b0[:, 256:512], Ib, T.ck[:, 256:512], True, False)], 256, "b0.x b0.w0 b0.w1 b0.n0 b0.n1 b0.g", "Ib ck2")
            for dst, k0, key in (("ts", 0, "W4"), ("td", 4, "W4d"), ("tx", 8, "W4x")):
                turn(dst, k0, key, k0 == 8, 256, "b0.x")
            V(lambda: v.tensor_tensor_scan(T.sx[:], T.d0x[:], T.b0[:, 256:512], 0.0, A.add, A.max), "sx", "d0x b0.x b0.w0 b0.w1 b0.n0 b0.n1", 256)
        else:
            S_(lambda: ACT(T.mM[:], T.b0[:, 0:256], F.Relu, bias=-64.0 * 16000000.0, scale=64.0), "mM", "b0.k", 256)
            V(lambda: TT(T.kr[:], T.b0[:, 0:256], T.mM[:], A.subtract), "kr", "b0.k mM", 256)
            V(lambda: v.tensor_tensor_scan(T.sx[:], T.d0x[:], T.kr[:], 0.0, A.add, A.max), "sx", "d0x kr", 256)
        add("v", [(lambda r=r: TC(T.li[:, LI.index("fI"), r:16:2], T.sx[:, 128 * r + 15:128 * r + 128:16])) for r in range(2)], "fI", "sx", 2 * dv(8))
        V(lambda: TS(foe, fI, 2.0 ** -16, T.hc[:, 3:4], A.mult, A.is_ge), "foe", "fI h", 16)
        V(lambda: TS(vs, fI, 4095, None, A.bitwise_and), "vs", "fI", 16)
        AF(vk, vs, "vk", "vs", 16, bias=-2048.0)
        AF(T.L2[:, 0:16], vs, "v16", "vs", 16, bias=-2048.0)
        V(lambda: TT(vrm, vs, tr, A.subtract), "vrm", "vs tr", 16)
        PM([(T.b4[:, j:512:16], T.Sp[:, j, :], T.L2[:], True, True) for j in R16], 32, "b4.0 b4.1", "Sp v16 mneg")
        evac(T.vrow[:, 0:256], T.b4[:, 0:256], "vrow", "b4.0", 256)
        evac(T.vrow[:, 256:512], T.b4[:, 256:512], "nrow", "b4.1", 256)
        V(lambda: TT(flg, foe, acc, A.mult), "flg.0", "foe acc", 16)
        V(lambda: TT(fv, flg, vrm, A.mult), "fv", "flg.0 vrm", 16)
        V(lambda: TT(fv, fv, T.sp[:, 0:16], A.add), "fv", "fv sp", 16)
        first("EQv", "b5", lambda x, y: T.vrow[:, x:y], "vrow", lambda b: lfc("vk", b), "vk", "flg", ALL, 0, True)
        V(lambda: TT(dl, WB, fv, A.max), "dl", "b5.w0 fv", 16)
        AF(dlu, dl, "dlu", "dl", 16, bias=2304.0)
        for x in (0, 8):
            V(lambda x=x: TC(T.R[:].indirect(T.lu[:, LU.index("dlu"), x:x + 8]), T.s64[:, 0:128]), "R Rd", "dlu s64", 128, SC)
        V(lambda: TT(T.la[:, 0:16], acc, T.RM[:, 0:16], A.mult), "la0", "acc RM", 16)
        V(lambda: TT(T.la[:, 16:32], acc, T.RM[:, 16:32], A.mult), "la1", "acc RM", 16)
        V(lambda: TT(T.la[:], T.la[:], T.T2c[:], A.add), "la0 la1", "la0 la1 T2c", 32)
        AF(T.lau[:], T.la[:], "lau", "la0 la1", 32)
        V(lambda zout=zout: TT(T.R[:].indirect(T.lau[:, 0:16]), zout[:], T.zof[:], A.add), "R Rd", "zof lau " + zo_, 256, SC)
        spread("b4", 256, fo, 16, "b4.1")
        S_(lambda: ACT(T.phr[:], T.b4[:, 256:512], F.Identity, bias=k2, scale=lfc("I16", 0)), "phr", "b4.1 k2", 256)
        if OFF:
            S_(lambda: ACT(T.PT[:].indirect(T.lau[:, 0:16]), T.phr[:], F.Silu), "PT PT1", "lau phr", 256, SC)
        else:
            V(lambda: TC(T.PT[:].indirect(T.lau[:, 0:16]), T.phr[:]), "PT PT1", "lau phr", 256, SC)
        Q = T.b1[:, 256:512]
        own = (Q, Ib, T.vrow[:, 256:512], False, False)
        PM([(Q, I6, T.on[:, 0:256], True, False), (Q, Y1, dd, False, False), own[:4] + (True,)], 256, "b1.q0 b1.q1 b1.g", "I6 on Y1 dd Ib nrow")
        S_(lambda: ACT(T.n1[:], Q, F.Copy, bias=-8192.0, scale=-1.0), "n1", "b1.q0 b1.q1", 256)
        V(lambda: TT(T.a1[:], Q, T.sF[:], A.min), "a1", "b1.q0 b1.q1 sF", 256)
        V(lambda: TT(T.C[:].indirect(T.lau[:, 16:32]), T.a1[:], T.n1[:], A.max), "C", "lau a1 n1", 256, SC)
        for k, (x, y) in enumerate(EP):
            dk = " ".join("b2.%d" % z for z, (l0, nl, m) in enumerate(EM) if l0 < 16 * y and 16 * x < l0 + nl)
            S_(lambda x=x, y=y: ACT(T.sup[:, 16 * x:16 * y], T.b2[:, 16 * x:16 * y], F.Relu, bias=T.hc[:, 0:1], scale=-1.0), "sup.%d" % k, dk + " h", 16 * (y - x))
            PM([(T.b3[:, 80 + x:80 + y], row("Wb", j), T.sup[:, 16 * x + j:16 * y:16], j == 0, j == 15) for j in R16], 16, "b3.c%d" % k, "Wb sup.%d" % k)
            V(lambda x=x, y=y: TT(lfc("cnd", x, y), T.accb[:, x:y], T.b3[:, 80 + x:80 + y], A.is_gt), "cnd.%d" % k, "acc b3.c%d" % k, 16)
        S_(lambda: ACT(T.sF2[:], T.C[:, 0:1024].indirect(eu), F.Copy), "sF2", "C eu", 256, GA)
        first("EQe", "b0", lambda x, y: T.rows[:, 256 + x:256 + y], "rows", lambda b: T.kf[:, 16 + b:17 + b], "kf", "cnd", EP, 16, True, SPLIT)
        for h, (x, y) in ((1, (8, 16)), (0, (0, 8))) if SPLIT else ((0, (0, 16)),):
            ln, Qh = slice(16 * x, 16 * y), T.b1[:, 256 + 16 * x:256 + 16 * y]
            S_(lambda ln=ln: ACT(T.sg2[:, ln], T.b2[:, ln], F.Sign, bias=-511.5), "sg2.%d" % h,
               " ".join("b2.%d" % z for z, (l0, nl, m) in enumerate(EM) if l0 < 16 * y and 16 * x < l0 + nl), 16 * (y - x))
            qk = "b1.q%d" % h if SPLIT else "b1.q0 b1.q1"
            PM([(Qh, Y2c, T.on[:, ln], True, False), (Qh, Ib, T.vrow[:, 256 + 16 * x:256 + 16 * y], False, False), (Qh, Y2, T.sg2[:, ln], False, True)],
               16 * (y - x), qk + " b1.g", "Y2c Y2 on Ib nrow sg2.%d" % h)
            S_(lambda ln=ln, Qh=Qh: ACT(T.n2[:, ln], Qh, F.Copy, bias=-8192.0, scale=-1.0), "n2.%d" % h, qk, 16 * (y - x))
            V(lambda ln=ln, Qh=Qh: TT(T.a2[:, ln], Qh, T.sF2[:, ln], A.min), "a2.%d" % h, qk + " sF2", 16 * (y - x))
            c_, l_, u_ = lfc("cr", x, y), lfc("l2", x, y), T.lu[:, LU.index("l2u"), x:y]
            V(lambda x=x, y=y, c_=c_: TT(c_, lfc("cnd", x, y), T.RM[:, 32 + x:32 + y], A.mult), "cr.%d" % h,
              "RM " + " ".join("cnd.%d" % k for k, (x1, y1) in enumerate(EP) if x1 < y and x < y1), 16)
            V(lambda x=x, y=y, c_=c_: TT(c_, c_, lfc("tc", x, y), A.add), "cr.%d" % h, "cr.%d tc" % h, 16)
            V(lambda x=x, y=y, c_=c_, l_=l_: TT(l_, T.b0[:, 256 + x:256 + y], c_, A.max), "l2.%d" % h, "b0.w%d cr.%d" % (h, h), 16)
            AF(u_, l_, "l2u.%d" % h, "l2.%d" % h, 16)
            for x in range(y - 8, x - 8, -8):
                V(lambda x=x: TT(T.C[:].indirect(T.lu[:, LU.index("l2u"), x:x + 8]), T.a2[:, 16 * x:16 * x + 128], T.n2[:, 16 * x:16 * x + 128], A.max),
                  "C", "l2u.@ a2.@ n2.@".replace("@", str(h)), 128, SC)
    now[0] = -2
    i = D("yrec", T.yrec[:], T.R[:, 0:4096], "", "R", 7.0)
    add("n", [], "", "", 9.5, None, 0, i)
    D("ycel", T.ycel[:], T.C[:, 0:1024], "", "C", 4.5, "a")
    if OFF:
        D("pb", T.posf[:], T.PT[0:128:16, 0:4096], "posf", "PT PT1", 2.5)
        V(lambda: TS(T.pos[:], T.posf[:], -OFF, None, A.add), "pos", "posf", 256)
        V(lambda: TC(T.posf[:], T.pos[:]), "posf", "pos", 256)
        D("ypo", T.ypo[:], T.posf[:], "", "posf", 2.5)
    else:
        D("ypo", T.ypo[:], T.PT[0:128:16, 0:4096], "", "PT PT1", 3.0)
    zl, fl = "zin%d" % NV, "fin%d" % NV
    S_(lambda: ACT(T.xs[:], T[zl][:], F.Copy, bias=-ZO), "xs", zl, 256)
    D("ypat", T.ypat[:], T.xs[:], "", "xs", 2.0)
    spread("b4", 0, fl, 16, "b4.0")
    S_(lambda: ACT(T.phr[:], T.b4[:, 0:256], F.Copy, bias=2048.0), "phr", "b4.0", 256)
    D("yphi", T.yphi[:], T.phr[0:128:16, :], "", "phr", 2.0)
    return ops


def schedule(ops):
    n = len(ops)
    occ = [0.0 if o["q"] == "n" else 0.1 if o["sem"] and o["sem"][0] == "d" else o["d"] for o in ops]
    fwd, bwd = [[] for _ in ops], [[] for _ in ops]
    for k, o in enumerate(ops):
        for x in o["wait"] | o["ord"] | ({o["net"]} if o["net"] is not None else set()):
            lag = ops[x]["d"] + WAKE if x in o["wait"] else occ[x]
            fwd[k].append((x, lag))
            bwd[x].append((k, lag + occ[k] - occ[x]))

    holds = [[(o["q"], 0.0)] * (o["q"] != "n") + [(b, WAKE) for b in o["bank"]] for o in ops]

    queue, zero, tail = [o["q"] for o in ops], [0.0] * n, [o["d"] - occ[o["i"]] for o in ops]

    def place(order, before, first):
        at, lines = [0.0] * n, {key: [] for held in holds for key, gap in held}
        for i in order:
            t, d, me, held = first[i], occ[i] - 1e-9, queue[i], holds[i]
            for x, lag in before[i]:
                if at[x] + lag > t:
                    t = at[x] + lag
            if len(held) == 1:
                line = lines[me]
                m = k = len(line)
                while k and line[k - 1][1] > t + 1e-9:
                    k -= 1
                while k < m and line[k][0] < t + d:
                    t = line[k][1]
                    k += 1
                line.insert(k, (t, t + occ[i], me))
                at[i] = t
                continue
            moved = True
            while moved:
                moved = False
                for key, gap in held:
                    line = lines[key]
                    m = k = len(line)
                    lim = t - gap + 1e-9
                    while k and line[k - 1][1] > lim:
                        k -= 1
                    while k < m:
                        s, e, q = line[k]
                        if s >= t + d + gap:
                            break
                        if gap == 0.0 or q != me:
                            t, moved = e + gap, len(held) > 1
                        k += 1
            for key, gap in held:
                line = lines[key]
                k = len(line)
                while k and line[k - 1][0] > t:
                    k -= 1
                line.insert(k, (t, t + occ[i], me))
            at[i] = t
        return at

    def run(order):
        at, why, last, end, final = [0.0] * n, [None] * n, {}, 0.0, 0
        for i in order:
            t, w = 0.0, None
            for x, lag in fwd[i]:
                if at[x] + lag > t:
                    t, w = at[x] + lag, (x, False)
            for key, gap in holds[i]:
                x = last.get(key)
                if x is not None and (gap == 0.0 or queue[x] != queue[i]) and at[x] + occ[x] + gap > t + 1e-9:
                    t, w = at[x] + occ[x] + gap, (x, True)
                last[key] = i
            at[i], why[i] = t, w
            if t + ops[i]["d"] > end:
                end, final = t + ops[i]["d"], i
        return at, why, final, end

    def tighten(at):
        back = place(np.argsort(np.add(at, occ), kind="stable")[::-1].tolist(), bwd, tail)
        at = place(np.argsort(-np.add(back, occ), kind="stable").tolist(), fwd, zero)
        order = np.argsort(at, kind="stable").tolist()
        at, why, final, end = run(order)
        return end + 0.1 * sum(at) / n, order, why, final, end

    def swap(order, x, i, up):
        lo, hi = order.index(x), order.index(i)
        if lo > hi:
            return False
        part, moved = order[lo:hi + 1], {i if up else x}
        for y in part[-2::-1] if up else part[1:]:
            if any(z in moved for z, lag in (bwd if up else fwd)[y]):
                if y in (x, i):
                    return False
                moved.add(y)
        order[lo:hi + 1] = sorted(part, key=lambda y: (y in moved) != up)
        return True

    if not ORDER:
        rng, same = np.random.default_rng(SEED), {o["tag"]: o["i"] for o in ops}
        now = best = tighten(place(range(n), fwd, zero))
        for k in range(ROUNDS):
            order, why, i = now[1][:], now[2], now[3]
            pairs = []
            while why[i]:
                if why[i][1]:
                    pairs.append((why[i][0], i))
                i = why[i][0]
            j, up = int(rng.integers(len(pairs))), rng.random() < 0.5
            x, i = pairs[j]
            for _ in range(int(rng.integers(4))):
                if up and j + 1 < len(pairs) and pairs[j + 1][1] == x:
                    j, x = j + 1, pairs[j + 1][0]
                if not up and j and pairs[j - 1][0] == i:
                    j, i = j - 1, pairs[j - 1][1]
            (a, ta), (b, tb) = ops[x]["tag"], ops[i]["tag"]
            todo = [(x, i)]
            if rng.random() < 0.8 and min(ta, tb) >= 0:
                todo = [(same[a, ta + d], same[b, tb + d]) for d in range(-min(ta, tb), NV) if (a, ta + d) in same and (b, tb + d) in same]
            if k % SHARE == SHARE - 1:
                at, m = run(order)[0], int(rng.integers(NV))
                t0 = [at[same["su", t]] for t in range(NV)]
                rank = [t0[t] + at[same[a, m]] - t0[m] if t >= 0 and (a, m) in same else at[i] for i, (a, t) in enumerate(o["tag"] for o in ops)]
                for i in range(n):
                    rank[i] = max([rank[i]] + [rank[x] + 1e-6 for x, lag in fwd[i]])
                todo, order = [], sorted(range(n), key=lambda i: rank[i])
            if not todo or any([swap(order, x, i, up) for x, i in todo]):
                new = tighten(run(order)[0])
                if new[0] <= now[0] + HEAT * (1 - k / ROUNDS) * rng.random():
                    now = new
                    best = min(best, now, key=lambda y: y[4])
        ORDER.extend([best[1], best[4]])
    order = ORDER[0]
    held = {}
    for i in order:
        for b in ops[i]["bank"]:
            if b in held and ops[held[b]]["q"] != ops[i]["q"]:
                ops[i]["wait"].add(held[b])
            held[b] = i
    return order


def rank_program(g, core, T, topo):
    rank = T.rank_of(core)
    if rank is None:
        return
    nxt = T.cores[(rank + 1) % len(T.cores)]
    ops = program(T, g, core, nxt, topo)
    eng = {"v": g.vector, "a": g.scalar, "p": g.tensor, "g": g, "s": g.sync}
    cnt = {q: 0 for q in "vapg"}
    seen = {q: {} for q in "vapgs"}
    clock, ev, final = {}, {}, {}
    for i in schedule(ops):
        o = ops[i]
        q = o["q"]
        if q == "n":
            if o["sem"] is None:
                continue
            ev[i] = (o["sem"], o["val"])
            clock[i] = {o["sem"]: o["val"]}
            final[o["sem"]] = o["val"]
            continue
        for x in sorted(o["wait"], key=lambda x: (-ev[x][1], x)):
            sm, val = ev[x]
            if seen[q].get(sm, 0) < val:
                eng[q].wait_ge(T.sem[sm], val)
                for k, y in clock[x].items():
                    if seen[q].get(k, 0) < y:
                        seen[q][k] = y
        for f in o["f"]:
            ins = f()
            if f is not o["f"][-1]:
                continue
            if o["sem"] is None:
                ins.then_inc(T.sem["q" + q], 1)
                cnt[q] += 1
            elif o["sem"][0] == "d":
                ins.then_inc(T.sem[o["sem"]], 16)
        ev[i] = (o["sem"], o["val"]) if o["sem"] else ("q" + q, cnt[q])
        clock[i] = dict(seen[q])
        clock[i][ev[i][0]] = ev[i][1]
        final[ev[i][0]] = ev[i][1]
    for sm, val in final.items():
        g.wait_ge(T.sem[sm], val)
